import numpy as np
import ml_dtypes


def mxq(x, axis, fmt="e4m3"):
    dtype, down = {"e4m3": (ml_dtypes.float8_e4m3fn, 7), "e5m2": (ml_dtypes.float8_e5m2, 14)}[fmt]
    v = np.moveaxis(np.asarray(x, np.float32).astype(ml_dtypes.bfloat16).astype(np.float64), axis, -1)
    blocks = v.reshape(v.shape[:-1] + (-1, 32))
    amax = np.abs(blocks).max(-1, keepdims=True)
    byte = np.maximum(np.where(amax > 0, np.frexp(amax)[1] - 1 + 127, 0) - down, 1)
    scale = np.exp2(byte - 127.0)
    codes = (blocks / scale).astype(np.float32).astype(dtype).astype(np.float64)
    return np.moveaxis((codes * scale).reshape(v.shape), -1, axis)


WIDE = False


def mx_kscale(k):
    if not WIDE:
        return np.ones(k)
    levels = np.array([10, -10, 5, -5, 0])
    if k % 512:
        return np.exp2(np.random.permutation(np.resize(levels, k // 32))).repeat(32)
    a = np.empty((k // 512, 16))
    for p in range(k // 512):
        a[p, :8] = np.random.permutation(np.resize(levels, 8))
        for g in range(8):
            far = levels[np.abs(levels - a[p, g]) >= 10]
            a[p, g + 8] = far[np.random.randint(len(far))]
    return np.exp2(a.ravel()).repeat(32)


BF16 = ml_dtypes.bfloat16


def bf(x):
    return np.asarray(x, np.float32).astype(BF16)


def f64(x):
    return np.asarray(x).astype(np.float64)


C, G, H, R = 2048, 1024, 512, 256

SLOPE = 0.1


def draw0():
    s, t, u = mx_kscale(G), mx_kscale(H), mx_kscale(C)
    size = np.exp(0.4 * np.random.standard_normal(C))
    return {"x": bf(np.random.standard_normal((C, G)) * size[:, None] * s * u[:, None]),
            "lib": bf(size * u),
            "w_enc": bf(np.random.standard_normal((G, H)) / np.sqrt(G) / s[:, None] * t),
            "b_enc": bf(0.4 * np.random.standard_normal(H) * t),
            "w_dec": bf(np.sqrt(2.0) * np.random.standard_normal((H, G)) / np.sqrt(H) / t[:, None]),
            "b_dec": bf(0.4 * np.random.standard_normal(G)),
            "depth": bf(np.exp(0.4 * np.random.standard_normal(C))),
            "q": bf(np.random.standard_normal((R, C)) / np.sqrt(C) / u),
            "unit": bf(np.exp(0.3 * np.random.standard_normal(H)) / t)}


def core(x, lib, w_enc, b_enc, w_dec, b_dec, depth, q, unit):
    size = f64(lib)[:, None]
    y = (mxq(f64(x), 1, "e4m3") @ mxq(f64(w_enc), 0, "e4m3")) + size * f64(b_enc)[None, :]
    h = np.maximum(y, SLOPE * y)
    d = mxq(h, 1, "e4m3") @ mxq(f64(w_dec), 0, "e4m3")
    z = d / size + f64(b_dec)[None, :]
    mean = f64(depth)[:, None] * np.log(1.0 + np.exp(z))
    k = mxq(f64(q), 1, "e4m3") @ mxq(h, 0, "e4m3")
    contrast = k * f64(unit)[None, :]
    return mean, contrast


def e4m3fn_bytes(y):
    return np.clip(np.asarray(y, np.float64), -448.0, 448.0).astype(np.float32).astype(ml_dtypes.float8_e4m3fn).view(np.uint8)


def e4m3fn_values(b):
    return np.asarray(b, np.uint8).view(ml_dtypes.float8_e4m3fn).astype(np.float64)


def setup_inputs():
    d = draw0()
    x0 = np.asarray(d['w_dec']).astype(np.float64)
    s = (np.max(np.abs(x0), axis=(1,), keepdims=True) / 448.0).astype(np.float32)
    out = {}
    for k, v in d.items():
        if k == 'w_dec':
            out['w_dec_bytes'] = e4m3fn_bytes(x0 / s.astype(np.float64))
            out['w_dec_scale'] = s
        else:
            out[k] = v
    return out


def reference(x, lib, w_enc, b_enc, w_dec_bytes, w_dec_scale, b_dec, depth, q, unit):
    return core(x, lib, w_enc, b_enc, e4m3fn_values(w_dec_bytes) * w_dec_scale.astype(np.float64), b_dec, depth, q, unit)

@@ -1,0 +1,542 @@
+from contextlib import ExitStack
+
+import concourse.mybir as mybir
+from concourse.masks import make_identity
+
+C, G, H, R = 2048, 1024, 512, 256
+FLOPS = 2 * C * G * H + 2 * C * H * G + 2 * R * C * H
+SLOPE = 0.1
+EARLY = 4
+TB, YB, DB = 3, 2, 3
+
+F32 = mybir.dt.float32
+BF16 = mybir.dt.bfloat16
+U32 = mybir.dt.uint32
+U8 = mybir.dt.uint8
+E4M3 = mybir.dt.float8_e4m3fn
+FP8X4 = mybir.dt.float8_e4m3fn_x4
+ALU = mybir.AluOpType
+ACT = mybir.ActivationFunctionType
+
+P = 128
+PACK = 4
+GROUP = P * PACK
+GROUPS = C // GROUP
+KP = G // GROUP
+
+
+def tile_library_size_autoencoder_f6_kernel(
+    tc, x, lib, w_enc, b_enc, w_dec_bytes, w_dec_scale, b_dec, depth, q, unit, out_mean, out_contrast
+):
+    nc = tc.nc
+    with ExitStack() as ctx:
+        keep = ctx.enter_context(tc.tile_pool(name="keep", bufs=1))
+        work = ctx.enter_context(tc.tile_pool(name="work", bufs=2))
+        psum = ctx.enter_context(tc.psum_pool(name="psum", bufs=2))
+        ctx.enter_context(tc.manual_schedule())
+
+        lib_sb = keep.tile([P, GROUPS, PACK], BF16, name="lib_sb")
+        nc.scalar.dma_start(out=lib_sb[:], in_=lib.rearrange("(g p s) -> p g s", p=P, s=PACK))
+        bdec_sb = keep.tile([P, 2, PACK], BF16, name="bdec_sb")
+        nc.scalar.dma_start(out=bdec_sb[:], in_=b_dec.rearrange("(h n m) -> n h m", h=2, m=PACK))
+        benc_sb = keep.tile([P, PACK], BF16, name="benc_sb")
+        nc.scalar.dma_start(out=benc_sb[:], in_=b_enc.rearrange("(p t) -> p t", t=PACK))
+        wsc_sb = keep.tile([P, PACK], F32, name="wsc_sb")
+        nc.scalar.dma_start(out=wsc_sb[:], in_=w_dec_scale.rearrange("(p t) o -> p (t o)", t=PACK))
+        depth_sb = keep.tile([P, GROUPS, PACK], BF16, name="depth_sb")
+        nc.scalar.dma_start(out=depth_sb[:], in_=depth.rearrange("(g p s) -> p g s", p=P, s=PACK))
+
+        x_view = x.rearrange("(g p s) k -> g p s k", p=P, s=PACK)
+        w_view = w_enc.rearrange("(c p j) n -> c p j n", p=P, j=PACK)
+        x_first = [keep.tile([P, PACK, GROUP], BF16, name="x_first")]
+        x_late = [keep.tile([P, 2, GROUP], BF16, name=f"x_late{half}") for half in range(2)]
+        lib_first = keep.tile([P, GROUP], BF16, name="lib_first")
+        lib_bc = keep.tile([P, C - GROUP], BF16, name="lib_bc")
+        bdec_bc = [keep.tile([P, 512], BF16, name=f"bdec_bc{n}") for n in range(2)]
+        unit_bc = keep.tile([P, H], BF16, name="unit_bc")
+        x_sb = [None] + [keep.tile([P, PACK, G], BF16, name=f"x_sb{g}") for g in range(1, GROUPS)]
+        w_raw = [work.tile([P, PACK, H], BF16, name="w_raw", align_bytes=256) for c in range(KP)]
+        wd_bytes = keep.tile([P, PACK, G], U8, name="wd_bytes")
+        q_sb = keep.tile([P, 2, C], BF16, name="q_sb")
+        for c in range(KP):
+            nc.sync.dma_start(out=w_raw[c][:], in_=w_view[c])
+        nc.sync.dma_start(out=x_first[0][:], in_=x_view[0][:, :, 0:GROUP])
+        for half in range(2):
+            nc.sync.dma_start(
+                out=x_late[half][:], in_=x_view[0][:, 2 * half : 2 * half + 2, GROUP:G]
+            )
+        nc.sync.dma_start(out=wd_bytes[:], in_=w_dec_bytes.rearrange("(p t) g -> p t g", t=PACK))
+        nc.sync.dma_start(out=x_sb[1][:], in_=x_view[1])
+        nc.sync.dma_start(out=x_sb[2][:], in_=x_view[2])
+        nc.sync.dma_start(out=lib_bc[:], in_=lib[GROUP:C].partition_broadcast(P))
+        nc.sync.dma_start(out=q_sb[:], in_=q.rearrange("(b r) c -> r b c", r=P))
+        nc.sync.dma_start(out=x_sb[3][:], in_=x_view[3])
+        nc.sync.dma_start(out=unit_bc[:], in_=unit.partition_broadcast(P))
+
+        ident32 = keep.tile([P, P], F32, name="ident32")
+        make_identity(nc, ident32[:])
+        ident16 = keep.tile([P, P], BF16, name="ident16")
+        make_identity(nc, ident16[:])
+        warm = keep.tile([P, 1], F32, name="warm")
+        nc.vector.memset(warm[:], 0.0)
+        nc.scalar.activation(out=warm[:], in_=warm[:], func=ACT.Exp)
+        invlib = keep.tile([P, GROUPS, PACK], F32, name="invlib")
+        nc.vector.reciprocal(out=invlib[:], in_=lib_sb[:])
+
+        dummy_in = keep.tile([P, 512], BF16, name="dummy_in")
+        nc.vector.memset(dummy_in[:], 0.0)
+
+        def keep_busy(n):
+            for i in range(n):
+                bank = psum.tile([P, 512], F32, name="d_bank", bufs=DB)
+                nc.tensor.matmul(out=bank[:], lhsT=ident16[:], rhs=dummy_in[:], start=True, stop=True)
+
+        def spread(which):
+            columns = lib_sb[:, 0, :] if which == 0 else bdec_sb[:, which - 1, :]
+            bank = psum.tile([P, PACK, P], F32, name="tp", bufs=TB)
+            for m in range(PACK):
+                nc.tensor.matmul(
+                    out=bank[:, m, :], lhsT=columns[:, m : m + 1].to_broadcast([P, P]), rhs=ident16[:], start=True, stop=True
+                )
+            if which == 0:
+                nc.scalar.copy(out=lib_first[:].rearrange("p (m n) -> p m n", m=PACK), in_=bank[:])
+            else:
+                nc.scalar.copy(
+                    out=bdec_bc[which - 1][:].rearrange("p (n m) -> p n m", m=PACK),
+                    in_=bank[:].rearrange("p m n -> p n m"),
+                )
+
+        x_grouped = {}
+        x_codes, x_scales = {}, {}
+        we_codes = [keep.tile([P, H], U32, name=f"we_codes{c}", align_bytes=256) for c in range(KP)]
+        we_scales = [keep.tile([P, H], U8, name=f"we_scales{c}", align_bytes=256) for c in range(KP)]
+        wd_codes = keep.tile([P, G], U32, name="wd_codes", align_bytes=256)
+        wd_scales = keep.tile([P, G], U8, name="wd_scales", align_bytes=256)
+
+        def turn_x(g, c, half, engine):
+            bank = psum.tile([P, 2, 2 * P], F32, name="tp", bufs=TB)
+            if g > 0:
+                words = x_sb[g][:, 2 * half : 2 * half + 2, c * GROUP : (c + 1) * GROUP].bitcast(F32)
+            elif c == 0:
+                words = x_first[0][:, 2 * half : 2 * half + 2, :].bitcast(F32)
+            else:
+                words = x_late[half][:].bitcast(F32)
+            for u in (0, 1):
+                for s in (0, 1):
+                    nc.tensor.transpose(
+                        bank[:, u, s * P : (s + 1) * P],
+                        words[:, s, u : 2 * P : 2],
+                        ident32[:],
+                    )
+            if (g, c) not in x_grouped:
+                x_grouped[g, c] = work.tile([P, GROUP, PACK], BF16, name=f"x_grouped{c}", align_bytes=256)
+            dst = x_grouped[g, c][:].bitcast(F32)[:, half * 256 : (half + 1) * 256, :]
+            src = bank[:].rearrange("p u c -> p c u")
+            if engine == "S":
+                nc.scalar.copy(out=dst, in_=src)
+            else:
+                nc.vector.tensor_copy(out=dst, in_=src)
+
+        def quant_x(g, c, parts=1):
+            x_codes[g, c] = work.tile([P, GROUP], U32, name=f"x_codes{c}", align_bytes=256)
+            x_scales[g, c] = work.tile([P, GROUP], U8, name=f"x_scales{c}", align_bytes=256)
+            width = GROUP // parts
+            for i in range(parts):
+                cols = slice(i * width, (i + 1) * width)
+                nc.vector.quantize_mx(
+                    out=x_codes[g, c][:, cols].bitcast(FP8X4),
+                    scales=x_scales[g, c][:, cols],
+                    in_=x_grouped[g, c][:, cols, :].rearrange("p c j -> p (c j)"),
+                )
+
+        w_grouped = {}
+
+        def group_w(c, lo, hi, engine):
+            if c not in w_grouped:
+                w_grouped[c] = work.tile([P, H, PACK], BF16, name="w_grouped", align_bytes=256)
+            dst = w_grouped[c][:].rearrange("p (t m) j -> p t m j", t=PACK)[:, lo:hi]
+            src = w_raw[c][:].rearrange("p j (m t) -> p t m j", t=PACK)[:, lo:hi]
+            if engine == "S":
+                nc.scalar.copy(out=dst, in_=src)
+            else:
+                nc.vector.tensor_copy(out=dst, in_=src)
+
+        def quant_w(c):
+            nc.vector.quantize_mx(
+                out=we_codes[c][:].bitcast(FP8X4), scales=we_scales[c][:], in_=w_grouped[c][:].rearrange("p c j -> p (c j)")
+            )
+
+        wd_wide = [keep.tile([P, PACK, 512], BF16, name=f"wd_wide{n}") for n in range(2)]
+        wd_grouped = {}
+
+        def widen_wd(n):
+            cols = slice(n * 512, (n + 1) * 512)
+            for t in range(PACK):
+                nc.scalar.activation(
+                    out=wd_wide[n][:, t, :],
+                    in_=wd_bytes[:, t, cols].bitcast(E4M3),
+                    func=ACT.Copy,
+                    scale=wsc_sb[:, t : t + 1],
+                )
+
+        def group_wd(n, engine):
+            wd_grouped[n] = work.tile([P, H, PACK], BF16, name="w_grouped", align_bytes=256)
+            src = wd_wide[n][:].rearrange("p t g -> p g t")
+            if engine == "S":
+                nc.scalar.copy(out=wd_grouped[n][:], in_=src)
+            else:
+                nc.vector.tensor_copy(out=wd_grouped[n][:], in_=src)
+
+        def quant_wd(n):
+            cols = slice(n * 512, (n + 1) * 512)
+            nc.vector.quantize_mx(
+                out=wd_codes[:, cols].bitcast(FP8X4),
+                scales=wd_scales[:, cols],
+                in_=wd_grouped[n][:].rearrange("p g t -> p (g t)"),
+            )
+
+        sums = {}
+        h_grouped, h_codes, h_scales = {}, {}, {}
+
+        def encode(g, t):
+            bank = psum.tile([P, GROUP], F32, name="y_bank", bufs=YB)
+            for c in range(KP):
+                nc.tensor.matmul_mx(
+                    out=bank[:],
+                    lhsT=we_codes[c][:, t * P : (t + 1) * P].bitcast(FP8X4),
+                    lhsT_scale=we_scales[c][:, t * P : (t + 1) * P],
+                    rhs=x_codes[g, c][:].bitcast(FP8X4),
+                    rhs_scale=x_scales[g, c][:],
+                    start=(c == 0),
+                    stop=(c == KP - 1),
+                )
+            if g not in sums:
+                sums[g] = work.tile([P, PACK, GROUP], F32, name="sums", bufs=1)
+            if g == 0:
+                lib_row = lib_first[:].rearrange("p (s n) -> p s n", s=PACK)
+            else:
+                lib_row = lib_bc[:, (g - 1) * GROUP : g * GROUP].rearrange("p (n s) -> p s n", s=PACK)
+            nc.vector.scalar_tensor_tensor(
+                out=sums[g][:, t, :].rearrange("p (s n) -> p s n", s=PACK),
+                in0=lib_row,
+                scalar=benc_sb[:, t : t + 1],
+                in1=bank[:].rearrange("p (s n) -> p s n", s=PACK),
+                op0=ALU.mult,
+                op1=ALU.add,
+            )
+
+        def leaky(g, part):
+            if g not in h_grouped:
+                h_grouped[g] = work.tile([P, GROUP, PACK], BF16, name="h_grouped", align_bytes=256)
+            cols = slice(part * 256, (part + 1) * 256)
+            src = sums[g][:, :, cols].rearrange("p t c -> p c t")
+            nc.vector.scalar_tensor_tensor(
+                out=h_grouped[g][:, cols, :], in0=src, scalar=SLOPE, in1=src, op0=ALU.mult, op1=ALU.max
+            )
+
+        def quant_h(g, part):
+            if g not in h_codes:
+                h_codes[g] = work.tile([P, GROUP], U32, name="h_codes", align_bytes=256)
+                h_scales[g] = work.tile([P, GROUP], U8, name="h_scales", align_bytes=256)
+            cols = slice(part * 256, (part + 1) * 256)
+            nc.vector.quantize_mx(
+                out=h_codes[g][:, cols].bitcast(FP8X4),
+                scales=h_scales[g][:, cols],
+                in_=h_grouped[g][:, cols, :].rearrange("p c t -> p (c t)"),
+            )
+
+        z = {}
+
+        def decode(g, s, n):
+            bank = psum.tile([P, 512], F32, name="d_bank", bufs=DB)
+            nc.tensor.matmul_mx(
+                out=bank[:],
+                lhsT=h_codes[g][:, s * P : (s + 1) * P].bitcast(FP8X4),
+                lhsT_scale=h_scales[g][:, s * P : (s + 1) * P],
+                rhs=wd_codes[:, n * 512 : (n + 1) * 512].bitcast(FP8X4),
+                rhs_scale=wd_scales[:, n * 512 : (n + 1) * 512],
+                start=True,
+                stop=True,
+            )
+            if (g, s // 2) not in z:
+                z[g, s // 2] = keep.tile([P, 2, G], F32, name=f"z{g}_{s // 2}")
+            nc.vector.scalar_tensor_tensor(
+                out=z[g, s // 2][:, s % 2, n * 512 : (n + 1) * 512],
+                in0=bank[:],
+                scalar=invlib[:, g, s : s + 1],
+                in1=bdec_bc[n][:],
+                op0=ALU.mult,
+                op1=ALU.add,
+            )
+
+        def exp(g, half):
+            nc.scalar.activation(out=z[g, half][:], in_=z[g, half][:], func=ACT.Exp)
+
+        mean_view = out_mean.rearrange("(g p s) n -> g p s n", p=P, s=PACK)
+
+        def log(g, half):
+            if 2 * g + half < EARLY:
+                pieces = [(0, 2, 0, G)]
+            elif (g, half) != (GROUPS - 1, 1):
+                pieces = [(0, 1, 0, G), (1, 2, 0, G)]
+            else:
+                pieces = [(0, 1, 0, G), (1, 2, 0, 512), (1, 2, 512, G)]
+            for s0, s1, lo, hi in pieces:
+                part = z[g, half][:, s0:s1, lo:hi]
+                nc.scalar.activation(out=part, in_=part, func=ACT.Ln, bias=1.0)
+
+        def finish(g, half):
+            if 2 * g + half < EARLY:
+                pieces = [(0, 2, 0, G)]
+            elif (g, half) != (GROUPS - 1, 1):
+                pieces = [(0, 1, 0, G), (1, 2, 0, G)]
+            else:
+                pieces = [(0, 1, 0, G), (1, 2, 0, 512), (1, 2, 512, G)]
+            for s0, s1, lo, hi in pieces:
+                for s in range(s0, s1):
+                    part = z[g, half][:, s, lo:hi]
+                    nc.vector.tensor_scalar(
+                        out=part,
+                        in0=part,
+                        scalar1=depth_sb[:, g, 2 * half + s : 2 * half + s + 1],
+                        scalar2=None,
+                        op0=ALU.mult,
+                    )
+                nc.sync.dma_start(
+                    out=mean_view[g][:, 2 * half + s0 : 2 * half + s1, lo:hi], in_=z[g, half][:, s0:s1, lo:hi]
+                )
+
+        hc_grouped, hc_codes, hc_scales = {}, {}, {}
+
+        def turn_h(g, tt, engine):
+            bank = psum.tile([P, PACK, P], F32, name="tp", bufs=TB)
+            words = h_grouped[g][:].bitcast(F32)
+            for s in range(PACK):
+                nc.tensor.transpose(bank[:, s, :], words[:, s * P : (s + 1) * P, tt : tt + 1].rearrange("p c o -> p (c o)"), ident32[:])
+            if g not in hc_grouped:
+                hc_grouped[g] = work.tile([P, H, PACK], BF16, name="w_raw" if g < 2 else "w_grouped", align_bytes=256)
+            dst = hc_grouped[g][:, tt * 256 : (tt + 1) * 256, :]
+            src = bank[:].bitcast(BF16).rearrange("p s c -> p c s")
+            if engine == "S":
+                nc.scalar.copy(out=dst, in_=src)
+            else:
+                nc.vector.tensor_copy(out=dst, in_=src)
+
+        def quant_hc(g):
+            hc_codes[g] = keep.tile([P, H], U32, name=f"hc_codes{g}", align_bytes=256)
+            hc_scales[g] = keep.tile([P, H], U8, name=f"hc_scales{g}", align_bytes=256)
+            nc.vector.quantize_mx(
+                out=hc_codes[g][:].bitcast(FP8X4), scales=hc_scales[g][:], in_=hc_grouped[g][:].rearrange("p c j -> p (c j)")
+            )
+
+        q_grouped, q_codes, q_scales = {}, {}, {}
+
+        def turn_q(g):
+            bank = psum.tile([P, 2, 2 * P], F32, name="tp", bufs=TB)
+            words = q_sb[:].bitcast(F32)
+            for u in (0, 1):
+                for b in (0, 1):
+                    nc.tensor.transpose(
+                        bank[:, u, b * P : (b + 1) * P], words[:, b, 256 * g + u : 256 * (g + 1) : 2], ident32[:]
+                    )
+            q_grouped[g] = work.tile([P, R, PACK], BF16, name="q_grouped", align_bytes=256, bufs=4)
+            nc.scalar.copy(out=q_grouped[g][:].bitcast(F32), in_=bank[:].rearrange("p u c -> p c u"))
+
+        def quant_q(g):
+            q_codes[g] = keep.tile([P, R], U32, name=f"q_codes{g}", align_bytes=256)
+            q_scales[g] = keep.tile([P, R], U8, name=f"q_scales{g}", align_bytes=256)
+            nc.vector.quantize_mx(
+                out=q_codes[g][:].bitcast(FP8X4), scales=q_scales[g][:], in_=q_grouped[g][:].rearrange("p c j -> p (c j)")
+            )
+
+        def contrast(b):
+            bank = psum.tile([P, H], F32, name="d_bank", bufs=DB)
+            for g in range(GROUPS):
+                nc.tensor.matmul_mx(
+                    out=bank[:],
+                    lhsT=q_codes[g][:, b * P : (b + 1) * P].bitcast(FP8X4),
+                    lhsT_scale=q_scales[g][:, b * P : (b + 1) * P],
+                    rhs=hc_codes[g][:].bitcast(FP8X4),
+                    rhs_scale=hc_scales[g][:],
+                    start=(g == 0),
+                    stop=(g == GROUPS - 1),
+                )
+            res = work.tile([P, H], F32, name="contrast_sb")
+            nc.vector.tensor_tensor(
+                out=res[:].rearrange("p (m v e) -> p m v e", v=2, e=2),
+                in0=bank[:].rearrange("p (v m e) -> p m v e", v=2, e=2),
+                in1=unit_bc[:].rearrange("p (m v e) -> p m v e", v=2, e=2),
+                op=ALU.mult,
+            )
+            nc.sync.dma_start(out=out_contrast[b * P : (b + 1) * P, :], in_=res[:])
+
+        group_w(1, 0, 4, "V")
+        spread(2)
+        group_w(0, 2, 4, "S")
+        keep_busy(1)
+        quant_w(1)
+        spread(1)
+        keep_busy(1)
+        keep_busy(1)
+        keep_busy(1)
+        turn_x(0, 0, 1, "S")
+        group_w(0, 0, 2, "V")
+        quant_w(0)
+        turn_x(0, 0, 0, "S")
+        keep_busy(1)
+        widen_wd(0)
+        turn_x(0, 1, 0, "S")
+        turn_x(0, 1, 1, "S")
+        spread(0)
+        widen_wd(1)
+        quant_x(0, 0)
+        group_wd(1, "S")
+        keep_busy(1)
+        group_wd(0, "V")
+        quant_x(0, 1, 2)
+        keep_busy(1)
+        keep_busy(1)
+        quant_wd(0)
+        encode(0, 3)
+        encode(0, 2)
+        encode(0, 0)
+        encode(0, 1)
+        turn_x(1, 1, 0, "S")
+        turn_x(1, 0, 0, "S")
+        leaky(0, 0)
+        keep_busy(1)
+        quant_wd(1)
+        keep_busy(1)
+        quant_h(0, 0)
+        turn_x(1, 1, 1, "S")
+        leaky(0, 1)
+        turn_x(1, 0, 1, "S")
+        decode(0, 1, 1)
+        decode(0, 0, 1)
+        turn_x(2, 1, 1, "S")
+        quant_x(1, 0)
+        turn_h(0, 0, "S")
+        decode(0, 0, 0)
+        quant_x(1, 1)
+        quant_h(0, 1)
+        decode(0, 1, 0)
+        turn_h(0, 1, "S")
+        turn_x(2, 0, 1, "S")
+        encode(1, 2)
+        decode(0, 3, 0)
+        encode(1, 3)
+        exp(0, 0)
+        turn_x(2, 1, 0, "S")
+        decode(0, 2, 0)
+        decode(0, 2, 1)
+        encode(1, 0)
+        encode(1, 1)
+        decode(0, 3, 1)
+        leaky(1, 0)
+        turn_q(0)
+        turn_x(2, 0, 0, "S")
+        keep_busy(1)
+        exp(0, 1)
+        quant_h(1, 0)
+        keep_busy(1)
+        turn_x(3, 1, 1, "S")
+        leaky(1, 1)
+        turn_q(1)
+        decode(1, 0, 0)
+        decode(1, 1, 1)
+        turn_h(1, 0, "S")
+        quant_h(1, 1)
+        decode(1, 0, 1)
+        decode(1, 1, 0)
+        turn_x(3, 0, 0, "S")
+        quant_x(2, 0)
+        turn_x(3, 0, 1, "S")
+        exp(1, 0)
+        decode(1, 2, 1)
+        decode(1, 3, 0)
+        quant_x(2, 1)
+        turn_h(1, 1, "S")
+        turn_x(3, 1, 0, "S")
+        decode(1, 3, 1)
+        decode(1, 2, 0)
+        encode(2, 3)
+        quant_q(0)
+        encode(2, 2)
+        quant_x(3, 1)
+        encode(2, 0)
+        encode(2, 1)
+        exp(1, 1)
+        quant_x(3, 0)
+        log(0, 1)
+        log(1, 1)
+        leaky(2, 1)
+        quant_q(1)
+        quant_h(2, 1)
+        turn_q(2)
+        keep_busy(1)
+        log(1, 0)
+        leaky(2, 0)
+        encode(3, 0)
+        decode(2, 3, 1)
+        encode(3, 2)
+        finish(0, 1)
+        encode(3, 1)
+        encode(3, 3)
+        log(0, 0)
+        keep_busy(1)
+        quant_h(2, 0)
+        keep_busy(1)
+        leaky(3, 0)
+        keep_busy(1)
+        decode(2, 0, 1)
+        decode(2, 0, 0)
+        turn_h(2, 1, "S")
+        quant_h(3, 0)
+        decode(2, 1, 1)
+        decode(2, 2, 1)
+        decode(2, 1, 0)
+        turn_h(2, 0, "S")
+        leaky(3, 1)
+        decode(3, 0, 0)
+        keep_busy(1)
+        quant_h(3, 1)
+        exp(2, 0)
+        decode(2, 3, 0)
+        decode(3, 1, 0)
+        decode(2, 2, 0)
+        decode(3, 3, 0)
+        decode(3, 1, 1)
+        decode(3, 0, 1)
+        decode(3, 2, 1)
+        finish(1, 1)
+        decode(3, 3, 1)
+        exp(2, 1)
+        keep_busy(1)
+        decode(3, 2, 0)
+        quant_hc(2)
+        exp(3, 0)
+        finish(1, 0)
+        keep_busy(1)
+        exp(3, 1)
+        log(2, 0)
+        quant_q(2)
+        quant_hc(1)
+        finish(0, 0)
+        keep_busy(1)
+        log(2, 1)
+        turn_h(3, 1, "V")
+        turn_h(3, 0, "V")
+        finish(2, 0)
+        quant_hc(0)
+        turn_q(3)
+        log(3, 0)
+        finish(2, 1)
+        keep_busy(1)
+        quant_q(3)
+        keep_busy(1)
+        log(3, 1)
+        quant_hc(3)
+        finish(3, 0)
+        contrast(1)
+        contrast(0)
+        finish(3, 1)

@@ -6,8 +6,6 @@ from concourse.masks import make_identity
 C, G, H, R = 2048, 1024, 512, 256
 FLOPS = 2 * C * G * H + 2 * C * H * G + 2 * R * C * H
 SLOPE = 0.1
-EARLY = 4
-TB, YB, DB = 3, 2, 3
 
 F32 = mybir.dt.float32
 BF16 = mybir.dt.bfloat16
@@ -20,9 +18,14 @@ ACT = mybir.ActivationFunctionType
 
 P = 128
 PACK = 4
-GROUP = P * PACK
-GROUPS = C // GROUP
-KP = G // GROUP
+PASS = P * PACK
+GROUPS = C // PASS
+PAIRS = 2 * GROUPS
+KP = G // PASS
+BANK = 512
+TURN_BANKS, Y_BANKS, D_BANKS = 2, 2, 3
+HC_BUFS = 4
+SUM_BUFS = 2
 
 
 def tile_library_size_autoencoder_f6_kernel(
@@ -35,508 +38,405 @@ def tile_library_size_autoencoder_f6_kernel(
         psum = ctx.enter_context(tc.psum_pool(name="psum", bufs=2))
         ctx.enter_context(tc.manual_schedule())
 
-        lib_sb = keep.tile([P, GROUPS, PACK], BF16, name="lib_sb")
-        nc.scalar.dma_start(out=lib_sb[:], in_=lib.rearrange("(g p s) -> p g s", p=P, s=PACK))
-        bdec_sb = keep.tile([P, 2, PACK], BF16, name="bdec_sb")
-        nc.scalar.dma_start(out=bdec_sb[:], in_=b_dec.rearrange("(h n m) -> n h m", h=2, m=PACK))
-        benc_sb = keep.tile([P, PACK], BF16, name="benc_sb")
-        nc.scalar.dma_start(out=benc_sb[:], in_=b_enc.rearrange("(p t) -> p t", t=PACK))
-        wsc_sb = keep.tile([P, PACK], F32, name="wsc_sb")
-        nc.scalar.dma_start(out=wsc_sb[:], in_=w_dec_scale.rearrange("(p t) o -> p (t o)", t=PACK))
-        depth_sb = keep.tile([P, GROUPS, PACK], BF16, name="depth_sb")
-        nc.scalar.dma_start(out=depth_sb[:], in_=depth.rearrange("(g p s) -> p g s", p=P, s=PACK))
-
         x_view = x.rearrange("(g p s) k -> g p s k", p=P, s=PACK)
         w_view = w_enc.rearrange("(c p j) n -> c p j n", p=P, j=PACK)
-        x_first = [keep.tile([P, PACK, GROUP], BF16, name="x_first")]
-        x_late = [keep.tile([P, 2, GROUP], BF16, name=f"x_late{half}") for half in range(2)]
-        lib_first = keep.tile([P, GROUP], BF16, name="lib_first")
-        lib_bc = keep.tile([P, C - GROUP], BF16, name="lib_bc")
-        bdec_bc = [keep.tile([P, 512], BF16, name=f"bdec_bc{n}") for n in range(2)]
-        unit_bc = keep.tile([P, H], BF16, name="unit_bc")
-        x_sb = [None] + [keep.tile([P, PACK, G], BF16, name=f"x_sb{g}") for g in range(1, GROUPS)]
-        w_raw = [work.tile([P, PACK, H], BF16, name="w_raw", align_bytes=256) for c in range(KP)]
+        x_sb = [work.tile([P, 2, G], BF16, name="x_pair", align_bytes=256, bufs=PAIRS + 1) for i in range(PAIRS)]
+        w_raw = [keep.tile([P, PACK, H], BF16, name=f"w_raw{c}") for c in range(KP)]
         wd_bytes = keep.tile([P, PACK, G], U8, name="wd_bytes")
         q_sb = keep.tile([P, 2, C], BF16, name="q_sb")
-        for c in range(KP):
-            nc.sync.dma_start(out=w_raw[c][:], in_=w_view[c])
-        nc.sync.dma_start(out=x_first[0][:], in_=x_view[0][:, :, 0:GROUP])
-        for half in range(2):
-            nc.sync.dma_start(
-                out=x_late[half][:], in_=x_view[0][:, 2 * half : 2 * half + 2, GROUP:G]
-            )
+        lib_first = keep.tile([P, PACK], BF16, name="lib_first")
+        lib_rest = keep.tile([P, GROUPS - 1, PACK], BF16, name="lib_rest")
+        depth_sb = keep.tile([P, GROUPS, PACK], BF16, name="depth_sb")
+        wsc_sb = keep.tile([P, PACK], F32, name="wsc_sb")
+        benc_bc = keep.tile([P, H], BF16, name="benc_bc")
+        bdec_bc = keep.tile([P, G], BF16, name="bdec_bc")
+        unit_bc = keep.tile([P, H], BF16, name="unit_bc")
+        benc_sb = keep.tile([P, PACK], BF16, name="benc_sb")
+        bdec_sb = keep.tile([P, 2 * PACK], BF16, name="bdec_sb")
+
+        def load_x(i):
+            nc.sync.dma_start(out=x_sb[i][:], in_=x_view[i // 2][:, 2 * (i % 2) : 2 * (i % 2) + 2, :])
+
+        nc.scalar.dma_start(out=wsc_sb[:], in_=w_dec_scale.rearrange("(p t) o -> p (t o)", t=PACK))
+        nc.scalar.dma_start(out=benc_sb[:], in_=b_enc.rearrange("(n m) -> n m", n=P))
+        nc.scalar.dma_start(
+            out=bdec_sb[:].rearrange("n (h m) -> n h m", h=2), in_=b_dec.rearrange("(h n m) -> n h m", h=2, n=P)
+        )
+        lib_view = lib.rearrange("(g p s) -> p g s", p=P, s=PACK)
+        nc.scalar.dma_start(out=lib_first[:], in_=lib_view[:, 0, :])
         nc.sync.dma_start(out=wd_bytes[:], in_=w_dec_bytes.rearrange("(p t) g -> p t g", t=PACK))
-        nc.sync.dma_start(out=x_sb[1][:], in_=x_view[1])
-        nc.sync.dma_start(out=x_sb[2][:], in_=x_view[2])
-        nc.sync.dma_start(out=lib_bc[:], in_=lib[GROUP:C].partition_broadcast(P))
-        nc.sync.dma_start(out=q_sb[:], in_=q.rearrange("(b r) c -> r b c", r=P))
-        nc.sync.dma_start(out=x_sb[3][:], in_=x_view[3])
+        nc.sync.dma_start(out=w_raw[0][:], in_=w_view[0])
+        load_x(0)
+        nc.sync.dma_start(out=w_raw[1][:], in_=w_view[1])
+        for i in range(1, PAIRS):
+            load_x(i)
+            if i == 2:
+                nc.sync.dma_start(out=lib_rest[:], in_=lib_view[:, 1:, :])
+            if i == 4:
+                nc.sync.dma_start(out=q_sb[:], in_=q.rearrange("(b r) c -> r b c", r=P))
+        nc.sync.dma_start(out=depth_sb[:], in_=depth.rearrange("(g p s) -> p g s", p=P, s=PACK))
         nc.sync.dma_start(out=unit_bc[:], in_=unit.partition_broadcast(P))
 
-        ident32 = keep.tile([P, P], F32, name="ident32")
-        make_identity(nc, ident32[:])
+        ident = keep.tile([P, P], F32, name="ident")
         ident16 = keep.tile([P, P], BF16, name="ident16")
         make_identity(nc, ident16[:])
-        warm = keep.tile([P, 1], F32, name="warm")
-        nc.vector.memset(warm[:], 0.0)
-        nc.scalar.activation(out=warm[:], in_=warm[:], func=ACT.Exp)
+        make_identity(nc, ident[:])
         invlib = keep.tile([P, GROUPS, PACK], F32, name="invlib")
-        nc.vector.reciprocal(out=invlib[:], in_=lib_sb[:])
 
-        dummy_in = keep.tile([P, 512], BF16, name="dummy_in")
-        nc.vector.memset(dummy_in[:], 0.0)
+        def copy(engine, out, in_):
+            if engine == "S":
+                nc.scalar.copy(out=out, in_=in_)
+            elif engine == "V":
+                nc.vector.tensor_copy(out=out, in_=in_)
+            else:
+                nc.gpsimd.tensor_scalar(out=out, in0=in_, scalar1=1.0, scalar2=0.0, op0=ALU.mult, op1=ALU.add)
 
-        def keep_busy(n):
-            for i in range(n):
-                bank = psum.tile([P, 512], F32, name="d_bank", bufs=DB)
-                nc.tensor.matmul(out=bank[:], lhsT=ident16[:], rhs=dummy_in[:], start=True, stop=True)
+        def interleave(engine, grouped, rows, lo, hi):
+            copy(
+                engine,
+                grouped[:, lo:hi, :].rearrange("p (c i) t -> p c t i", i=PACK),
+                rows[:, :, lo:hi].rearrange("p t (c i) -> p c t i", i=PACK),
+            )
 
-        def spread(which):
-            columns = lib_sb[:, 0, :] if which == 0 else bdec_sb[:, which - 1, :]
-            bank = psum.tile([P, PACK, P], F32, name="tp", bufs=TB)
+        def quantize(codes, scales, grouped):
+            nc.vector.quantize_mx(out=codes.bitcast(FP8X4), scales=scales, in_=grouped)
+
+        def mx_tiles(pool, name, width, bufs=None):
+            return (
+                pool.tile([P, width], U32, name=f"{name}_codes", align_bytes=256, bufs=bufs),
+                pool.tile([P, width], U8, name=f"{name}_scales", align_bytes=256, bufs=bufs),
+            )
+
+        def mx_pass(bank, lhs, lhs_cols, rhs, rhs_cols, start, stop):
+            nc.tensor.matmul_mx(
+                out=bank,
+                lhsT=lhs[0][:, lhs_cols].bitcast(FP8X4),
+                lhsT_scale=lhs[1][:, lhs_cols],
+                rhs=rhs[0][:, rhs_cols].bitcast(FP8X4),
+                rhs_scale=rhs[1][:, rhs_cols],
+                start=start,
+                stop=stop,
+            )
+
+        def spread(columns, first, out, pattern, **sizes):
+            bank = psum.tile([P, PACK, P], F32, name="turn_bank", bufs=TURN_BANKS)
             for m in range(PACK):
                 nc.tensor.matmul(
-                    out=bank[:, m, :], lhsT=columns[:, m : m + 1].to_broadcast([P, P]), rhs=ident16[:], start=True, stop=True
+                    out=bank[:, m, :],
+                    lhsT=columns[:, first + m : first + m + 1].to_broadcast([P, P]),
+                    rhs=ident16[:],
+                    start=True,
+                    stop=True,
                 )
-            if which == 0:
-                nc.scalar.copy(out=lib_first[:].rearrange("p (m n) -> p m n", m=PACK), in_=bank[:])
-            else:
-                nc.scalar.copy(
-                    out=bdec_bc[which - 1][:].rearrange("p (n m) -> p n m", m=PACK),
-                    in_=bank[:].rearrange("p m n -> p n m"),
-                )
+            nc.scalar.copy(out=out, in_=bank[:].rearrange(pattern, **sizes))
 
-        x_grouped = {}
-        x_codes, x_scales = {}, {}
-        we_codes = [keep.tile([P, H], U32, name=f"we_codes{c}", align_bytes=256) for c in range(KP)]
-        we_scales = [keep.tile([P, H], U8, name=f"we_scales{c}", align_bytes=256) for c in range(KP)]
-        wd_codes = keep.tile([P, G], U32, name="wd_codes", align_bytes=256)
-        wd_scales = keep.tile([P, G], U8, name="wd_scales", align_bytes=256)
+        def spread_benc():
+            out = benc_bc[:].rearrange("p (u n e) -> p u n e", u=2, e=2)
+            spread(benc_sb, 0, out, "p (u e) n -> p u n e", u=2)
 
-        def turn_x(g, c, half, engine):
-            bank = psum.tile([P, 2, 2 * P], F32, name="tp", bufs=TB)
-            if g > 0:
-                words = x_sb[g][:, 2 * half : 2 * half + 2, c * GROUP : (c + 1) * GROUP].bitcast(F32)
-            elif c == 0:
-                words = x_first[0][:, 2 * half : 2 * half + 2, :].bitcast(F32)
-            else:
-                words = x_late[half][:].bitcast(F32)
-            for u in (0, 1):
-                for s in (0, 1):
-                    nc.tensor.transpose(
-                        bank[:, u, s * P : (s + 1) * P],
-                        words[:, s, u : 2 * P : 2],
-                        ident32[:],
-                    )
-            if (g, c) not in x_grouped:
-                x_grouped[g, c] = work.tile([P, GROUP, PACK], BF16, name=f"x_grouped{c}", align_bytes=256)
-            dst = x_grouped[g, c][:].bitcast(F32)[:, half * 256 : (half + 1) * 256, :]
-            src = bank[:].rearrange("p u c -> p c u")
-            if engine == "S":
-                nc.scalar.copy(out=dst, in_=src)
-            else:
-                nc.vector.tensor_copy(out=dst, in_=src)
+        def spread_bdec(half):
+            out = bdec_bc[:, half * BANK : (half + 1) * BANK].rearrange("p (n m) -> p n m", m=PACK)
+            spread(bdec_sb, half * PACK, out, "p m n -> p n m")
 
-        def quant_x(g, c, parts=1):
-            x_codes[g, c] = work.tile([P, GROUP], U32, name=f"x_codes{c}", align_bytes=256)
-            x_scales[g, c] = work.tile([P, GROUP], U8, name=f"x_scales{c}", align_bytes=256)
-            width = GROUP // parts
-            for i in range(parts):
-                cols = slice(i * width, (i + 1) * width)
-                nc.vector.quantize_mx(
-                    out=x_codes[g, c][:, cols].bitcast(FP8X4),
-                    scales=x_scales[g, c][:, cols],
-                    in_=x_grouped[g, c][:, cols, :].rearrange("p c j -> p (c j)"),
-                )
+        we_grouped = [keep.tile([P, H, PACK], BF16, name=f"we_grouped{c}", align_bytes=256) for c in range(KP)]
+        we_mx = [mx_tiles(keep, f"we{c}", H) for c in range(KP)]
 
-        w_grouped = {}
-
-        def group_w(c, lo, hi, engine):
-            if c not in w_grouped:
-                w_grouped[c] = work.tile([P, H, PACK], BF16, name="w_grouped", align_bytes=256)
-            dst = w_grouped[c][:].rearrange("p (t m) j -> p t m j", t=PACK)[:, lo:hi]
-            src = w_raw[c][:].rearrange("p j (m t) -> p t m j", t=PACK)[:, lo:hi]
-            if engine == "S":
-                nc.scalar.copy(out=dst, in_=src)
-            else:
-                nc.vector.tensor_copy(out=dst, in_=src)
-
-        def quant_w(c):
-            nc.vector.quantize_mx(
-                out=we_codes[c][:].bitcast(FP8X4), scales=we_scales[c][:], in_=w_grouped[c][:].rearrange("p c j -> p (c j)")
+        def group_we(c, lo, hi, engine):
+            copy(
+                engine,
+                we_grouped[c][:].rearrange("p (u m e) j -> p m u e j", u=2, e=2)[:, lo:hi],
+                w_raw[c][:].rearrange("p j (m u e) -> p m u e j", u=2, e=2)[:, lo:hi],
             )
 
-        wd_wide = [keep.tile([P, PACK, 512], BF16, name=f"wd_wide{n}") for n in range(2)]
-        wd_grouped = {}
+        def quant_we(c):
+            quantize(we_mx[c][0][:], we_mx[c][1][:], we_grouped[c][:].rearrange("p c j -> p (c j)"))
 
-        def widen_wd(n):
-            cols = slice(n * 512, (n + 1) * 512)
+        wd_wide_both = keep.tile([P, 2, PACK, BANK], BF16, name="wd_wide")
+        wd_wide = [wd_wide_both[:, n] for n in range(2)]
+        wd_grouped = [keep.tile([P, BANK, PACK], BF16, name=f"wd_grouped{n}", align_bytes=256) for n in range(2)]
+        wd_mx = [mx_tiles(keep, f"wd{n}", BANK) for n in range(2)]
+
+        def widen_wd(n, engine):
             for t in range(PACK):
-                nc.scalar.activation(
-                    out=wd_wide[n][:, t, :],
-                    in_=wd_bytes[:, t, cols].bitcast(E4M3),
-                    func=ACT.Copy,
-                    scale=wsc_sb[:, t : t + 1],
-                )
+                src = wd_bytes[:, t, n * BANK : (n + 1) * BANK].bitcast(E4M3)
+                if engine == "S":
+                    nc.scalar.activation(out=wd_wide[n][:, t, :], in_=src, func=ACT.Copy, scale=wsc_sb[:, t : t + 1])
+                else:
+                    nc.vector.tensor_scalar(
+                        out=wd_wide[n][:, t, :], in0=src, scalar1=wsc_sb[:, t : t + 1], scalar2=None, op0=ALU.mult
+                    )
 
         def group_wd(n, engine):
-            wd_grouped[n] = work.tile([P, H, PACK], BF16, name="w_grouped", align_bytes=256)
-            src = wd_wide[n][:].rearrange("p t g -> p g t")
-            if engine == "S":
-                nc.scalar.copy(out=wd_grouped[n][:], in_=src)
-            else:
-                nc.vector.tensor_copy(out=wd_grouped[n][:], in_=src)
+            interleave(engine, wd_grouped[n], wd_wide[n], 0, BANK)
 
         def quant_wd(n):
-            cols = slice(n * 512, (n + 1) * 512)
-            nc.vector.quantize_mx(
-                out=wd_codes[:, cols].bitcast(FP8X4),
-                scales=wd_scales[:, cols],
-                in_=wd_grouped[n][:].rearrange("p g t -> p (g t)"),
-            )
+            quantize(wd_mx[n][0][:], wd_mx[n][1][:], wd_grouped[n][:].rearrange("p g t -> p (g t)"))
 
-        sums = {}
-        h_grouped, h_codes, h_scales = {}, {}, {}
+        x_grouped, x_mx = {}, {}
 
-        def encode(g, t):
-            bank = psum.tile([P, GROUP], F32, name="y_bank", bufs=YB)
+        def turn_x(i, s, engine):
+            bank = psum.tile([P, KP, 2, P], F32, name="turn_bank", bufs=TURN_BANKS)
+            words = x_sb[i][:, s, :].bitcast(F32)
             for c in range(KP):
-                nc.tensor.matmul_mx(
-                    out=bank[:],
-                    lhsT=we_codes[c][:, t * P : (t + 1) * P].bitcast(FP8X4),
-                    lhsT_scale=we_scales[c][:, t * P : (t + 1) * P],
-                    rhs=x_codes[g, c][:].bitcast(FP8X4),
-                    rhs_scale=x_scales[g, c][:],
-                    start=(c == 0),
-                    stop=(c == KP - 1),
-                )
-            if g not in sums:
-                sums[g] = work.tile([P, PACK, GROUP], F32, name="sums", bufs=1)
-            if g == 0:
-                lib_row = lib_first[:].rearrange("p (s n) -> p s n", s=PACK)
-            else:
-                lib_row = lib_bc[:, (g - 1) * GROUP : g * GROUP].rearrange("p (n s) -> p s n", s=PACK)
+                for u in range(2):
+                    nc.tensor.transpose(bank[:, c, u, :], words[:, 256 * c + u : 256 * (c + 1) : 2], ident[:])
+            if s == 0:
+                x_grouped[i] = work.tile([P, 2, KP, P, PACK], BF16, name="x_pair", align_bytes=256, bufs=PAIRS + 1)
+            copy(engine, x_grouped[i][:, s].bitcast(F32), bank[:].rearrange("p c u n -> p c n u"))
+
+        def turn_pair(i):
+            turn_x(i, 0, "S")
+            turn_x(i, 1, "S")
+
+        def quant_x(i, lo=0, hi=2):
+            if lo == 0:
+                x_mx[i] = mx_tiles(work, "x", 2 * KP * P, bufs=3)
+            cols = slice(lo * KP * P, hi * KP * P)
+            quantize(
+                x_mx[i][0][:, cols], x_mx[i][1][:, cols], x_grouped[i][:, lo:hi].rearrange("p s c n j -> p (s c n j)")
+            )
+
+        y_banks, sums, h_rows, h_grouped, h_mx = {}, {}, {}, {}, {}
+
+        def encode(i, s):
+            y_banks[i, s] = psum.tile([P, H], F32, name="y_bank", bufs=Y_BANKS)
+            for c in range(KP):
+                cols = slice((s * KP + c) * P, (s * KP + c + 1) * P)
+                mx_pass(y_banks[i, s][:], x_mx[i], cols, we_mx[c], slice(0, H), c == 0, c == KP - 1)
+
+        def bias_y(i, s):
+            if s == 0:
+                sums[i] = work.tile([P, 2, H], F32, name="sums", bufs=SUM_BUFS)
+            slot = 2 * (i % 2) + s
             nc.vector.scalar_tensor_tensor(
-                out=sums[g][:, t, :].rearrange("p (s n) -> p s n", s=PACK),
-                in0=lib_row,
-                scalar=benc_sb[:, t : t + 1],
-                in1=bank[:].rearrange("p (s n) -> p s n", s=PACK),
+                out=sums[i][:, s, :],
+                in0=benc_bc[:],
+                scalar=lib_first[:, slot : slot + 1] if i < 2 else lib_rest[:, i // 2 - 1, slot : slot + 1],
+                in1=y_banks[i, s][:],
                 op0=ALU.mult,
                 op1=ALU.add,
             )
 
-        def leaky(g, part):
-            if g not in h_grouped:
-                h_grouped[g] = work.tile([P, GROUP, PACK], BF16, name="h_grouped", align_bytes=256)
-            cols = slice(part * 256, (part + 1) * 256)
-            src = sums[g][:, :, cols].rearrange("p t c -> p c t")
+        def leaky(i):
+            if i % 2 == 0:
+                h_rows[i // 2] = keep.tile([P, PACK * H], BF16, name=f"h_rows{i // 2}")
+            src = sums[i][:].rearrange("p s j -> p (s j)")
             nc.vector.scalar_tensor_tensor(
-                out=h_grouped[g][:, cols, :], in0=src, scalar=SLOPE, in1=src, op0=ALU.mult, op1=ALU.max
+                out=h_rows[i // 2][:, (i % 2) * 2 * H : (i % 2 + 1) * 2 * H],
+                in0=src, scalar=SLOPE, in1=src, op0=ALU.mult, op1=ALU.max,
             )
 
-        def quant_h(g, part):
-            if g not in h_codes:
-                h_codes[g] = work.tile([P, GROUP], U32, name="h_codes", align_bytes=256)
-                h_scales[g] = work.tile([P, GROUP], U8, name="h_scales", align_bytes=256)
-            cols = slice(part * 256, (part + 1) * 256)
-            nc.vector.quantize_mx(
-                out=h_codes[g][:, cols].bitcast(FP8X4),
-                scales=h_scales[g][:, cols],
-                in_=h_grouped[g][:, cols, :].rearrange("p c t -> p (c t)"),
-            )
+        h_banks = {}
 
+        def turn_h(i):
+            bank = psum.tile([P, 2, 2, P], F32, name="h_bank", bufs=1)
+            words = h_rows[i // 2][:, (i % 2) * 2 * H : (i % 2 + 1) * 2 * H].bitcast(F32)
+            for s in range(2):
+                for u in range(2):
+                    nc.tensor.transpose(bank[:, s, u, :], words[:, (2 * s + u) * P : (2 * s + u + 1) * P], ident[:])
+            h_banks[i] = bank
+
+        def copy_h(i, engine):
+            h_grouped[i] = work.tile([P, 2, P, PACK], BF16, name="h_grouped", align_bytes=256)
+            copy(engine, h_grouped[i][:].bitcast(F32), h_banks[i][:].rearrange("p s u n -> p s n u"))
+
+        def quant_h(i):
+            h_mx[i] = mx_tiles(work, "h", 2 * P, bufs=3)
+            quantize(h_mx[i][0][:], h_mx[i][1][:], h_grouped[i][:].rearrange("p s n t -> p (s n t)"))
+
+        d_banks = {}
         z = {}
+        z_names = [f"z{i}" for i in range(PAIRS - 1)] + ["wd_wide"]
 
-        def decode(g, s, n):
-            bank = psum.tile([P, 512], F32, name="d_bank", bufs=DB)
-            nc.tensor.matmul_mx(
-                out=bank[:],
-                lhsT=h_codes[g][:, s * P : (s + 1) * P].bitcast(FP8X4),
-                lhsT_scale=h_scales[g][:, s * P : (s + 1) * P],
-                rhs=wd_codes[:, n * 512 : (n + 1) * 512].bitcast(FP8X4),
-                rhs_scale=wd_scales[:, n * 512 : (n + 1) * 512],
-                start=True,
-                stop=True,
-            )
-            if (g, s // 2) not in z:
-                z[g, s // 2] = keep.tile([P, 2, G], F32, name=f"z{g}_{s // 2}")
+        def decode(i, m):
+            s, n = divmod(m, 2)
+            d_banks[i, m] = psum.tile([P, BANK], F32, name="d_bank", bufs=D_BANKS)
+            mx_pass(d_banks[i, m][:], h_mx[i], slice(s * P, (s + 1) * P), wd_mx[n], slice(0, BANK), True, True)
+
+        def bias_d(i, m):
+            s, n = divmod(m, 2)
+            slot = 2 * (i % 2) + s
+            if i not in z:
+                z[i] = keep.tile([P, 2, G], F32, name=z_names[i])
             nc.vector.scalar_tensor_tensor(
-                out=z[g, s // 2][:, s % 2, n * 512 : (n + 1) * 512],
-                in0=bank[:],
-                scalar=invlib[:, g, s : s + 1],
-                in1=bdec_bc[n][:],
+                out=z[i][:, s, n * BANK : (n + 1) * BANK],
+                in0=d_banks[i, m][:],
+                scalar=invlib[:, i // 2, slot : slot + 1],
+                in1=bdec_bc[:, n * BANK : (n + 1) * BANK],
                 op0=ALU.mult,
                 op1=ALU.add,
             )
 
-        def exp(g, half):
-            nc.scalar.activation(out=z[g, half][:], in_=z[g, half][:], func=ACT.Exp)
+        def exp(i, lo=0, hi=2):
+            part = z[i][:, lo:hi, :]
+            nc.scalar.activation(out=part, in_=part, func=ACT.Exp)
+
+        def log(i, lo=0, hi=2, c0=0, c1=G):
+            part = z[i][:, lo:hi, c0:c1]
+            nc.scalar.activation(out=part, in_=part, func=ACT.Ln, bias=1.0)
 
         mean_view = out_mean.rearrange("(g p s) n -> g p s n", p=P, s=PACK)
 
-        def log(g, half):
-            if 2 * g + half < EARLY:
-                pieces = [(0, 2, 0, G)]
-            elif (g, half) != (GROUPS - 1, 1):
-                pieces = [(0, 1, 0, G), (1, 2, 0, G)]
+        def finish(i, s, engine="V", lo=0, hi=G, paced=False):
+            slot = 2 * (i % 2) + s
+            part = z[i][:, s, lo:hi]
+            res = work.tile([P, G], F32, name="sums", bufs=SUM_BUFS)[:] if paced else part
+            factor = depth_sb[:, i // 2, slot : slot + 1]
+            if engine == "V":
+                nc.vector.tensor_scalar(out=res, in0=part, scalar1=factor, scalar2=None, op0=ALU.mult)
             else:
-                pieces = [(0, 1, 0, G), (1, 2, 0, 512), (1, 2, 512, G)]
-            for s0, s1, lo, hi in pieces:
-                part = z[g, half][:, s0:s1, lo:hi]
-                nc.scalar.activation(out=part, in_=part, func=ACT.Ln, bias=1.0)
+                nc.gpsimd.tensor_scalar(out=res, in0=part, scalar1=factor, scalar2=0.0, op0=ALU.mult, op1=ALU.add)
+            nc.sync.dma_start(out=mean_view[i // 2][:, slot, lo:hi], in_=res)
 
-        def finish(g, half):
-            if 2 * g + half < EARLY:
-                pieces = [(0, 2, 0, G)]
-            elif (g, half) != (GROUPS - 1, 1):
-                pieces = [(0, 1, 0, G), (1, 2, 0, G)]
-            else:
-                pieces = [(0, 1, 0, G), (1, 2, 0, 512), (1, 2, 512, G)]
-            for s0, s1, lo, hi in pieces:
-                for s in range(s0, s1):
-                    part = z[g, half][:, s, lo:hi]
-                    nc.vector.tensor_scalar(
-                        out=part,
-                        in0=part,
-                        scalar1=depth_sb[:, g, 2 * half + s : 2 * half + s + 1],
-                        scalar2=None,
-                        op0=ALU.mult,
-                    )
-                nc.sync.dma_start(
-                    out=mean_view[g][:, 2 * half + s0 : 2 * half + s1, lo:hi], in_=z[g, half][:, s0:s1, lo:hi]
-                )
+        hc_grouped, hc_mx = {}, {}
 
-        hc_grouped, hc_codes, hc_scales = {}, {}, {}
-
-        def turn_h(g, tt, engine):
-            bank = psum.tile([P, PACK, P], F32, name="tp", bufs=TB)
-            words = h_grouped[g][:].bitcast(F32)
-            for s in range(PACK):
-                nc.tensor.transpose(bank[:, s, :], words[:, s * P : (s + 1) * P, tt : tt + 1].rearrange("p c o -> p (c o)"), ident32[:])
-            if g not in hc_grouped:
-                hc_grouped[g] = work.tile([P, H, PACK], BF16, name="w_raw" if g < 2 else "w_grouped", align_bytes=256)
-            dst = hc_grouped[g][:, tt * 256 : (tt + 1) * 256, :]
-            src = bank[:].bitcast(BF16).rearrange("p s c -> p c s")
-            if engine == "S":
-                nc.scalar.copy(out=dst, in_=src)
-            else:
-                nc.vector.tensor_copy(out=dst, in_=src)
+        def group_hc(g, engine):
+            hc_grouped[g] = work.tile([P, H, PACK], BF16, name="hc_grouped", align_bytes=256, bufs=HC_BUFS)
+            interleave(engine, hc_grouped[g], h_rows[g][:].rearrange("p (s j) -> p s j", s=PACK), 0, H)
 
         def quant_hc(g):
-            hc_codes[g] = keep.tile([P, H], U32, name=f"hc_codes{g}", align_bytes=256)
-            hc_scales[g] = keep.tile([P, H], U8, name=f"hc_scales{g}", align_bytes=256)
-            nc.vector.quantize_mx(
-                out=hc_codes[g][:].bitcast(FP8X4), scales=hc_scales[g][:], in_=hc_grouped[g][:].rearrange("p c j -> p (c j)")
+            hc_mx[g] = mx_tiles(keep, f"hc{g}", H)
+            quantize(hc_mx[g][0][:], hc_mx[g][1][:], hc_grouped[g][:].rearrange("p c j -> p (c j)"))
+
+        q_grouped = keep.tile([P, GROUPS, R, PACK], BF16, name="q_grouped", align_bytes=256)
+        q_mx = mx_tiles(keep, "q", GROUPS * R)
+
+        def turn_q(g, engine):
+            bank = psum.tile([P, 2, 2, P], F32, name="turn_bank", bufs=TURN_BANKS)
+            for b in range(2):
+                words = q_sb[:, b, :].bitcast(F32)
+                for u in range(2):
+                    nc.tensor.transpose(bank[:, b, u, :], words[:, 256 * g + u : 256 * (g + 1) : 2], ident[:])
+            copy(
+                engine,
+                q_grouped[:, g].bitcast(F32).rearrange("p (b r) u -> p b r u", b=2),
+                bank[:].rearrange("p b u r -> p b r u"),
             )
 
-        q_grouped, q_codes, q_scales = {}, {}, {}
+        def quant_q():
+            quantize(q_mx[0][:], q_mx[1][:], q_grouped[:].rearrange("p g r j -> p (g r j)"))
 
-        def turn_q(g):
-            bank = psum.tile([P, 2, 2 * P], F32, name="tp", bufs=TB)
-            words = q_sb[:].bitcast(F32)
-            for u in (0, 1):
-                for b in (0, 1):
-                    nc.tensor.transpose(
-                        bank[:, u, b * P : (b + 1) * P], words[:, b, 256 * g + u : 256 * (g + 1) : 2], ident32[:]
-                    )
-            q_grouped[g] = work.tile([P, R, PACK], BF16, name="q_grouped", align_bytes=256, bufs=4)
-            nc.scalar.copy(out=q_grouped[g][:].bitcast(F32), in_=bank[:].rearrange("p u c -> p c u"))
-
-        def quant_q(g):
-            q_codes[g] = keep.tile([P, R], U32, name=f"q_codes{g}", align_bytes=256)
-            q_scales[g] = keep.tile([P, R], U8, name=f"q_scales{g}", align_bytes=256)
-            nc.vector.quantize_mx(
-                out=q_codes[g][:].bitcast(FP8X4), scales=q_scales[g][:], in_=q_grouped[g][:].rearrange("p c j -> p (c j)")
-            )
+        k_banks = {}
 
         def contrast(b):
-            bank = psum.tile([P, H], F32, name="d_bank", bufs=DB)
+            k_banks[b] = psum.tile([P, H], F32, name="y_bank", bufs=Y_BANKS)
             for g in range(GROUPS):
-                nc.tensor.matmul_mx(
-                    out=bank[:],
-                    lhsT=q_codes[g][:, b * P : (b + 1) * P].bitcast(FP8X4),
-                    lhsT_scale=q_scales[g][:, b * P : (b + 1) * P],
-                    rhs=hc_codes[g][:].bitcast(FP8X4),
-                    rhs_scale=hc_scales[g][:],
-                    start=(g == 0),
-                    stop=(g == GROUPS - 1),
-                )
+                cols = slice(g * R + b * P, g * R + (b + 1) * P)
+                mx_pass(k_banks[b][:], q_mx, cols, hc_mx[g], slice(0, H), g == 0, g == GROUPS - 1)
+
+        def finish_contrast(b):
             res = work.tile([P, H], F32, name="contrast_sb")
             nc.vector.tensor_tensor(
-                out=res[:].rearrange("p (m v e) -> p m v e", v=2, e=2),
-                in0=bank[:].rearrange("p (v m e) -> p m v e", v=2, e=2),
-                in1=unit_bc[:].rearrange("p (m v e) -> p m v e", v=2, e=2),
+                out=res[:].rearrange("p (m u e) -> p m u e", u=2, e=2),
+                in0=k_banks[b][:].rearrange("p (u m e) -> p m u e", u=2, e=2),
+                in1=unit_bc[:].rearrange("p (m u e) -> p m u e", u=2, e=2),
                 op=ALU.mult,
             )
             nc.sync.dma_start(out=out_contrast[b * P : (b + 1) * P, :], in_=res[:])
 
-        group_w(1, 0, 4, "V")
-        spread(2)
-        group_w(0, 2, 4, "S")
-        keep_busy(1)
-        quant_w(1)
-        spread(1)
-        keep_busy(1)
-        keep_busy(1)
-        keep_busy(1)
-        turn_x(0, 0, 1, "S")
-        group_w(0, 0, 2, "V")
-        quant_w(0)
-        turn_x(0, 0, 0, "S")
-        keep_busy(1)
-        widen_wd(0)
-        turn_x(0, 1, 0, "S")
-        turn_x(0, 1, 1, "S")
-        spread(0)
-        widen_wd(1)
-        quant_x(0, 0)
-        group_wd(1, "S")
-        keep_busy(1)
+        spread_benc()
+        widen_wd(0, "V")
+        group_we(0, 0, P, "S")
         group_wd(0, "V")
-        quant_x(0, 1, 2)
-        keep_busy(1)
-        keep_busy(1)
+        turn_pair(0)
+        spread_bdec(0)
+        spread_bdec(1)
+        nc.vector.reciprocal(out=invlib[:, 0, :], in_=lib_first[:])
         quant_wd(0)
-        encode(0, 3)
-        encode(0, 2)
+        group_we(1, 0, P, "V")
+        quant_we(0)
+        quant_x(0)
+        quant_we(1)
+        turn_pair(1)
         encode(0, 0)
         encode(0, 1)
-        turn_x(1, 1, 0, "S")
-        turn_x(1, 0, 0, "S")
-        leaky(0, 0)
-        keep_busy(1)
-        quant_wd(1)
-        keep_busy(1)
-        quant_h(0, 0)
-        turn_x(1, 1, 1, "S")
-        leaky(0, 1)
-        turn_x(1, 0, 1, "S")
-        decode(0, 1, 1)
-        decode(0, 0, 1)
-        turn_x(2, 1, 1, "S")
-        quant_x(1, 0)
-        turn_h(0, 0, "S")
-        decode(0, 0, 0)
-        quant_x(1, 1)
-        quant_h(0, 1)
-        decode(0, 1, 0)
-        turn_h(0, 1, "S")
-        turn_x(2, 0, 1, "S")
-        encode(1, 2)
-        decode(0, 3, 0)
-        encode(1, 3)
-        exp(0, 0)
-        turn_x(2, 1, 0, "S")
-        decode(0, 2, 0)
-        decode(0, 2, 1)
+        widen_wd(1, "V")
+        group_wd(1, "S")
+        turn_pair(2)
+        bias_y(0, 0)
+        quant_x(1)
+        bias_y(0, 1)
         encode(1, 0)
         encode(1, 1)
-        decode(0, 3, 1)
-        leaky(1, 0)
-        turn_q(0)
-        turn_x(2, 0, 0, "S")
-        keep_busy(1)
-        exp(0, 1)
-        quant_h(1, 0)
-        keep_busy(1)
-        turn_x(3, 1, 1, "S")
-        leaky(1, 1)
-        turn_q(1)
-        decode(1, 0, 0)
-        decode(1, 1, 1)
-        turn_h(1, 0, "S")
-        quant_h(1, 1)
-        decode(1, 0, 1)
-        decode(1, 1, 0)
-        turn_x(3, 0, 0, "S")
-        quant_x(2, 0)
-        turn_x(3, 0, 1, "S")
-        exp(1, 0)
-        decode(1, 2, 1)
-        decode(1, 3, 0)
-        quant_x(2, 1)
-        turn_h(1, 1, "S")
-        turn_x(3, 1, 0, "S")
-        decode(1, 3, 1)
-        decode(1, 2, 0)
-        encode(2, 3)
-        quant_q(0)
-        encode(2, 2)
-        quant_x(3, 1)
-        encode(2, 0)
-        encode(2, 1)
-        exp(1, 1)
-        quant_x(3, 0)
-        log(0, 1)
-        log(1, 1)
-        leaky(2, 1)
-        quant_q(1)
-        quant_h(2, 1)
-        turn_q(2)
-        keep_busy(1)
-        log(1, 0)
-        leaky(2, 0)
-        encode(3, 0)
-        decode(2, 3, 1)
-        encode(3, 2)
-        finish(0, 1)
-        encode(3, 1)
-        encode(3, 3)
-        log(0, 0)
-        keep_busy(1)
-        quant_h(2, 0)
-        keep_busy(1)
-        leaky(3, 0)
-        keep_busy(1)
-        decode(2, 0, 1)
-        decode(2, 0, 0)
-        turn_h(2, 1, "S")
-        quant_h(3, 0)
-        decode(2, 1, 1)
-        decode(2, 2, 1)
-        decode(2, 1, 0)
-        turn_h(2, 0, "S")
-        leaky(3, 1)
-        decode(3, 0, 0)
-        keep_busy(1)
-        quant_h(3, 1)
-        exp(2, 0)
-        decode(2, 3, 0)
-        decode(3, 1, 0)
-        decode(2, 2, 0)
-        decode(3, 3, 0)
-        decode(3, 1, 1)
-        decode(3, 0, 1)
-        decode(3, 2, 1)
-        finish(1, 1)
-        decode(3, 3, 1)
-        exp(2, 1)
-        keep_busy(1)
-        decode(3, 2, 0)
-        quant_hc(2)
-        exp(3, 0)
-        finish(1, 0)
-        keep_busy(1)
-        exp(3, 1)
-        log(2, 0)
-        quant_q(2)
-        quant_hc(1)
-        finish(0, 0)
-        keep_busy(1)
-        log(2, 1)
-        turn_h(3, 1, "V")
-        turn_h(3, 0, "V")
-        finish(2, 0)
-        quant_hc(0)
-        turn_q(3)
-        log(3, 0)
-        finish(2, 1)
-        keep_busy(1)
-        quant_q(3)
-        keep_busy(1)
-        log(3, 1)
-        quant_hc(3)
-        finish(3, 0)
-        contrast(1)
-        contrast(0)
-        finish(3, 1)
+        nc.vector.reciprocal(out=invlib[:, 1:, :], in_=lib_rest[:])
+        leaky(0)
+        turn_h(0)
+        copy_h(0, "S")
+        turn_pair(3)
+        bias_y(1, 0)
+        bias_y(1, 1)
+        quant_wd(1)
+        for i in range(1, PAIRS + 1):
+            j = i - 1
+            early = i <= PAIRS // 2
+            quant_h(j)
+            for m in range(D_BANKS):
+                decode(j, m)
+            if i == 1:
+                turn_pair(4)
+            elif early:
+                turn_q(i - 2, "S")
+            if i + 1 < PAIRS:
+                quant_x(i + 1)
+            if i == PAIRS:
+                quant_q()
+            if i < PAIRS:
+                leaky(i)
+                turn_h(i)
+            if i in (1, 3, 5):
+                group_hc(i // 2, "G")
+            if early:
+                copy_h(i, "S")
+            bias_d(j, 0)
+            decode(j, 3)
+            if i + 1 < PAIRS:
+                encode(i + 1, 0)
+            bias_d(j, 1)
+            if early:
+                exp(j, 0, 1)
+            if i + 4 < PAIRS:
+                turn_x(i + 4, 0, "S")
+            if i == PAIRS // 2:
+                turn_q(GROUPS - 1, "S")
+            if i + 1 < PAIRS:
+                encode(i + 1, 1)
+            if i + 4 < PAIRS:
+                turn_x(i + 4, 1, "S")
+            bias_d(j, 2)
+            bias_d(j, 3)
+            if early:
+                exp(j, 1, 2)
+            if not early and i < PAIRS:
+                copy_h(i, "V")
+            if i + 1 < PAIRS:
+                bias_y(i + 1, 0)
+                bias_y(i + 1, 1)
+            if i in (6, 7):
+                finish(i - 6, 0, "G", paced=True)
+                finish(i - 6, 1, "G")
+            if i == PAIRS // 2:
+                for k in range(PAIRS // 2):
+                    log(k)
+            if not early and i < PAIRS:
+                exp(j)
+        exp(7, 0, 1)
+        exp(7, 1, 2)
+        for k in (2, 3):
+            finish(k, 0)
+            finish(k, 1)
+        group_hc(3, "V")
+        between = [
+            lambda: quant_hc(0),
+            lambda: quant_hc(1),
+            lambda: quant_hc(2),
+            lambda: (quant_hc(3), contrast(0), contrast(1)),
+            lambda: None,
+            lambda: finish_contrast(0),
+            lambda: finish_contrast(1),
+            lambda: None,
+        ]
+        for k in range(PAIRS // 2, PAIRS):
+            for s in range(2):
+                log(k, s, s + 1)
+                finish(k, s)
+                between[2 * (k - PAIRS // 2) + s]()

@@ -57,13 +57,13 @@ def tile_library_size_autoencoder_f6_kernel(
         def load_x(i):
             nc.sync.dma_start(out=x_sb[i][:], in_=x_view[i // 2][:, 2 * (i % 2) : 2 * (i % 2) + 2, :])
 
-        nc.scalar.dma_start(out=wsc_sb[:], in_=w_dec_scale.rearrange("(p t) o -> p (t o)", t=PACK))
         nc.scalar.dma_start(out=benc_sb[:], in_=b_enc.rearrange("(n m) -> n m", n=P))
+        nc.scalar.dma_start(out=wsc_sb[:], in_=w_dec_scale.rearrange("(p t) o -> p (t o)", t=PACK))
+        lib_view = lib.rearrange("(g p s) -> p g s", p=P, s=PACK)
+        nc.scalar.dma_start(out=lib_first[:], in_=lib_view[:, 0, :])
         nc.scalar.dma_start(
             out=bdec_sb[:].rearrange("n (h m) -> n h m", h=2), in_=b_dec.rearrange("(h n m) -> n h m", h=2, n=P)
         )
-        lib_view = lib.rearrange("(g p s) -> p g s", p=P, s=PACK)
-        nc.scalar.dma_start(out=lib_first[:], in_=lib_view[:, 0, :])
         nc.sync.dma_start(out=wd_bytes[:], in_=w_dec_bytes.rearrange("(p t) g -> p t g", t=PACK))
         nc.sync.dma_start(out=w_raw[0][:], in_=w_view[0])
         load_x(0)
@@ -92,6 +92,9 @@ def tile_library_size_autoencoder_f6_kernel(
                 nc.gpsimd.tensor_scalar(out=out, in0=in_, scalar1=1.0, scalar2=0.0, op0=ALU.mult, op1=ALU.add)
 
         def interleave(engine, grouped, rows, lo, hi):
+            if engine == "G":
+                copy(engine, grouped[:, lo:hi, :], rows[:, :, lo:hi].rearrange("p t c -> p c t"))
+                return
             copy(
                 engine,
                 grouped[:, lo:hi, :].rearrange("p (c i) t -> p c t i", i=PACK),
@@ -119,7 +122,7 @@ def tile_library_size_autoencoder_f6_kernel(
             )
 
         def spread(columns, first, out, pattern, **sizes):
-            bank = psum.tile([P, PACK, P], F32, name="turn_bank", bufs=TURN_BANKS)
+            bank = psum.tile([P, PACK, P], F32, name="d_bank", bufs=D_BANKS)
             for m in range(PACK):
                 nc.tensor.matmul(
                     out=bank[:, m, :],
@@ -137,6 +140,11 @@ def tile_library_size_autoencoder_f6_kernel(
         def spread_bdec(half):
             out = bdec_bc[:, half * BANK : (half + 1) * BANK].rearrange("p (n m) -> p n m", m=PACK)
             spread(bdec_sb, half * PACK, out, "p m n -> p n m")
+
+        def warm(source, count):
+            bank = psum.tile([P, BANK], F32, name="d_bank", bufs=D_BANKS)
+            for n in range(count):
+                nc.tensor.matmul(out=bank[:], lhsT=ident16[:], rhs=source, start=True, stop=True)
 
         we_grouped = [keep.tile([P, H, PACK], BF16, name=f"we_grouped{c}", align_bytes=256) for c in range(KP)]
         we_mx = [mx_tiles(keep, f"we{c}", H) for c in range(KP)]
@@ -174,12 +182,20 @@ def tile_library_size_autoencoder_f6_kernel(
 
         x_grouped, x_mx = {}, {}
 
-        def turn_x(i, s, engine):
+        x_banks = {}
+
+        def turn_x(i, s, engine=None):
             bank = psum.tile([P, KP, 2, P], F32, name="turn_bank", bufs=TURN_BANKS)
             words = x_sb[i][:, s, :].bitcast(F32)
             for c in range(KP):
                 for u in range(2):
                     nc.tensor.transpose(bank[:, c, u, :], words[:, 256 * c + u : 256 * (c + 1) : 2], ident[:])
+            x_banks[i, s] = bank
+            if engine:
+                copy_x(i, s, engine)
+
+        def copy_x(i, s, engine):
+            bank = x_banks[i, s]
             if s == 0:
                 x_grouped[i] = work.tile([P, 2, KP, P, PACK], BF16, name="x_pair", align_bytes=256, bufs=PAIRS + 1)
             copy(engine, x_grouped[i][:, s].bitcast(F32), bank[:].rearrange("p c u n -> p c n u"))
@@ -226,6 +242,16 @@ def tile_library_size_autoencoder_f6_kernel(
                 in0=src, scalar=SLOPE, in1=src, op0=ALU.mult, op1=ALU.max,
             )
 
+        def leaky_split(i):
+            if i % 2 == 0:
+                h_rows[i // 2] = keep.tile([P, PACK * H], BF16, name=f"h_rows{i // 2}")
+            src = sums[i][:].rearrange("p s j -> p (s j)")
+            lift = work.tile([P, 2 * H], F32, name="lift", bufs=1)
+            nc.scalar.activation(out=lift[:], in_=src, func=ACT.Relu, scale=SLOPE - 1.0)
+            nc.gpsimd.tensor_tensor(
+                out=h_rows[i // 2][:, (i % 2) * 2 * H : (i % 2 + 1) * 2 * H], in0=src, in1=lift[:], op=ALU.add
+            )
+
         h_banks = {}
 
         def turn_h(i):
@@ -237,7 +263,7 @@ def tile_library_size_autoencoder_f6_kernel(
             h_banks[i] = bank
 
         def copy_h(i, engine):
-            h_grouped[i] = work.tile([P, 2, P, PACK], BF16, name="h_grouped", align_bytes=256)
+            h_grouped[i] = work.tile([P, 2, P, PACK], BF16, name="h_grouped", align_bytes=256, bufs=1)
             copy(engine, h_grouped[i][:].bitcast(F32), h_banks[i][:].rearrange("p s u n -> p s n u"))
 
         def quant_h(i):
@@ -267,6 +293,21 @@ def tile_library_size_autoencoder_f6_kernel(
                 op1=ALU.add,
             )
 
+        def scale_d(i, m):
+            s, n = divmod(m, 2)
+            slot = 2 * (i % 2) + s
+            if i not in z:
+                z[i] = keep.tile([P, 2, G], F32, name=z_names[i])
+            nc.scalar.activation(
+                out=z[i][:, s, n * BANK : (n + 1) * BANK],
+                in_=d_banks[i, m][:],
+                func=ACT.Copy,
+                scale=invlib[:, i // 2, slot : slot + 1],
+            )
+
+        def add_bdec(i, s):
+            nc.gpsimd.tensor_tensor(out=z[i][:, s, :], in0=z[i][:, s, :], in1=bdec_bc[:], op=ALU.add)
+
         def exp(i, lo=0, hi=2):
             part = z[i][:, lo:hi, :]
             nc.scalar.activation(out=part, in_=part, func=ACT.Exp)
@@ -280,7 +321,11 @@ def tile_library_size_autoencoder_f6_kernel(
         def finish(i, s, engine="V", lo=0, hi=G, paced=False):
             slot = 2 * (i % 2) + s
             part = z[i][:, s, lo:hi]
-            res = work.tile([P, G], F32, name="sums", bufs=SUM_BUFS)[:] if paced else part
+            res = part
+            if paced == "leaky":
+                res = work.tile([P, G], F32, name="sums", bufs=SUM_BUFS)[:]
+            if paced == "q":
+                res = work.tile([P, G], F32, name="h_grouped", align_bytes=256, bufs=1)[:]
             factor = depth_sb[:, i // 2, slot : slot + 1]
             if engine == "V":
                 nc.vector.tensor_scalar(out=res, in0=part, scalar1=factor, scalar2=None, op0=ALU.mult)
@@ -301,16 +346,23 @@ def tile_library_size_autoencoder_f6_kernel(
         q_grouped = keep.tile([P, GROUPS, R, PACK], BF16, name="q_grouped", align_bytes=256)
         q_mx = mx_tiles(keep, "q", GROUPS * R)
 
-        def turn_q(g, engine):
+        q_banks = {}
+
+        def turn_q(g, engine=None):
             bank = psum.tile([P, 2, 2, P], F32, name="turn_bank", bufs=TURN_BANKS)
             for b in range(2):
                 words = q_sb[:, b, :].bitcast(F32)
                 for u in range(2):
                     nc.tensor.transpose(bank[:, b, u, :], words[:, 256 * g + u : 256 * (g + 1) : 2], ident[:])
+            q_banks[g] = bank
+            if engine:
+                copy_q(g, engine)
+
+        def copy_q(g, engine):
             copy(
                 engine,
                 q_grouped[:, g].bitcast(F32).rearrange("p (b r) u -> p b r u", b=2),
-                bank[:].rearrange("p b u r -> p b r u"),
+                q_banks[g][:].rearrange("p b u r -> p b r u"),
             )
 
         def quant_q():
@@ -318,11 +370,12 @@ def tile_library_size_autoencoder_f6_kernel(
 
         k_banks = {}
 
-        def contrast(b):
-            k_banks[b] = psum.tile([P, H], F32, name="y_bank", bufs=Y_BANKS)
-            for g in range(GROUPS):
+        def contrast(g, first, last):
+            for b in range(2):
+                if first:
+                    k_banks[b] = psum.tile([P, H], F32, name="y_bank", bufs=Y_BANKS)
                 cols = slice(g * R + b * P, g * R + (b + 1) * P)
-                mx_pass(k_banks[b][:], q_mx, cols, hc_mx[g], slice(0, H), g == 0, g == GROUPS - 1)
+                mx_pass(k_banks[b][:], q_mx, cols, hc_mx[g], slice(0, H), first, last)
 
         def finish_contrast(b):
             res = work.tile([P, H], F32, name="contrast_sb")
@@ -334,15 +387,16 @@ def tile_library_size_autoencoder_f6_kernel(
             )
             nc.sync.dma_start(out=out_contrast[b * P : (b + 1) * P, :], in_=res[:])
 
-        spread_benc()
         widen_wd(0, "V")
-        group_we(0, 0, P, "S")
-        group_wd(0, "V")
-        turn_pair(0)
+        spread_benc()
+        widen_wd(1, "S")
         spread_bdec(0)
         spread_bdec(1)
+        group_we(0, 0, P, "V")
+        turn_x(0, 0, "S")
+        group_wd(0, "V")
+        turn_x(0, 1, "S")
         nc.vector.reciprocal(out=invlib[:, 0, :], in_=lib_first[:])
-        quant_wd(0)
         group_we(1, 0, P, "V")
         quant_we(0)
         quant_x(0)
@@ -350,11 +404,11 @@ def tile_library_size_autoencoder_f6_kernel(
         turn_pair(1)
         encode(0, 0)
         encode(0, 1)
-        widen_wd(1, "V")
+        quant_wd(0)
         group_wd(1, "S")
         turn_pair(2)
-        bias_y(0, 0)
         quant_x(1)
+        bias_y(0, 0)
         bias_y(0, 1)
         encode(1, 0)
         encode(1, 1)
@@ -368,68 +422,91 @@ def tile_library_size_autoencoder_f6_kernel(
         quant_wd(1)
         for i in range(1, PAIRS + 1):
             j = i - 1
-            early = i <= PAIRS // 2
+            shared = i in ()
             quant_h(j)
             for m in range(D_BANKS):
                 decode(j, m)
-            if i == 1:
-                turn_pair(4)
-            elif early:
-                turn_q(i - 2, "S")
             if i + 1 < PAIRS:
                 quant_x(i + 1)
+            if shared:
+                scale_d(j, 0)
+                decode(j, 3)
+                scale_d(j, 1)
+                add_bdec(j, 0)
+            if i == 1:
+                turn_pair(4)
+            elif i + 1 < PAIRS:
+                encode(i + 1, 0)
+            if i == 5:
+                log(0, 0, 1)
+            if i == 6:
+                log(2)
             if i == PAIRS:
-                quant_q()
+                copy_q(3, "V")
+                finish(2, 0, "G", paced="q")
+                finish(2, 1, "G")
             if i < PAIRS:
                 leaky(i)
                 turn_h(i)
             if i in (1, 3, 5):
                 group_hc(i // 2, "G")
-            if early:
+            if i <= 5:
                 copy_h(i, "S")
-            bias_d(j, 0)
-            decode(j, 3)
-            if i + 1 < PAIRS:
+            if not shared:
+                bias_d(j, 0)
+                decode(j, 3)
+            if i == 1:
                 encode(i + 1, 0)
-            bias_d(j, 1)
-            if early:
-                exp(j, 0, 1)
+            if not shared:
+                bias_d(j, 1)
+                if j < 4:
+                    exp(j, 0, 1)
             if i + 4 < PAIRS:
                 turn_x(i + 4, 0, "S")
-            if i == PAIRS // 2:
-                turn_q(GROUPS - 1, "S")
             if i + 1 < PAIRS:
                 encode(i + 1, 1)
             if i + 4 < PAIRS:
                 turn_x(i + 4, 1, "S")
+            if i == 5:
+                turn_q(3)
+            if 2 <= i <= 3:
+                turn_q(i - 2, "S")
             bias_d(j, 2)
             bias_d(j, 3)
-            if early:
+            if j < 4:
                 exp(j, 1, 2)
-            if not early and i < PAIRS:
+                if shared:
+                    exp(j, 0, 1)
+            if 5 < i < PAIRS:
                 copy_h(i, "V")
             if i + 1 < PAIRS:
                 bias_y(i + 1, 0)
                 bias_y(i + 1, 1)
+            if i == 3:
+                turn_q(2, "S")
+            if i == 5:
+                log(0, 1, 2)
+                log(1)
+            if i == 6:
+                log(3)
             if i in (6, 7):
-                finish(i - 6, 0, "G", paced=True)
+                finish(i - 6, 0, "G", paced="leaky")
                 finish(i - 6, 1, "G")
-            if i == PAIRS // 2:
-                for k in range(PAIRS // 2):
-                    log(k)
-            if not early and i < PAIRS:
-                exp(j)
+            if i == 7:
+                for k in (4, 5, 6):
+                    exp(k)
         exp(7, 0, 1)
         exp(7, 1, 2)
-        for k in (2, 3):
-            finish(k, 0)
-            finish(k, 1)
+        finish(3, 0)
+        finish(3, 1)
         group_hc(3, "V")
+        quant_q()
+        quant_hc(0)
+        contrast(0, True, False)
         between = [
-            lambda: quant_hc(0),
-            lambda: quant_hc(1),
-            lambda: quant_hc(2),
-            lambda: (quant_hc(3), contrast(0), contrast(1)),
+            lambda: (quant_hc(1), contrast(1, False, False)),
+            lambda: (quant_hc(2), contrast(2, False, False)),
+            lambda: (quant_hc(3), contrast(3, False, True)),
             lambda: None,
             lambda: finish_contrast(0),
             lambda: finish_contrast(1),
@@ -437,6 +514,11 @@ def tile_library_size_autoencoder_f6_kernel(
         ]
         for k in range(PAIRS // 2, PAIRS):
             for s in range(2):
-                log(k, s, s + 1)
-                finish(k, s)
-                between[2 * (k - PAIRS // 2) + s]()
+                if (k, s) == (PAIRS - 1, 1):
+                    for lo in (0, BANK):
+                        log(k, s, s + 1, lo, lo + BANK)
+                        finish(k, s, "V", lo, lo + BANK)
+                else:
+                    log(k, s, s + 1)
+                    finish(k, s)
+                    between[2 * (k - PAIRS // 2) + s]()

@@ -26,6 +26,7 @@ BANK = 512
 TURN_BANKS, Y_BANKS, D_BANKS = 2, 2, 3
 HC_BUFS = 4
 SUM_BUFS = 2
+HALF = PAIRS // 2
 
 
 def tile_library_size_autoencoder_f6_kernel(
@@ -57,8 +58,8 @@ def tile_library_size_autoencoder_f6_kernel(
         def load_x(i):
             nc.sync.dma_start(out=x_sb[i][:], in_=x_view[i // 2][:, 2 * (i % 2) : 2 * (i % 2) + 2, :])
 
-        nc.scalar.dma_start(out=benc_sb[:], in_=b_enc.rearrange("(n m) -> n m", n=P))
         nc.scalar.dma_start(out=wsc_sb[:], in_=w_dec_scale.rearrange("(p t) o -> p (t o)", t=PACK))
+        nc.scalar.dma_start(out=benc_sb[:], in_=b_enc.rearrange("(n m) -> n m", n=P))
         lib_view = lib.rearrange("(g p s) -> p g s", p=P, s=PACK)
         nc.scalar.dma_start(out=lib_first[:], in_=lib_view[:, 0, :])
         nc.scalar.dma_start(
@@ -142,7 +143,7 @@ def tile_library_size_autoencoder_f6_kernel(
             spread(bdec_sb, half * PACK, out, "p m n -> p n m")
 
         def warm(source, count):
-            bank = psum.tile([P, BANK], F32, name="d_bank", bufs=D_BANKS)
+            bank = psum.tile([P, BANK], F32, name="y_bank", bufs=Y_BANKS)
             for n in range(count):
                 nc.tensor.matmul(out=bank[:], lhsT=ident16[:], rhs=source, start=True, stop=True)
 
@@ -174,8 +175,8 @@ def tile_library_size_autoencoder_f6_kernel(
                         out=wd_wide[n][:, t, :], in0=src, scalar1=wsc_sb[:, t : t + 1], scalar2=None, op0=ALU.mult
                     )
 
-        def group_wd(n, engine):
-            interleave(engine, wd_grouped[n], wd_wide[n], 0, BANK)
+        def group_wd(n, engine, lo=0, hi=BANK):
+            interleave(engine, wd_grouped[n], wd_wide[n], lo, hi)
 
         def quant_wd(n):
             quantize(wd_mx[n][0][:], wd_mx[n][1][:], wd_grouped[n][:].rearrange("p g t -> p (g t)"))
@@ -305,8 +306,10 @@ def tile_library_size_autoencoder_f6_kernel(
                 scale=invlib[:, i // 2, slot : slot + 1],
             )
 
-        def add_bdec(i, s):
-            nc.gpsimd.tensor_tensor(out=z[i][:, s, :], in0=z[i][:, s, :], in1=bdec_bc[:], op=ALU.add)
+        def add_bdec(i, m):
+            s, n = divmod(m, 2)
+            cols = slice(n * BANK, (n + 1) * BANK)
+            nc.gpsimd.tensor_tensor(out=z[i][:, s, cols], in0=z[i][:, s, cols], in1=bdec_bc[:, cols], op=ALU.add)
 
         def exp(i, lo=0, hi=2):
             part = z[i][:, lo:hi, :]
@@ -325,7 +328,7 @@ def tile_library_size_autoencoder_f6_kernel(
             if paced == "leaky":
                 res = work.tile([P, G], F32, name="sums", bufs=SUM_BUFS)[:]
             if paced == "q":
-                res = work.tile([P, G], F32, name="h_grouped", align_bytes=256, bufs=1)[:]
+                res = keep.tile([P, G], F32, name="q_grouped", align_bytes=256)[:]
             factor = depth_sb[:, i // 2, slot : slot + 1]
             if engine == "V":
                 nc.vector.tensor_scalar(out=res, in0=part, scalar1=factor, scalar2=None, op0=ALU.mult)
@@ -377,6 +380,10 @@ def tile_library_size_autoencoder_f6_kernel(
                 cols = slice(g * R + b * P, g * R + (b + 1) * P)
                 mx_pass(k_banks[b][:], q_mx, cols, hc_mx[g], slice(0, H), first, last)
 
+        def quant_and_contrast(g):
+            quant_hc(g)
+            contrast(g, g == 0, g == GROUPS - 1)
+
         def finish_contrast(b):
             res = work.tile([P, H], F32, name="contrast_sb")
             nc.vector.tensor_tensor(
@@ -396,7 +403,6 @@ def tile_library_size_autoencoder_f6_kernel(
         turn_x(0, 0, "S")
         group_wd(0, "V")
         turn_x(0, 1, "S")
-        nc.vector.reciprocal(out=invlib[:, 0, :], in_=lib_first[:])
         group_we(1, 0, P, "V")
         quant_we(0)
         quant_x(0)
@@ -411,107 +417,94 @@ def tile_library_size_autoencoder_f6_kernel(
         bias_y(0, 0)
         bias_y(0, 1)
         encode(1, 0)
-        encode(1, 1)
-        nc.vector.reciprocal(out=invlib[:, 1:, :], in_=lib_rest[:])
+        turn_x(3, 0)
         leaky(0)
         turn_h(0)
+        copy_x(3, 0, "S")
         copy_h(0, "S")
-        turn_pair(3)
+        encode(1, 1)
+        turn_x(3, 1, "S")
+        turn_q(0, "S")
         bias_y(1, 0)
-        bias_y(1, 1)
         quant_wd(1)
+        nc.vector.reciprocal(out=invlib[:, 0, :], in_=lib_first[:])
+        nc.vector.reciprocal(out=invlib[:, 1:, :], in_=lib_rest[:])
+        bias_y(1, 1)
+        extra_turns = [(turn_x, i, s) for i in range(5, PAIRS) for s in range(2)]
+        extra_turns += [(turn_q, g) for g in range(1, GROUPS)]
+
+        def extra_turn(i, slot):
+            if i < HALF:
+                turn, *which = extra_turns[3 * (i - 1) + slot]
+                turn(*which, "S")
+
         for i in range(1, PAIRS + 1):
             j = i - 1
-            shared = i in ()
+            early = i <= HALF
             quant_h(j)
             for m in range(D_BANKS):
                 decode(j, m)
             if i + 1 < PAIRS:
                 quant_x(i + 1)
-            if shared:
-                scale_d(j, 0)
-                decode(j, 3)
-                scale_d(j, 1)
-                add_bdec(j, 0)
+            if i == PAIRS:
+                quant_q()
             if i == 1:
                 turn_pair(4)
             elif i + 1 < PAIRS:
                 encode(i + 1, 0)
-            if i == 5:
-                log(0, 0, 1)
-            if i == 6:
-                log(2)
-            if i == PAIRS:
-                copy_q(3, "V")
-                finish(2, 0, "G", paced="q")
-                finish(2, 1, "G")
             if i < PAIRS:
                 leaky(i)
-                turn_h(i)
             if i in (1, 3, 5):
                 group_hc(i // 2, "G")
-            if i <= 5:
+            if early:
+                turn_h(i)
                 copy_h(i, "S")
-            if not shared:
-                bias_d(j, 0)
-                decode(j, 3)
+            bias_d(j, 0)
+            decode(j, 3)
+            if not early and i < PAIRS:
+                turn_h(i)
             if i == 1:
                 encode(i + 1, 0)
-            if not shared:
-                bias_d(j, 1)
-                if j < 4:
-                    exp(j, 0, 1)
-            if i + 4 < PAIRS:
-                turn_x(i + 4, 0, "S")
-            if i + 1 < PAIRS:
                 encode(i + 1, 1)
-            if i + 4 < PAIRS:
-                turn_x(i + 4, 1, "S")
-            if i == 5:
-                turn_q(3)
-            if 2 <= i <= 3:
-                turn_q(i - 2, "S")
+            bias_d(j, 1)
+            if early:
+                exp(j, 0, 1)
+            extra_turn(i, 0)
+            if 1 < i < PAIRS - 1:
+                encode(i + 1, 1)
+            extra_turn(i, 1)
             bias_d(j, 2)
+            if i == PAIRS - 1:
+                copy_h(i, "V")
             bias_d(j, 3)
-            if j < 4:
+            if early:
                 exp(j, 1, 2)
-                if shared:
-                    exp(j, 0, 1)
-            if 5 < i < PAIRS:
+            extra_turn(i, 2)
+            if not early and i < PAIRS - 1:
                 copy_h(i, "V")
             if i + 1 < PAIRS:
                 bias_y(i + 1, 0)
                 bias_y(i + 1, 1)
-            if i == 3:
-                turn_q(2, "S")
-            if i == 5:
-                log(0, 1, 2)
-                log(1)
+            if i == HALF:
+                for k in range(HALF):
+                    log(k)
             if i == 6:
-                log(3)
-            if i in (6, 7):
-                finish(i - 6, 0, "G", paced="leaky")
-                finish(i - 6, 1, "G")
+                finish(0, 0, "G", paced="leaky")
+                finish(0, 1, "G")
             if i == 7:
-                for k in (4, 5, 6):
+                finish(1, 0, "G", paced="leaky")
+                for k in range(HALF, PAIRS - 1):
                     exp(k)
+            if i == PAIRS:
+                finish(1, 1, "G", paced="q")
         exp(7, 0, 1)
         exp(7, 1, 2)
-        finish(3, 0)
-        finish(3, 1)
+        for k in (2, 3):
+            finish(k, 0)
+            finish(k, 1)
         group_hc(3, "V")
-        quant_q()
-        quant_hc(0)
-        contrast(0, True, False)
-        between = [
-            lambda: (quant_hc(1), contrast(1, False, False)),
-            lambda: (quant_hc(2), contrast(2, False, False)),
-            lambda: (quant_hc(3), contrast(3, False, True)),
-            lambda: None,
-            lambda: finish_contrast(0),
-            lambda: finish_contrast(1),
-            lambda: None,
-        ]
+        quant_and_contrast(0)
+        between = [lambda g=g: quant_and_contrast(g) for g in range(1, GROUPS)] + [None, lambda: finish_contrast(0), lambda: finish_contrast(1), None]
         for k in range(PAIRS // 2, PAIRS):
             for s in range(2):
                 if (k, s) == (PAIRS - 1, 1):
@@ -521,4 +514,6 @@ def tile_library_size_autoencoder_f6_kernel(
                 else:
                     log(k, s, s + 1)
                     finish(k, s)
-                    between[2 * (k - PAIRS // 2) + s]()
+                    extra = between[2 * (k - PAIRS // 2) + s]
+                    if extra:
+                        extra()

@@ -153,8 +153,8 @@ def tile_library_size_autoencoder_f6_kernel(
         def group_we(c, lo, hi, engine):
             copy(
                 engine,
-                we_grouped[c][:].rearrange("p (u m e) j -> p m u e j", u=2, e=2)[:, lo:hi],
-                w_raw[c][:].rearrange("p j (m u e) -> p m u e j", u=2, e=2)[:, lo:hi],
+                we_grouped[c][:].rearrange("p (u m e) j -> p m u j e", u=2, e=2)[:, lo:hi],
+                w_raw[c][:].rearrange("p j (m u e) -> p m u j e", u=2, e=2)[:, lo:hi],
             )
 
         def quant_we(c):
@@ -284,7 +284,12 @@ def tile_library_size_autoencoder_f6_kernel(
             s, n = divmod(m, 2)
             slot = 2 * (i % 2) + s
             if i not in z:
-                z[i] = keep.tile([P, 2, G], F32, name=z_names[i])
+                if i >= PAIRS - 2:
+                    z[i] = keep.tile([P, 2, G], F32, name=("q_sb", "wd_wide")[i % 2])
+                else:
+                    if i % 2 == 0:
+                        z_group[i // 2] = keep.tile([P, PACK, G], F32, name=f"z{i // 2}")
+                    z[i] = z_group[i // 2][:, 2 * (i % 2) : 2 * (i % 2) + 2, :]
             nc.vector.scalar_tensor_tensor(
                 out=z[i][:, s, n * BANK : (n + 1) * BANK],
                 in0=d_banks[i, m][:],
@@ -298,7 +303,12 @@ def tile_library_size_autoencoder_f6_kernel(
             s, n = divmod(m, 2)
             slot = 2 * (i % 2) + s
             if i not in z:
-                z[i] = keep.tile([P, 2, G], F32, name=z_names[i])
+                if i >= PAIRS - 2:
+                    z[i] = keep.tile([P, 2, G], F32, name=("q_sb", "wd_wide")[i % 2])
+                else:
+                    if i % 2 == 0:
+                        z_group[i // 2] = keep.tile([P, PACK, G], F32, name=f"z{i // 2}")
+                    z[i] = z_group[i // 2][:, 2 * (i % 2) : 2 * (i % 2) + 2, :]
             nc.scalar.activation(
                 out=z[i][:, s, n * BANK : (n + 1) * BANK],
                 in_=d_banks[i, m][:],
@@ -311,9 +321,17 @@ def tile_library_size_autoencoder_f6_kernel(
             cols = slice(n * BANK, (n + 1) * BANK)
             nc.gpsimd.tensor_tensor(out=z[i][:, s, cols], in0=z[i][:, s, cols], in1=bdec_bc[:, cols], op=ALU.add)
 
+        z_group = {}
+
         def exp(i, lo=0, hi=2):
             part = z[i][:, lo:hi, :]
             nc.scalar.activation(out=part, in_=part, func=ACT.Exp)
+
+        def exp_group(g):
+            nc.scalar.activation(out=z_group[g][:], in_=z_group[g][:], func=ACT.Exp)
+
+        def log_group(g):
+            nc.scalar.activation(out=z_group[g][:], in_=z_group[g][:], func=ACT.Ln, bias=1.0)
 
         def log(i, lo=0, hi=2, c0=0, c1=G):
             part = z[i][:, lo:hi, c0:c1]
@@ -456,12 +474,12 @@ def tile_library_size_autoencoder_f6_kernel(
                 leaky(i)
             if i in (1, 3, 5):
                 group_hc(i // 2, "G")
-            if early:
+            if early and i not in (2, 3):
                 turn_h(i)
                 copy_h(i, "S")
             bias_d(j, 0)
             decode(j, 3)
-            if not early and i < PAIRS:
+            if i in (2, 3) or HALF < i < PAIRS:
                 turn_h(i)
             if i == 1:
                 encode(i + 1, 0)
@@ -469,6 +487,8 @@ def tile_library_size_autoencoder_f6_kernel(
             bias_d(j, 1)
             if early:
                 exp(j, 0, 1)
+            if i in (2, 3):
+                copy_h(i, "S")
             extra_turn(i, 0)
             if 1 < i < PAIRS - 1:
                 encode(i + 1, 1)
@@ -486,15 +506,15 @@ def tile_library_size_autoencoder_f6_kernel(
                 bias_y(i + 1, 0)
                 bias_y(i + 1, 1)
             if i == HALF:
-                for k in range(HALF):
-                    log(k)
+                log_group(0)
+                log_group(1)
             if i == 6:
                 finish(0, 0, "G", paced="leaky")
                 finish(0, 1, "G")
             if i == 7:
                 finish(1, 0, "G", paced="leaky")
-                for k in range(HALF, PAIRS - 1):
-                    exp(k)
+                exp_group(2)
+                exp(6)
             if i == PAIRS:
                 finish(1, 1, "G", paced="q")
         exp(7, 0, 1)

@@ -66,8 +66,8 @@ def tile_library_size_autoencoder_f6_kernel(
             out=bdec_sb[:].rearrange("n (h m) -> n h m", h=2), in_=b_dec.rearrange("(h n m) -> n h m", h=2, n=P)
         )
         nc.sync.dma_start(out=wd_bytes[:], in_=w_dec_bytes.rearrange("(p t) g -> p t g", t=PACK))
-        nc.sync.dma_start(out=w_raw[0][:], in_=w_view[0])
         load_x(0)
+        nc.sync.dma_start(out=w_raw[0][:], in_=w_view[0])
         nc.sync.dma_start(out=w_raw[1][:], in_=w_view[1])
         for i in range(1, PAIRS):
             load_x(i)
@@ -143,7 +143,7 @@ def tile_library_size_autoencoder_f6_kernel(
             spread(bdec_sb, half * PACK, out, "p m n -> p n m")
 
         def warm(source, count):
-            bank = psum.tile([P, BANK], F32, name="y_bank", bufs=Y_BANKS)
+            bank = psum.tile([P, BANK], F32, name="d_bank", bufs=D_BANKS)
             for n in range(count):
                 nc.tensor.matmul(out=bank[:], lhsT=ident16[:], rhs=source, start=True, stop=True)
 
@@ -415,12 +415,11 @@ def tile_library_size_autoencoder_f6_kernel(
         widen_wd(0, "V")
         spread_benc()
         widen_wd(1, "S")
+        turn_pair(0)
         spread_bdec(0)
         spread_bdec(1)
-        group_we(0, 0, P, "V")
-        turn_x(0, 0, "S")
         group_wd(0, "V")
-        turn_x(0, 1, "S")
+        group_we(0, 0, P, "V")
         group_we(1, 0, P, "V")
         quant_we(0)
         quant_x(0)

@@ -58,30 +58,36 @@ def tile_library_size_autoencoder_f6_kernel(
         def load_x(i):
             nc.sync.dma_start(out=x_sb[i][:], in_=x_view[i // 2][:, 2 * (i % 2) : 2 * (i % 2) + 2, :])
 
+        lib_view = lib.rearrange("(g p s) -> p g s", p=P, s=PACK)
         nc.scalar.dma_start(out=wsc_sb[:], in_=w_dec_scale.rearrange("(p t) o -> p (t o)", t=PACK))
         nc.scalar.dma_start(out=benc_sb[:], in_=b_enc.rearrange("(n m) -> n m", n=P))
-        lib_view = lib.rearrange("(g p s) -> p g s", p=P, s=PACK)
-        nc.scalar.dma_start(out=lib_first[:], in_=lib_view[:, 0, :])
         nc.scalar.dma_start(
             out=bdec_sb[:].rearrange("n (h m) -> n h m", h=2), in_=b_dec.rearrange("(h n m) -> n h m", h=2, n=P)
         )
-        nc.sync.dma_start(out=wd_bytes[:], in_=w_dec_bytes.rearrange("(p t) g -> p t g", t=PACK))
+        wd_view = w_dec_bytes.rearrange("(p t) g -> p t g", t=PACK)
+        nc.sync.dma_start(out=wd_bytes[:, :2], in_=wd_view[:, :2])
+        nc.sync.dma_start(out=wd_bytes[:, 2:], in_=wd_view[:, 2:])
         load_x(0)
         nc.sync.dma_start(out=w_raw[0][:], in_=w_view[0])
         nc.sync.dma_start(out=w_raw[1][:], in_=w_view[1])
-        for i in range(1, PAIRS):
-            load_x(i)
-            if i == 2:
-                nc.sync.dma_start(out=lib_rest[:], in_=lib_view[:, 1:, :])
-            if i == 4:
-                nc.sync.dma_start(out=q_sb[:], in_=q.rearrange("(b r) c -> r b c", r=P))
+        nc.sync.dma_start(out=lib_first[:], in_=lib_view[:, 0, :])
+        load_x(1)
+        load_x(2)
+        nc.sync.dma_start(out=lib_rest[:], in_=lib_view[:, 1:, :])
+        load_x(3)
+        load_x(4)
+        nc.sync.dma_start(out=q_sb[:], in_=q.rearrange("(b r) c -> r b c", r=P))
+        load_x(5)
+        load_x(6)
+        load_x(7)
         nc.sync.dma_start(out=depth_sb[:], in_=depth.rearrange("(g p s) -> p g s", p=P, s=PACK))
         nc.sync.dma_start(out=unit_bc[:], in_=unit.partition_broadcast(P))
 
         ident = keep.tile([P, P], F32, name="ident")
         ident16 = keep.tile([P, P], BF16, name="ident16")
-        make_identity(nc, ident16[:])
-        make_identity(nc, ident[:])
+        nc.vector.memset(ident[:], 0.0)
+        make_identity(nc, ident[:], nomemset=True)
+        nc.scalar.copy(out=ident16[:], in_=ident[:])
         invlib = keep.tile([P, GROUPS, PACK], F32, name="invlib")
 
         def copy(engine, out, in_):
@@ -413,9 +419,9 @@ def tile_library_size_autoencoder_f6_kernel(
             nc.sync.dma_start(out=out_contrast[b * P : (b + 1) * P, :], in_=res[:])
 
         widen_wd(0, "V")
-        spread_benc()
         widen_wd(1, "S")
         turn_pair(0)
+        spread_benc()
         spread_bdec(0)
         spread_bdec(1)
         group_wd(0, "V")

@@ -21,12 +21,12 @@ PACK = 4
 PASS = P * PACK
 GROUPS = C // PASS
 PAIRS = 2 * GROUPS
+TILES = 2 * PAIRS
 KP = G // PASS
 BANK = 512
 TURN_BANKS, Y_BANKS, D_BANKS = 2, 2, 3
-HC_BUFS = 4
-SUM_BUFS = 2
-HALF = PAIRS // 2
+SUM_BUFS = 3
+Z_BUFS = 8
 
 
 def tile_library_size_autoencoder_f6_kernel(
@@ -41,6 +41,9 @@ def tile_library_size_autoencoder_f6_kernel(
 
         x_view = x.rearrange("(g p s) k -> g p s k", p=P, s=PACK)
         w_view = w_enc.rearrange("(c p j) n -> c p j n", p=P, j=PACK)
+        wd_view = w_dec_bytes.rearrange("(p t) g -> p t g", t=PACK)
+        lib_view = lib.rearrange("(g p s) -> p g s", p=P, s=PACK)
+        mean_view = out_mean.rearrange("(g p s) n -> g p s n", p=P, s=PACK)
         x_sb = [work.tile([P, 2, G], BF16, name="x_pair", align_bytes=256, bufs=PAIRS + 1) for i in range(PAIRS)]
         w_raw = [keep.tile([P, PACK, H], BF16, name=f"w_raw{c}") for c in range(KP)]
         wd_bytes = keep.tile([P, PACK, G], U8, name="wd_bytes")
@@ -54,41 +57,19 @@ def tile_library_size_autoencoder_f6_kernel(
         unit_bc = keep.tile([P, H], BF16, name="unit_bc")
         benc_sb = keep.tile([P, PACK], BF16, name="benc_sb")
         bdec_sb = keep.tile([P, 2 * PACK], BF16, name="bdec_sb")
-
-        def load_x(i):
-            nc.sync.dma_start(out=x_sb[i][:], in_=x_view[i // 2][:, 2 * (i % 2) : 2 * (i % 2) + 2, :])
-
-        lib_view = lib.rearrange("(g p s) -> p g s", p=P, s=PACK)
-        nc.scalar.dma_start(out=wsc_sb[:], in_=w_dec_scale.rearrange("(p t) o -> p (t o)", t=PACK))
-        nc.scalar.dma_start(out=benc_sb[:], in_=b_enc.rearrange("(n m) -> n m", n=P))
-        nc.scalar.dma_start(
-            out=bdec_sb[:].rearrange("n (h m) -> n h m", h=2), in_=b_dec.rearrange("(h n m) -> n h m", h=2, n=P)
-        )
-        wd_view = w_dec_bytes.rearrange("(p t) g -> p t g", t=PACK)
-        nc.sync.dma_start(out=wd_bytes[:, :2], in_=wd_view[:, :2])
-        nc.sync.dma_start(out=wd_bytes[:, 2:], in_=wd_view[:, 2:])
-        load_x(0)
-        nc.sync.dma_start(out=w_raw[0][:], in_=w_view[0])
-        nc.sync.dma_start(out=w_raw[1][:], in_=w_view[1])
-        nc.sync.dma_start(out=lib_first[:], in_=lib_view[:, 0, :])
-        load_x(1)
-        load_x(2)
-        nc.sync.dma_start(out=lib_rest[:], in_=lib_view[:, 1:, :])
-        load_x(3)
-        load_x(4)
-        nc.sync.dma_start(out=q_sb[:], in_=q.rearrange("(b r) c -> r b c", r=P))
-        load_x(5)
-        load_x(6)
-        load_x(7)
-        nc.sync.dma_start(out=depth_sb[:], in_=depth.rearrange("(g p s) -> p g s", p=P, s=PACK))
-        nc.sync.dma_start(out=unit_bc[:], in_=unit.partition_broadcast(P))
-
         ident = keep.tile([P, P], F32, name="ident")
         ident16 = keep.tile([P, P], BF16, name="ident16")
-        nc.vector.memset(ident[:], 0.0)
-        make_identity(nc, ident[:], nomemset=True)
-        nc.scalar.copy(out=ident16[:], in_=ident[:])
         invlib = keep.tile([P, GROUPS, PACK], F32, name="invlib")
+
+        def load_x(i, lo=0, hi=2):
+            first = 2 * (i % 2)
+            nc.sync.dma_start(out=x_sb[i][:, lo:hi], in_=x_view[i // 2][:, first + lo : first + hi, :])
+
+        def load_w(c):
+            nc.sync.dma_start(out=w_raw[c][:], in_=w_view[c])
+
+        def load_wd(lo, hi):
+            nc.sync.dma_start(out=wd_bytes[:, lo:hi], in_=wd_view[:, lo:hi])
 
         def copy(engine, out, in_):
             if engine == "S":
@@ -128,35 +109,31 @@ def tile_library_size_autoencoder_f6_kernel(
                 stop=stop,
             )
 
-        def spread(columns, first, out, pattern, **sizes):
-            bank = psum.tile([P, PACK, P], F32, name="d_bank", bufs=D_BANKS)
+        spread_banks = {}
+
+        def spread(key, columns, first):
+            spread_banks[key] = psum.tile([P, PACK, P], F32, name="d_bank", bufs=D_BANKS)
             for m in range(PACK):
                 nc.tensor.matmul(
-                    out=bank[:, m, :],
+                    out=spread_banks[key][:, m, :],
                     lhsT=columns[:, first + m : first + m + 1].to_broadcast([P, P]),
                     rhs=ident16[:],
                     start=True,
                     stop=True,
                 )
-            nc.scalar.copy(out=out, in_=bank[:].rearrange(pattern, **sizes))
 
-        def spread_benc():
+        def copy_benc(engine):
             out = benc_bc[:].rearrange("p (u n e) -> p u n e", u=2, e=2)
-            spread(benc_sb, 0, out, "p (u e) n -> p u n e", u=2)
+            copy(engine, out, spread_banks["enc"][:].rearrange("p (u e) n -> p u n e", u=2))
 
-        def spread_bdec(half):
+        def copy_bdec(half, engine):
             out = bdec_bc[:, half * BANK : (half + 1) * BANK].rearrange("p (n m) -> p n m", m=PACK)
-            spread(bdec_sb, half * PACK, out, "p m n -> p n m")
-
-        def warm(source, count):
-            bank = psum.tile([P, BANK], F32, name="d_bank", bufs=D_BANKS)
-            for n in range(count):
-                nc.tensor.matmul(out=bank[:], lhsT=ident16[:], rhs=source, start=True, stop=True)
+            copy(engine, out, spread_banks[half][:].rearrange("p m n -> p n m"))
 
         we_grouped = [keep.tile([P, H, PACK], BF16, name=f"we_grouped{c}", align_bytes=256) for c in range(KP)]
         we_mx = [mx_tiles(keep, f"we{c}", H) for c in range(KP)]
 
-        def group_we(c, lo, hi, engine):
+        def group_we(c, engine, lo=0, hi=P):
             copy(
                 engine,
                 we_grouped[c][:].rearrange("p (u m e) j -> p m u j e", u=2, e=2)[:, lo:hi],
@@ -166,13 +143,12 @@ def tile_library_size_autoencoder_f6_kernel(
         def quant_we(c):
             quantize(we_mx[c][0][:], we_mx[c][1][:], we_grouped[c][:].rearrange("p c j -> p (c j)"))
 
-        wd_wide_both = keep.tile([P, 2, PACK, BANK], BF16, name="wd_wide")
-        wd_wide = [wd_wide_both[:, n] for n in range(2)]
+        wd_wide = [keep.tile([P, PACK, BANK], BF16, name=f"wd_wide{n}") for n in range(2)]
         wd_grouped = [keep.tile([P, BANK, PACK], BF16, name=f"wd_grouped{n}", align_bytes=256) for n in range(2)]
         wd_mx = [mx_tiles(keep, f"wd{n}", BANK) for n in range(2)]
 
-        def widen_wd(n, engine):
-            for t in range(PACK):
+        def widen_wd(n, engine, lo=0, hi=PACK):
+            for t in range(lo, hi):
                 src = wd_bytes[:, t, n * BANK : (n + 1) * BANK].bitcast(E4M3)
                 if engine == "S":
                     nc.scalar.activation(out=wd_wide[n][:, t, :], in_=src, func=ACT.Copy, scale=wsc_sb[:, t : t + 1])
@@ -187,29 +163,24 @@ def tile_library_size_autoencoder_f6_kernel(
         def quant_wd(n):
             quantize(wd_mx[n][0][:], wd_mx[n][1][:], wd_grouped[n][:].rearrange("p g t -> p (g t)"))
 
-        x_grouped, x_mx = {}, {}
+        x_grouped, x_mx, x_banks = {}, {}, {}
 
-        x_banks = {}
-
-        def turn_x(i, s, engine=None):
+        def turn_x(i, s):
             bank = psum.tile([P, KP, 2, P], F32, name="turn_bank", bufs=TURN_BANKS)
             words = x_sb[i][:, s, :].bitcast(F32)
             for c in range(KP):
                 for u in range(2):
                     nc.tensor.transpose(bank[:, c, u, :], words[:, 256 * c + u : 256 * (c + 1) : 2], ident[:])
             x_banks[i, s] = bank
-            if engine:
-                copy_x(i, s, engine)
 
-        def copy_x(i, s, engine):
-            bank = x_banks[i, s]
+        def copy_x(i, s, engine="S"):
             if s == 0:
                 x_grouped[i] = work.tile([P, 2, KP, P, PACK], BF16, name="x_pair", align_bytes=256, bufs=PAIRS + 1)
-            copy(engine, x_grouped[i][:, s].bitcast(F32), bank[:].rearrange("p c u n -> p c n u"))
+            copy(engine, x_grouped[i][:, s].bitcast(F32), x_banks[i, s][:].rearrange("p c u n -> p c n u"))
 
-        def turn_pair(i):
-            turn_x(i, 0, "S")
-            turn_x(i, 1, "S")
+        def move_x(i, s, engine="S"):
+            turn_x(i, s)
+            copy_x(i, s, engine)
 
         def quant_x(i, lo=0, hi=2):
             if lo == 0:
@@ -219,7 +190,7 @@ def tile_library_size_autoencoder_f6_kernel(
                 x_mx[i][0][:, cols], x_mx[i][1][:, cols], x_grouped[i][:, lo:hi].rearrange("p s c n j -> p (s c n j)")
             )
 
-        y_banks, sums, h_rows, h_grouped, h_mx = {}, {}, {}, {}, {}
+        y_banks, sums, h_rows, h_grouped, h_mx, h_banks = {}, {}, {}, {}, {}, {}
 
         def encode(i, s):
             y_banks[i, s] = psum.tile([P, H], F32, name="y_bank", bufs=Y_BANKS)
@@ -229,10 +200,10 @@ def tile_library_size_autoencoder_f6_kernel(
 
         def bias_y(i, s):
             if s == 0:
-                sums[i] = work.tile([P, 2, H], F32, name="sums", bufs=SUM_BUFS)
+                sums[i] = work.tile([P, 2 * H], F32, name="sums", bufs=SUM_BUFS)
             slot = 2 * (i % 2) + s
             nc.vector.scalar_tensor_tensor(
-                out=sums[i][:, s, :],
+                out=sums[i][:, s * H : (s + 1) * H],
                 in0=benc_bc[:],
                 scalar=lib_first[:, slot : slot + 1] if i < 2 else lib_rest[:, i // 2 - 1, slot : slot + 1],
                 in1=y_banks[i, s][:],
@@ -243,23 +214,14 @@ def tile_library_size_autoencoder_f6_kernel(
         def leaky(i):
             if i % 2 == 0:
                 h_rows[i // 2] = keep.tile([P, PACK * H], BF16, name=f"h_rows{i // 2}")
-            src = sums[i][:].rearrange("p s j -> p (s j)")
             nc.vector.scalar_tensor_tensor(
                 out=h_rows[i // 2][:, (i % 2) * 2 * H : (i % 2 + 1) * 2 * H],
-                in0=src, scalar=SLOPE, in1=src, op0=ALU.mult, op1=ALU.max,
+                in0=sums[i][:],
+                scalar=SLOPE,
+                in1=sums[i][:],
+                op0=ALU.mult,
+                op1=ALU.max,
             )
-
-        def leaky_split(i):
-            if i % 2 == 0:
-                h_rows[i // 2] = keep.tile([P, PACK * H], BF16, name=f"h_rows{i // 2}")
-            src = sums[i][:].rearrange("p s j -> p (s j)")
-            lift = work.tile([P, 2 * H], F32, name="lift", bufs=1)
-            nc.scalar.activation(out=lift[:], in_=src, func=ACT.Relu, scale=SLOPE - 1.0)
-            nc.gpsimd.tensor_tensor(
-                out=h_rows[i // 2][:, (i % 2) * 2 * H : (i % 2 + 1) * 2 * H], in0=src, in1=lift[:], op=ALU.add
-            )
-
-        h_banks = {}
 
         def turn_h(i):
             bank = psum.tile([P, 2, 2, P], F32, name="h_bank", bufs=1)
@@ -269,7 +231,7 @@ def tile_library_size_autoencoder_f6_kernel(
                     nc.tensor.transpose(bank[:, s, u, :], words[:, (2 * s + u) * P : (2 * s + u + 1) * P], ident[:])
             h_banks[i] = bank
 
-        def copy_h(i, engine):
+        def copy_h(i, engine="S"):
             h_grouped[i] = work.tile([P, 2, P, PACK], BF16, name="h_grouped", align_bytes=256, bufs=1)
             copy(engine, h_grouped[i][:].bitcast(F32), h_banks[i][:].rearrange("p s u n -> p s n u"))
 
@@ -277,9 +239,7 @@ def tile_library_size_autoencoder_f6_kernel(
             h_mx[i] = mx_tiles(work, "h", 2 * P, bufs=3)
             quantize(h_mx[i][0][:], h_mx[i][1][:], h_grouped[i][:].rearrange("p s n t -> p (s n t)"))
 
-        d_banks = {}
-        z = {}
-        z_names = [f"z{i}" for i in range(PAIRS - 1)] + ["wd_wide"]
+        d_banks, z = {}, {}
 
         def decode(i, m):
             s, n = divmod(m, 2)
@@ -289,13 +249,8 @@ def tile_library_size_autoencoder_f6_kernel(
         def bias_d(i, m):
             s, n = divmod(m, 2)
             slot = 2 * (i % 2) + s
-            if i not in z:
-                if i >= PAIRS - 2:
-                    z[i] = keep.tile([P, 2, G], F32, name=("q_sb", "wd_wide")[i % 2])
-                else:
-                    if i % 2 == 0:
-                        z_group[i // 2] = keep.tile([P, PACK, G], F32, name=f"z{i // 2}")
-                    z[i] = z_group[i // 2][:, 2 * (i % 2) : 2 * (i % 2) + 2, :]
+            if m == 0:
+                z[i] = work.tile([P, 2, G], F32, name="z", bufs=Z_BUFS)
             nc.vector.scalar_tensor_tensor(
                 out=z[i][:, s, n * BANK : (n + 1) * BANK],
                 in0=d_banks[i, m][:],
@@ -305,54 +260,19 @@ def tile_library_size_autoencoder_f6_kernel(
                 op1=ALU.add,
             )
 
-        def scale_d(i, m):
-            s, n = divmod(m, 2)
-            slot = 2 * (i % 2) + s
-            if i not in z:
-                if i >= PAIRS - 2:
-                    z[i] = keep.tile([P, 2, G], F32, name=("q_sb", "wd_wide")[i % 2])
-                else:
-                    if i % 2 == 0:
-                        z_group[i // 2] = keep.tile([P, PACK, G], F32, name=f"z{i // 2}")
-                    z[i] = z_group[i // 2][:, 2 * (i % 2) : 2 * (i % 2) + 2, :]
-            nc.scalar.activation(
-                out=z[i][:, s, n * BANK : (n + 1) * BANK],
-                in_=d_banks[i, m][:],
-                func=ACT.Copy,
-                scale=invlib[:, i // 2, slot : slot + 1],
-            )
-
-        def add_bdec(i, m):
-            s, n = divmod(m, 2)
-            cols = slice(n * BANK, (n + 1) * BANK)
-            nc.gpsimd.tensor_tensor(out=z[i][:, s, cols], in0=z[i][:, s, cols], in1=bdec_bc[:, cols], op=ALU.add)
-
-        z_group = {}
-
         def exp(i, lo=0, hi=2):
             part = z[i][:, lo:hi, :]
             nc.scalar.activation(out=part, in_=part, func=ACT.Exp)
-
-        def exp_group(g):
-            nc.scalar.activation(out=z_group[g][:], in_=z_group[g][:], func=ACT.Exp)
-
-        def log_group(g):
-            nc.scalar.activation(out=z_group[g][:], in_=z_group[g][:], func=ACT.Ln, bias=1.0)
 
         def log(i, lo=0, hi=2, c0=0, c1=G):
             part = z[i][:, lo:hi, c0:c1]
             nc.scalar.activation(out=part, in_=part, func=ACT.Ln, bias=1.0)
 
-        mean_view = out_mean.rearrange("(g p s) n -> g p s n", p=P, s=PACK)
-
-        def finish(i, s, engine="V", lo=0, hi=G, paced=False):
+        def finish(i, s, engine="V", lo=0, hi=G, res=None):
             slot = 2 * (i % 2) + s
             part = z[i][:, s, lo:hi]
-            res = part
-            if paced == "leaky":
-                res = work.tile([P, G], F32, name="sums", bufs=SUM_BUFS)[:]
-            if paced == "q":
-                res = keep.tile([P, G], F32, name="q_grouped", align_bytes=256)[:]
+            if res is None:
+                res = part
             factor = depth_sb[:, i // 2, slot : slot + 1]
             if engine == "V":
                 nc.vector.tensor_scalar(out=res, in0=part, scalar1=factor, scalar2=None, op0=ALU.mult)
@@ -363,50 +283,42 @@ def tile_library_size_autoencoder_f6_kernel(
         hc_grouped, hc_mx = {}, {}
 
         def group_hc(g, engine):
-            hc_grouped[g] = work.tile([P, H, PACK], BF16, name="hc_grouped", align_bytes=256, bufs=HC_BUFS)
+            hc_grouped[g] = keep.tile([P, H, PACK], BF16, name=("we_grouped", "wd_grouped")[g // 2] + str(g % 2), align_bytes=256)
             interleave(engine, hc_grouped[g], h_rows[g][:].rearrange("p (s j) -> p s j", s=PACK), 0, H)
 
         def quant_hc(g):
             hc_mx[g] = mx_tiles(keep, f"hc{g}", H)
             quantize(hc_mx[g][0][:], hc_mx[g][1][:], hc_grouped[g][:].rearrange("p c j -> p (c j)"))
 
-        q_grouped = keep.tile([P, GROUPS, R, PACK], BF16, name="q_grouped", align_bytes=256)
+        q_grouped = keep.tile([P, GROUPS * R * PACK], BF16, name="q_grouped", align_bytes=256)
         q_mx = mx_tiles(keep, "q", GROUPS * R)
+        q_banks, k_banks = {}, {}
 
-        q_banks = {}
-
-        def turn_q(g, engine=None):
+        def turn_q(g):
             bank = psum.tile([P, 2, 2, P], F32, name="turn_bank", bufs=TURN_BANKS)
             for b in range(2):
                 words = q_sb[:, b, :].bitcast(F32)
                 for u in range(2):
                     nc.tensor.transpose(bank[:, b, u, :], words[:, 256 * g + u : 256 * (g + 1) : 2], ident[:])
             q_banks[g] = bank
-            if engine:
-                copy_q(g, engine)
 
-        def copy_q(g, engine):
-            copy(
-                engine,
-                q_grouped[:, g].bitcast(F32).rearrange("p (b r) u -> p b r u", b=2),
-                q_banks[g][:].rearrange("p b u r -> p b r u"),
-            )
+        def copy_q(g, engine="S"):
+            words = q_grouped[:, g * R * PACK : (g + 1) * R * PACK].bitcast(F32)
+            copy(engine, words.rearrange("p (b r u) -> p b r u", b=2, u=2), q_banks[g][:].rearrange("p b u r -> p b r u"))
+
+        def move_q(g, engine="S"):
+            turn_q(g)
+            copy_q(g, engine)
 
         def quant_q():
-            quantize(q_mx[0][:], q_mx[1][:], q_grouped[:].rearrange("p g r j -> p (g r j)"))
+            quantize(q_mx[0][:], q_mx[1][:], q_grouped[:])
 
-        k_banks = {}
-
-        def contrast(g, first, last):
+        def contrast(g):
             for b in range(2):
-                if first:
+                if g == 0:
                     k_banks[b] = psum.tile([P, H], F32, name="y_bank", bufs=Y_BANKS)
                 cols = slice(g * R + b * P, g * R + (b + 1) * P)
-                mx_pass(k_banks[b][:], q_mx, cols, hc_mx[g], slice(0, H), first, last)
-
-        def quant_and_contrast(g):
-            quant_hc(g)
-            contrast(g, g == 0, g == GROUPS - 1)
+                mx_pass(k_banks[b][:], q_mx, cols, hc_mx[g], slice(0, H), g == 0, g == GROUPS - 1)
 
         def finish_contrast(b):
             res = work.tile([P, H], F32, name="contrast_sb")
@@ -418,127 +330,168 @@ def tile_library_size_autoencoder_f6_kernel(
             )
             nc.sync.dma_start(out=out_contrast[b * P : (b + 1) * P, :], in_=res[:])
 
+        def load_small():
+            nc.scalar.dma_start(out=wsc_sb[:], in_=w_dec_scale.rearrange("(p t) o -> p (t o)", t=PACK))
+            nc.scalar.dma_start(out=benc_sb[:], in_=b_enc.rearrange("(n m) -> n m", n=P))
+
+        def load_bdec():
+            nc.scalar.dma_start(
+                out=bdec_sb[:].rearrange("n (h m) -> n h m", h=2), in_=b_dec.rearrange("(h n m) -> n h m", h=2, n=P)
+            )
+
+        def identities():
+            nc.vector.memset(ident[:], 0.0)
+            make_identity(nc, ident[:], nomemset=True)
+            nc.scalar.copy(out=ident16[:], in_=ident[:])
+
+        def reciprocals():
+            nc.vector.reciprocal(out=invlib[:, 0, :], in_=lib_first[:])
+            nc.vector.reciprocal(out=invlib[:, 1:, :], in_=lib_rest[:])
+
+        load_small()
+        load_bdec()
+        load_wd(0, 2)
+        load_wd(2, 4)
+        load_w(0)
+        load_x(0, 0, 1)
+        load_w(1)
+        load_x(0, 1, 2)
+        load_x(1)
+        nc.sync.dma_start(out=lib_first[:], in_=lib_view[:, 0, :])
+        load_x(2)
+        load_x(3)
+        nc.sync.dma_start(out=lib_rest[:], in_=lib_view[:, 1:, :])
+        load_x(4)
+        load_x(5)
+        nc.sync.dma_start(out=q_sb[:], in_=q.rearrange("(b r) c -> r b c", r=P))
+        load_x(6)
+        load_x(7)
+        nc.sync.dma_start(out=depth_sb[:], in_=depth.rearrange("(g p s) -> p g s", p=P, s=PACK))
+        nc.sync.dma_start(out=unit_bc[:], in_=unit.partition_broadcast(P))
+        identities()
         widen_wd(0, "V")
-        widen_wd(1, "S")
-        turn_pair(0)
-        spread_benc()
-        spread_bdec(0)
-        spread_bdec(1)
+        widen_wd(1, "S", 0, 2)
+        spread("enc", benc_sb, 0)
+        spread(0, bdec_sb, 0)
+        spread(1, bdec_sb, PACK)
+        widen_wd(1, "S", 2, 4)
+        copy_benc("S")
+        copy_bdec(0, "S")
+        move_x(0, 0)
+        copy_bdec(1, "S")
+        move_x(0, 1)
+        move_x(1, 0)
+        move_x(1, 1)
         group_wd(0, "V")
-        group_we(0, 0, P, "V")
-        group_we(1, 0, P, "V")
+        group_we(0, "V")
+        group_we(1, "V")
         quant_we(0)
-        quant_x(0)
         quant_we(1)
-        turn_pair(1)
+        quant_x(0)
         encode(0, 0)
         encode(0, 1)
         quant_wd(0)
-        group_wd(1, "S")
-        turn_pair(2)
         quant_x(1)
+        group_wd(1, "S")
+        move_x(2, 0)
+        move_x(2, 1)
         bias_y(0, 0)
-        bias_y(0, 1)
         encode(1, 0)
-        turn_x(3, 0)
+        reciprocals()
+        bias_y(0, 1)
+        encode(1, 1)
         leaky(0)
         turn_h(0)
-        copy_x(3, 0, "S")
-        copy_h(0, "S")
-        encode(1, 1)
-        turn_x(3, 1, "S")
-        turn_q(0, "S")
-        bias_y(1, 0)
+        copy_h(0)
+        move_x(3, 0)
+        move_x(3, 1)
         quant_wd(1)
-        nc.vector.reciprocal(out=invlib[:, 0, :], in_=lib_first[:])
-        nc.vector.reciprocal(out=invlib[:, 1:, :], in_=lib_rest[:])
+        bias_y(1, 0)
+        quant_x(2)
+        encode(2, 0)
         bias_y(1, 1)
-        extra_turns = [(turn_x, i, s) for i in range(5, PAIRS) for s in range(2)]
-        extra_turns += [(turn_q, g) for g in range(1, GROUPS)]
+        move_x(4, 0)
+        moves = [(turn_x, copy_x, i, s) for i in range(4, PAIRS) for s in range(2)][1:]
+        moves += [(turn_q, copy_q, g) for g in range(GROUPS)]
 
-        def extra_turn(i, slot):
-            if i < HALF:
-                turn, *which = extra_turns[3 * (i - 1) + slot]
-                turn(*which, "S")
+        def move(count):
+            for n in range(min(count, len(moves))):
+                turn, empty, *which = moves.pop(0)
+                turn(*which)
+                empty(*which)
 
         for i in range(1, PAIRS + 1):
             j = i - 1
-            early = i <= HALF
             quant_h(j)
             for m in range(D_BANKS):
                 decode(j, m)
-            if i + 1 < PAIRS:
-                quant_x(i + 1)
-            if i == PAIRS:
-                quant_q()
-            if i == 1:
-                turn_pair(4)
-            elif i + 1 < PAIRS:
-                encode(i + 1, 0)
+            if i + 2 < PAIRS:
+                quant_x(i + 2)
+            move(2 if i == 1 else 1)
             if i < PAIRS:
                 leaky(i)
+                turn_h(i)
+            if i == PAIRS:
+                quant_q()
             if i in (1, 3, 5):
                 group_hc(i // 2, "G")
-            if early and i not in (2, 3):
-                turn_h(i)
-                copy_h(i, "S")
+            if i in (6, 7):
+                finish(i - 6, 0, "G", res=sums[i][:])
+                finish(i - 6, 1, "G")
+            if i == PAIRS:
+                finish(2, 0, "G", res=q_grouped[:, : 2 * G].bitcast(F32))
             bias_d(j, 0)
             decode(j, 3)
-            if i in (2, 3) or HALF < i < PAIRS:
-                turn_h(i)
-            if i == 1:
-                encode(i + 1, 0)
+            if i + 1 < PAIRS:
                 encode(i + 1, 1)
             bias_d(j, 1)
-            if early:
+            if i <= 4:
+                copy_h(i)
                 exp(j, 0, 1)
-            if i in (2, 3):
-                copy_h(i, "S")
-            extra_turn(i, 0)
-            if 1 < i < PAIRS - 1:
-                encode(i + 1, 1)
-            extra_turn(i, 1)
             bias_d(j, 2)
-            if i == PAIRS - 1:
+            if i == 7:
                 copy_h(i, "V")
             bias_d(j, 3)
-            if early:
-                exp(j, 1, 2)
-            extra_turn(i, 2)
-            if not early and i < PAIRS - 1:
+            if i in (5, 6):
                 copy_h(i, "V")
+            if i <= 4:
+                exp(j, 1, 2)
+            move(2)
             if i + 1 < PAIRS:
                 bias_y(i + 1, 0)
+            if i + 2 < PAIRS:
+                encode(i + 2, 0)
+            if i + 1 < PAIRS:
                 bias_y(i + 1, 1)
-            if i == HALF:
-                log_group(0)
-                log_group(1)
+            if i == 4:
+                for k in range(4):
+                    log(k)
             if i == 6:
-                finish(0, 0, "G", paced="leaky")
-                finish(0, 1, "G")
+                exp(4)
+                exp(5)
             if i == 7:
-                finish(1, 0, "G", paced="leaky")
-                exp_group(2)
                 exp(6)
-            if i == PAIRS:
-                finish(1, 1, "G", paced="q")
         exp(7, 0, 1)
         exp(7, 1, 2)
-        for k in (2, 3):
-            finish(k, 0)
-            finish(k, 1)
+        finish(2, 1)
+        finish(3, 0)
+        finish(3, 1)
         group_hc(3, "V")
-        quant_and_contrast(0)
-        between = [lambda g=g: quant_and_contrast(g) for g in range(1, GROUPS)] + [None, lambda: finish_contrast(0), lambda: finish_contrast(1), None]
-        for k in range(PAIRS // 2, PAIRS):
+        for g in range(GROUPS - 1):
+            quant_hc(g)
+            contrast(g)
+        for k in range(4, PAIRS):
             for s in range(2):
-                if (k, s) == (PAIRS - 1, 1):
+                if (k, s) in ((4, 0), (7, 1)):
                     for lo in (0, BANK):
                         log(k, s, s + 1, lo, lo + BANK)
                         finish(k, s, "V", lo, lo + BANK)
                 else:
                     log(k, s, s + 1)
                     finish(k, s)
-                    extra = between[2 * (k - PAIRS // 2) + s]
-                    if extra:
-                        extra()
+                n = 2 * (k - 4) + s
+                if n == 0:
+                    quant_hc(3)
+                    contrast(3)
+                if n in (1, 2):
+                    finish_contrast(n - 1)

@@ -241,15 +241,18 @@ def tile_library_size_autoencoder_f6_kernel(
 
         d_banks, z = {}, {}
 
-        def decode(i, m):
+        def decode(i, m, spare=False):
             s, n = divmod(m, 2)
-            d_banks[i, m] = psum.tile([P, BANK], F32, name="d_bank", bufs=D_BANKS)
+            if spare:
+                d_banks[i, m] = psum.tile([P, BANK], F32, name="turn_bank", bufs=TURN_BANKS)
+            else:
+                d_banks[i, m] = psum.tile([P, BANK], F32, name="d_bank", bufs=D_BANKS)
             mx_pass(d_banks[i, m][:], h_mx[i], slice(s * P, (s + 1) * P), wd_mx[n], slice(0, BANK), True, True)
 
         def bias_d(i, m):
             s, n = divmod(m, 2)
             slot = 2 * (i % 2) + s
-            if m == 0:
+            if i not in z:
                 z[i] = work.tile([P, 2, G], F32, name="z", bufs=Z_BUFS)
             nc.vector.scalar_tensor_tensor(
                 out=z[i][:, s, n * BANK : (n + 1) * BANK],
@@ -259,6 +262,20 @@ def tile_library_size_autoencoder_f6_kernel(
                 op0=ALU.mult,
                 op1=ALU.add,
             )
+
+        def scale_d(i):
+            z[i] = work.tile([P, 2, G], F32, name="z", bufs=Z_BUFS)
+            slot = 2 * (i % 2)
+            nc.scalar.activation(
+                out=z[i][:, 0, :BANK], in_=d_banks[i, 0][:], func=ACT.Copy, scale=invlib[:, i // 2, slot : slot + 1]
+            )
+
+        def add_bdec(i, res):
+            nc.gpsimd.tensor_tensor(out=res, in0=z[i][:, 0, :BANK], in1=bdec_bc[:, :BANK], op=ALU.add)
+
+        def exp_from(i, res):
+            nc.scalar.activation(out=z[i][:, 0, :BANK], in_=res, func=ACT.Exp)
+            nc.scalar.activation(out=z[i][:, 0, BANK:], in_=z[i][:, 0, BANK:], func=ACT.Exp)
 
         def exp(i, lo=0, hi=2):
             part = z[i][:, lo:hi, :]
@@ -282,9 +299,12 @@ def tile_library_size_autoencoder_f6_kernel(
 
         hc_grouped, hc_mx = {}, {}
 
-        def group_hc(g, engine):
-            hc_grouped[g] = keep.tile([P, H, PACK], BF16, name=("we_grouped", "wd_grouped")[g // 2] + str(g % 2), align_bytes=256)
-            interleave(engine, hc_grouped[g], h_rows[g][:].rearrange("p (s j) -> p s j", s=PACK), 0, H)
+        def group_hc(g, engine, lo=0, hi=H, into=None):
+            if into is not None:
+                hc_grouped[g] = into[:].rearrange("p s c n j -> p (s c n) j")
+            elif lo == 0:
+                hc_grouped[g] = keep.tile([P, H, PACK], BF16, name=("we_grouped", "wd_grouped")[g // 2] + str(g % 2), align_bytes=256)
+            interleave(engine, hc_grouped[g], h_rows[g][:].rearrange("p (s j) -> p s j", s=PACK), lo, hi)
 
         def quant_hc(g):
             hc_mx[g] = mx_tiles(keep, f"hc{g}", H)
@@ -329,6 +349,10 @@ def tile_library_size_autoencoder_f6_kernel(
                 op=ALU.mult,
             )
             nc.sync.dma_start(out=out_contrast[b * P : (b + 1) * P, :], in_=res[:])
+
+        def warm(bank, count):
+            for n in range(count):
+                nc.tensor.matmul(out=bank, lhsT=ident16[:], rhs=benc_bc[:], start=True, stop=True)
 
         def load_small():
             nc.scalar.dma_start(out=wsc_sb[:], in_=w_dec_scale.rearrange("(p t) o -> p (t o)", t=PACK))
@@ -386,8 +410,8 @@ def tile_library_size_autoencoder_f6_kernel(
         group_we(0, "V")
         group_we(1, "V")
         quant_we(0)
-        quant_we(1)
         quant_x(0)
+        quant_we(1)
         encode(0, 0)
         encode(0, 1)
         quant_wd(0)
@@ -412,72 +436,135 @@ def tile_library_size_autoencoder_f6_kernel(
         bias_y(1, 1)
         move_x(4, 0)
         moves = [(turn_x, copy_x, i, s) for i in range(4, PAIRS) for s in range(2)][1:]
-        moves += [(turn_q, copy_q, g) for g in range(GROUPS)]
+        moves += [(turn_q, copy_q, g) for g in range(2)]
 
         def move(count):
-            for n in range(min(count, len(moves))):
+            for n in range(count):
                 turn, empty, *which = moves.pop(0)
                 turn(*which)
                 empty(*which)
 
-        for i in range(1, PAIRS + 1):
-            j = i - 1
+        def open_decoder(j):
             quant_h(j)
             for m in range(D_BANKS):
                 decode(j, m)
-            if i + 2 < PAIRS:
-                quant_x(i + 2)
-            move(2 if i == 1 else 1)
-            if i < PAIRS:
-                leaky(i)
-                turn_h(i)
-            if i == PAIRS:
-                quant_q()
-            if i in (1, 3, 5):
+
+        for i in range(1, 4):
+            j = i - 1
+            open_decoder(j)
+            if i == 2:
+                quant_x(4)
+            if i > 1:
+                move(1)
+            leaky(i)
+            turn_h(i)
+            if i == 1:
+                quant_x(3)
+                copy_h(1)
+                move(1)
+            if i % 2:
                 group_hc(i // 2, "G")
-            if i in (6, 7):
-                finish(i - 6, 0, "G", res=sums[i][:])
-                finish(i - 6, 1, "G")
-            if i == PAIRS:
-                finish(2, 0, "G", res=q_grouped[:, : 2 * G].bitcast(F32))
             bias_d(j, 0)
             decode(j, 3)
+            encode(i + 1, 1)
+            bias_d(j, 1)
+            if i > 1:
+                copy_h(i)
+            exp(j, 0, 1)
+            bias_d(j, 2)
+            bias_d(j, 3)
+            exp(j, 1, 2)
+            move(2)
+            bias_y(i + 1, 0)
+            if i < 3:
+                encode(i + 2, 0)
+            bias_y(i + 1, 1)
+        open_decoder(3)
+        quant_x(5)
+        encode(5, 0)
+        quant_x(6)
+        bias_d(3, 0)
+        decode(3, 3)
+        encode(5, 1)
+        turn_q(2)
+        turn_q(3)
+        bias_d(3, 1)
+        exp(3, 0, 1)
+        bias_d(3, 2)
+        bias_d(3, 3)
+        exp(3, 1, 2)
+        log(0)
+        log(1)
+        leaky(4)
+        turn_h(4)
+        bias_y(5, 0)
+        encode(6, 0)
+        bias_y(5, 1)
+        copy_h(4, "V")
+        quant_x(7)
+        for i in range(5, PAIRS):
+            j = i - 1
+            open_decoder(j)
+            leaky(i)
+            if i == 5:
+                group_hc(2, "G")
+            if i == 6:
+                finish(0, 0, "G", res=sums[i][:])
+                finish(0, 1, "G")
+            if i == 7:
+                finish(1, 0, "G", res=sums[i][:])
+            bias_d(j, 0)
+            if i == 7 or i == 5:
+                turn_h(i)
+            decode(j, 3)
+            if i == 6:
+                turn_h(i)
             if i + 1 < PAIRS:
                 encode(i + 1, 1)
+            if i == 5:
+                copy_h(i, "S")
+                log(2)
+                log(3)
             bias_d(j, 1)
-            if i <= 4:
-                copy_h(i)
-                exp(j, 0, 1)
+            if i == 7:
+                copy_q(2, "V")
+                copy_h(i, "V")
             bias_d(j, 2)
             if i == 7:
-                copy_h(i, "V")
+                quant_h(i)
+                paced = work.tile([P, G], F32, name="h_grouped", align_bytes=256, bufs=1)
+                finish(1, 1, "G", res=paced[:])
+                finish(2, 0, "G")
+                decode(i, 0)
+                decode(i, 1)
             bias_d(j, 3)
-            if i in (5, 6):
-                copy_h(i, "V")
-            if i <= 4:
-                exp(j, 1, 2)
-            move(2)
-            if i + 1 < PAIRS:
+            if i < 7:
                 bias_y(i + 1, 0)
-            if i + 2 < PAIRS:
-                encode(i + 2, 0)
-            if i + 1 < PAIRS:
+                if i + 2 < PAIRS:
+                    encode(i + 2, 0)
+                if i == 6:
+                    copy_h(i, "V")
                 bias_y(i + 1, 1)
-            if i == 4:
-                for k in range(4):
-                    log(k)
+            else:
+                decode(i, 2)
+                copy_q(3, "V")
             if i == 6:
                 exp(4)
                 exp(5)
-            if i == 7:
-                exp(6)
+        exp(6, 0, 1)
+        exp(6, 1, 2)
+        bias_d(7, 0)
+        decode(7, 3)
+        for m in range(1, 4):
+            bias_d(7, m)
+        LEFT = [(2, 1), (3, 0), (3, 1)]
         exp(7, 0, 1)
         exp(7, 1, 2)
-        finish(2, 1)
-        finish(3, 0)
-        finish(3, 1)
+        for k, s in LEFT:
+            finish(k, s)
+        quant_q()
         group_hc(3, "V")
-        for g in range(GROUPS - 1):
+        for g in range(0):
             quant_hc(g)
             contrast(g)
         for k in range(4, PAIRS):
@@ -490,8 +577,8 @@ def tile_library_size_autoencoder_f6_kernel(
                     log(k, s, s + 1)
                     finish(k, s)
                 n = 2 * (k - 4) + s
-                if n == 0:
-                    quant_hc(3)
-                    contrast(3)
-                if n in (1, 2):
-                    finish_contrast(n - 1)
+                if n + 0 < GROUPS:
+                    quant_hc(n + 0)
+                    contrast(n + 0)
+                if n + 0 in (GROUPS, GROUPS + 1):
+                    finish_contrast(n + 0 - GROUPS)

@@ -239,7 +239,7 @@ def tile_library_size_autoencoder_f6_kernel(
             h_mx[i] = mx_tiles(work, "h", 2 * P, bufs=3)
             quantize(h_mx[i][0][:], h_mx[i][1][:], h_grouped[i][:].rearrange("p s n t -> p (s n t)"))
 
-        d_banks, z = {}, {}
+        d_banks, z, z_group = {}, {}, {}
 
         def decode(i, m, spare=False):
             s, n = divmod(m, 2)
@@ -253,7 +253,9 @@ def tile_library_size_autoencoder_f6_kernel(
             s, n = divmod(m, 2)
             slot = 2 * (i % 2) + s
             if i not in z:
-                z[i] = work.tile([P, 2, G], F32, name="z", bufs=Z_BUFS)
+                if i % 2 == 0:
+                    z_group[i // 2] = keep.tile([P, PACK, G], F32, name=f"z{i // 2}")
+                z[i] = z_group[i // 2][:, 2 * (i % 2) : 2 * (i % 2) + 2, :]
             nc.vector.scalar_tensor_tensor(
                 out=z[i][:, s, n * BANK : (n + 1) * BANK],
                 in0=d_banks[i, m][:],
@@ -280,6 +282,12 @@ def tile_library_size_autoencoder_f6_kernel(
         def exp(i, lo=0, hi=2):
             part = z[i][:, lo:hi, :]
             nc.scalar.activation(out=part, in_=part, func=ACT.Exp)
+
+        def exp_group(g):
+            nc.scalar.activation(out=z_group[g][:], in_=z_group[g][:], func=ACT.Exp)
+
+        def log_group(g):
+            nc.scalar.activation(out=z_group[g][:], in_=z_group[g][:], func=ACT.Ln, bias=1.0)
 
         def log(i, lo=0, hi=2, c0=0, c1=G):
             part = z[i][:, lo:hi, c0:c1]
@@ -373,12 +381,11 @@ def tile_library_size_autoencoder_f6_kernel(
             nc.vector.reciprocal(out=invlib[:, 1:, :], in_=lib_rest[:])
 
         load_small()
-        load_bdec()
         load_wd(0, 2)
         load_wd(2, 4)
         load_w(0)
-        load_x(0, 0, 1)
         load_w(1)
+        load_x(0, 0, 1)
         load_x(0, 1, 2)
         load_x(1)
         nc.sync.dma_start(out=lib_first[:], in_=lib_view[:, 0, :])
@@ -386,6 +393,7 @@ def tile_library_size_autoencoder_f6_kernel(
         load_x(3)
         nc.sync.dma_start(out=lib_rest[:], in_=lib_view[:, 1:, :])
         load_x(4)
+        nc.sync.dma_start(out=bdec_bc[:], in_=b_dec.partition_broadcast(P))
         load_x(5)
         nc.sync.dma_start(out=q_sb[:], in_=q.rearrange("(b r) c -> r b c", r=P))
         load_x(6)
@@ -396,34 +404,32 @@ def tile_library_size_autoencoder_f6_kernel(
         widen_wd(0, "V")
         widen_wd(1, "S", 0, 2)
         spread("enc", benc_sb, 0)
-        spread(0, bdec_sb, 0)
-        spread(1, bdec_sb, PACK)
         widen_wd(1, "S", 2, 4)
+        group_wd(0, "S", 256, 512)
         copy_benc("S")
-        copy_bdec(0, "S")
         move_x(0, 0)
-        copy_bdec(1, "S")
         move_x(0, 1)
         move_x(1, 0)
         move_x(1, 1)
-        group_wd(0, "V")
+        group_wd(0, "V", 0, 256)
         group_we(0, "V")
         group_we(1, "V")
         quant_we(0)
-        quant_x(0)
         quant_we(1)
+        quant_x(0, 0, 1)
+        quant_wd(0)
+        quant_x(0, 1, 2)
         encode(0, 0)
         encode(0, 1)
-        quant_wd(0)
-        quant_x(1)
         group_wd(1, "S")
+        bias_y(0, 0)
+        quant_x(1)
         move_x(2, 0)
         move_x(2, 1)
-        bias_y(0, 0)
         encode(1, 0)
-        reciprocals()
         bias_y(0, 1)
         encode(1, 1)
+        reciprocals()
         leaky(0)
         turn_h(0)
         copy_h(0)
@@ -449,11 +455,9 @@ def tile_library_size_autoencoder_f6_kernel(
             for m in range(D_BANKS):
                 decode(j, m)
 
-        for i in range(1, 4):
+        for i in range(1, 3):
             j = i - 1
             open_decoder(j)
-            if i == 2:
-                quant_x(4)
             if i > 1:
                 move(1)
             leaky(i)
@@ -462,11 +466,15 @@ def tile_library_size_autoencoder_f6_kernel(
                 quant_x(3)
                 copy_h(1)
                 move(1)
-            if i % 2:
-                group_hc(i // 2, "G")
+                group_hc(0, "G")
             bias_d(j, 0)
             decode(j, 3)
-            encode(i + 1, 1)
+            if i == 1:
+                encode(2, 1)
+            else:
+                turn_x(6, 1)
+                encode(3, 1)
+                turn_x(7, 0)
             bias_d(j, 1)
             if i > 1:
                 copy_h(i)
@@ -474,27 +482,52 @@ def tile_library_size_autoencoder_f6_kernel(
             bias_d(j, 2)
             bias_d(j, 3)
             exp(j, 1, 2)
-            move(2)
+            if i == 1:
+                move(2)
             bias_y(i + 1, 0)
-            if i < 3:
-                encode(i + 2, 0)
+            if i == 1:
+                encode(3, 0)
             bias_y(i + 1, 1)
+        copy_x(6, 1)
+        copy_x(7, 0)
+        open_decoder(2)
+        leaky(3)
+        turn_h(3)
+        copy_h(3)
+        bias_d(2, 0)
+        decode(2, 3)
+        turn_x(7, 1)
+        turn_q(0)
+        bias_d(2, 1)
+        exp(2, 0, 1)
+        bias_d(2, 2)
+        bias_d(2, 3)
+        exp(2, 1, 2)
+        copy_x(7, 1)
+        copy_q(0)
         open_decoder(3)
+        quant_x(4)
+        encode(4, 0)
         quant_x(5)
-        encode(5, 0)
-        quant_x(6)
+        group_hc(1, "G", into=x_grouped[5])
         bias_d(3, 0)
         decode(3, 3)
-        encode(5, 1)
+        encode(4, 1)
+        turn_q(1)
         turn_q(2)
-        turn_q(3)
         bias_d(3, 1)
         exp(3, 0, 1)
         bias_d(3, 2)
         bias_d(3, 3)
         exp(3, 1, 2)
-        log(0)
-        log(1)
+        copy_q(1)
+        copy_q(2)
+        log_group(0)
+        bias_y(4, 0)
+        encode(5, 0)
+        bias_y(4, 1)
+        encode(5, 1)
+        quant_x(6)
         leaky(4)
         turn_h(4)
         bias_y(5, 0)
@@ -502,6 +535,7 @@ def tile_library_size_autoencoder_f6_kernel(
         bias_y(5, 1)
         copy_h(4, "V")
         quant_x(7)
+        turn_q(3)
         for i in range(5, PAIRS):
             j = i - 1
             open_decoder(j)
@@ -523,11 +557,9 @@ def tile_library_size_autoencoder_f6_kernel(
                 encode(i + 1, 1)
             if i == 5:
                 copy_h(i, "S")
-                log(2)
-                log(3)
+                log_group(1)
             bias_d(j, 1)
             if i == 7:
-                copy_q(2, "V")
                 copy_h(i, "V")
             bias_d(j, 2)
             if i == 7:
@@ -549,8 +581,7 @@ def tile_library_size_autoencoder_f6_kernel(
                 decode(i, 2)
                 copy_q(3, "V")
             if i == 6:
-                exp(4)
-                exp(5)
+                exp_group(2)
         exp(6, 0, 1)
         exp(6, 1, 2)
         bias_d(7, 0)

@@ -358,9 +358,10 @@ def tile_library_size_autoencoder_f6_kernel(
             )
             nc.sync.dma_start(out=out_contrast[b * P : (b + 1) * P, :], in_=res[:])
 
-        def warm(bank, count):
+        def warm(source, count):
+            bank = psum.tile([P, BANK], F32, name="d_bank", bufs=D_BANKS)
             for n in range(count):
-                nc.tensor.matmul(out=bank, lhsT=ident16[:], rhs=benc_bc[:], start=True, stop=True)
+                nc.tensor.matmul(out=bank[:], lhsT=ident16[:], rhs=source, start=True, stop=True)
 
         def load_small():
             nc.scalar.dma_start(out=wsc_sb[:], in_=w_dec_scale.rearrange("(p t) o -> p (t o)", t=PACK))
@@ -381,6 +382,7 @@ def tile_library_size_autoencoder_f6_kernel(
             nc.vector.reciprocal(out=invlib[:, 1:, :], in_=lib_rest[:])
 
         load_small()
+        load_bdec()
         load_wd(0, 2)
         load_wd(2, 4)
         load_w(0)
@@ -393,7 +395,6 @@ def tile_library_size_autoencoder_f6_kernel(
         load_x(3)
         nc.sync.dma_start(out=lib_rest[:], in_=lib_view[:, 1:, :])
         load_x(4)
-        nc.sync.dma_start(out=bdec_bc[:], in_=b_dec.partition_broadcast(P))
         load_x(5)
         nc.sync.dma_start(out=q_sb[:], in_=q.rearrange("(b r) c -> r b c", r=P))
         load_x(6)
@@ -404,6 +405,8 @@ def tile_library_size_autoencoder_f6_kernel(
         widen_wd(0, "V")
         widen_wd(1, "S", 0, 2)
         spread("enc", benc_sb, 0)
+        spread(0, bdec_sb, 0)
+        spread(1, bdec_sb, PACK)
         widen_wd(1, "S", 2, 4)
         group_wd(0, "S", 256, 512)
         copy_benc("S")
@@ -426,6 +429,7 @@ def tile_library_size_autoencoder_f6_kernel(
         quant_x(1)
         move_x(2, 0)
         move_x(2, 1)
+        copy_bdec(0, "S")
         encode(1, 0)
         bias_y(0, 1)
         encode(1, 1)
@@ -435,6 +439,7 @@ def tile_library_size_autoencoder_f6_kernel(
         copy_h(0)
         move_x(3, 0)
         move_x(3, 1)
+        copy_bdec(1, "S")
         quant_wd(1)
         bias_y(1, 0)
         quant_x(2)

@@ -165,8 +165,11 @@ def tile_library_size_autoencoder_f6_kernel(
 
         x_grouped, x_mx, x_banks = {}, {}, {}
 
-        def turn_x(i, s):
-            bank = psum.tile([P, KP, 2, P], F32, name="turn_bank", bufs=TURN_BANKS)
+        def turn_x(i, s, name="turn_bank", bufs=TURN_BANKS, into=None):
+            if into is None:
+                bank = psum.tile([P, KP, 2, P], F32, name=name, bufs=bufs)
+            else:
+                bank = into[:].rearrange("p (c u n) -> p c u n", c=KP, u=2)
             words = x_sb[i][:, s, :].bitcast(F32)
             for c in range(KP):
                 for u in range(2):
@@ -211,14 +214,15 @@ def tile_library_size_autoencoder_f6_kernel(
                 op1=ALU.add,
             )
 
-        def leaky(i):
-            if i % 2 == 0:
+        def leaky(i, lo=0, hi=2):
+            if i % 2 == 0 and lo == 0:
                 h_rows[i // 2] = keep.tile([P, PACK * H], BF16, name=f"h_rows{i // 2}")
+            first = 2 * (i % 2)
             nc.vector.scalar_tensor_tensor(
-                out=h_rows[i // 2][:, (i % 2) * 2 * H : (i % 2 + 1) * 2 * H],
-                in0=sums[i][:],
+                out=h_rows[i // 2][:, (first + lo) * H : (first + hi) * H],
+                in0=sums[i][:, lo * H : hi * H],
                 scalar=SLOPE,
-                in1=sums[i][:],
+                in1=sums[i][:, lo * H : hi * H],
                 op0=ALU.mult,
                 op1=ALU.max,
             )
@@ -358,8 +362,8 @@ def tile_library_size_autoencoder_f6_kernel(
             )
             nc.sync.dma_start(out=out_contrast[b * P : (b + 1) * P, :], in_=res[:])
 
-        def warm(source, count):
-            bank = psum.tile([P, BANK], F32, name="d_bank", bufs=D_BANKS)
+        def warm(source, count, name="h_bank", bufs=1):
+            bank = psum.tile([P, BANK], F32, name=name, bufs=bufs)
             for n in range(count):
                 nc.tensor.matmul(out=bank[:], lhsT=ident16[:], rhs=source, start=True, stop=True)
 
@@ -410,9 +414,12 @@ def tile_library_size_autoencoder_f6_kernel(
         widen_wd(1, "S", 2, 4)
         group_wd(0, "S", 256, 512)
         copy_benc("S")
+        copy_bdec(0, "S")
         move_x(0, 0)
         move_x(0, 1)
-        move_x(1, 0)
+        copy_bdec(1, "S")
+        turn_x(1, 0, "h_bank", 1)
+        copy_x(1, 0)
         move_x(1, 1)
         group_wd(0, "V", 0, 256)
         group_we(0, "V")
@@ -429,118 +436,115 @@ def tile_library_size_autoencoder_f6_kernel(
         quant_x(1)
         move_x(2, 0)
         move_x(2, 1)
-        copy_bdec(0, "S")
         encode(1, 0)
         bias_y(0, 1)
-        encode(1, 1)
+        turn_x(3, 0, "d_bank", D_BANKS)
+        copy_x(3, 0)
         reciprocals()
         leaky(0)
         turn_h(0)
+        encode(1, 1)
         copy_h(0)
-        move_x(3, 0)
         move_x(3, 1)
-        copy_bdec(1, "S")
+        move_x(4, 0)
         quant_wd(1)
         bias_y(1, 0)
         quant_x(2)
         encode(2, 0)
         bias_y(1, 1)
-        move_x(4, 0)
-        moves = [(turn_x, copy_x, i, s) for i in range(4, PAIRS) for s in range(2)][1:]
-        moves += [(turn_q, copy_q, g) for g in range(2)]
-
-        def move(count):
-            for n in range(count):
-                turn, empty, *which = moves.pop(0)
-                turn(*which)
-                empty(*which)
-
         def open_decoder(j):
             quant_h(j)
             for m in range(D_BANKS):
                 decode(j, m)
 
-        for i in range(1, 3):
-            j = i - 1
-            open_decoder(j)
-            if i > 1:
-                move(1)
-            leaky(i)
-            turn_h(i)
-            if i == 1:
-                quant_x(3)
-                copy_h(1)
-                move(1)
-                group_hc(0, "G")
-            bias_d(j, 0)
-            decode(j, 3)
-            if i == 1:
-                encode(2, 1)
-            else:
-                turn_x(6, 1)
-                encode(3, 1)
-                turn_x(7, 0)
-            bias_d(j, 1)
-            if i > 1:
-                copy_h(i)
-            exp(j, 0, 1)
-            bias_d(j, 2)
-            bias_d(j, 3)
-            exp(j, 1, 2)
-            if i == 1:
-                move(2)
-            bias_y(i + 1, 0)
-            if i == 1:
-                encode(3, 0)
-            bias_y(i + 1, 1)
-        copy_x(6, 1)
+        open_decoder(0)
+        leaky(1)
+        turn_h(1)
+        quant_x(3)
+        copy_h(1)
+        move_x(4, 1)
+        group_hc(0, "G")
+        bias_d(0, 0)
+        decode(0, 3)
+        encode(2, 1)
+        turn_x(5, 0)
+        turn_x(5, 1)
+        bias_d(0, 1)
+        exp(0, 0, 1)
+        bias_d(0, 2)
+        bias_d(0, 3)
+        exp(0, 1, 2)
+        copy_x(5, 0)
+        copy_x(5, 1)
+        bias_y(2, 0)
+        encode(3, 0)
+        bias_y(2, 1)
+        open_decoder(1)
+        quant_x(4)
+        turn_x(6, 0, into=y_banks[2, 1])
+        copy_x(6, 0)
+        move_x(6, 1)
+        leaky(2)
+        turn_h(2)
+        bias_d(1, 0)
+        decode(1, 3)
+        encode(3, 1)
+        turn_x(7, 0)
+        turn_x(7, 1)
+        bias_d(1, 1)
+        copy_h(2)
+        exp(1, 0, 1)
+        bias_d(1, 2)
+        bias_d(1, 3)
+        exp(1, 1, 2)
+        bias_y(3, 0)
+        encode(4, 0)
+        bias_y(3, 1)
         copy_x(7, 0)
+        copy_x(7, 1)
         open_decoder(2)
         leaky(3)
         turn_h(3)
         copy_h(3)
         bias_d(2, 0)
         decode(2, 3)
-        turn_x(7, 1)
+        encode(4, 1)
         turn_q(0)
+        turn_q(1)
         bias_d(2, 1)
         exp(2, 0, 1)
         bias_d(2, 2)
         bias_d(2, 3)
         exp(2, 1, 2)
-        copy_x(7, 1)
         copy_q(0)
+        copy_q(1)
         open_decoder(3)
-        quant_x(4)
-        encode(4, 0)
         quant_x(5)
-        group_hc(1, "G", into=x_grouped[5])
+        quant_x(6)
+        group_hc(1, "G", into=x_grouped[6])
         bias_d(3, 0)
         decode(3, 3)
-        encode(4, 1)
-        turn_q(1)
         turn_q(2)
+        turn_q(3)
         bias_d(3, 1)
         exp(3, 0, 1)
         bias_d(3, 2)
         bias_d(3, 3)
         exp(3, 1, 2)
-        copy_q(1)
         copy_q(2)
         log_group(0)
         bias_y(4, 0)
         encode(5, 0)
         bias_y(4, 1)
         encode(5, 1)
-        quant_x(6)
-        leaky(4)
+        leaky(4, 0, 1)
+        leaky(4, 1, 2)
         turn_h(4)
         bias_y(5, 0)
         encode(6, 0)
         bias_y(5, 1)
         copy_h(4, "V")
         quant_x(7)
-        turn_q(3)
         for i in range(5, PAIRS):
             j = i - 1
             open_decoder(j)

@@ -195,8 +195,10 @@ def tile_library_size_autoencoder_f6_kernel(
 
         y_banks, sums, h_rows, h_grouped, h_mx, h_banks = {}, {}, {}, {}, {}, {}
 
-        def encode(i, s):
-            y_banks[i, s] = psum.tile([P, H], F32, name="y_bank", bufs=Y_BANKS)
+        def encode(i, s, into=None):
+            if into is None:
+                into = psum.tile([P, H], F32, name="y_bank", bufs=Y_BANKS)
+            y_banks[i, s] = into
             for c in range(KP):
                 cols = slice((s * KP + c) * P, (s * KP + c + 1) * P)
                 mx_pass(y_banks[i, s][:], x_mx[i], cols, we_mx[c], slice(0, H), c == 0, c == KP - 1)
@@ -245,9 +247,11 @@ def tile_library_size_autoencoder_f6_kernel(
 
         d_banks, z, z_group = {}, {}, {}
 
-        def decode(i, m, spare=False):
+        def decode(i, m, spare=False, into=None):
             s, n = divmod(m, 2)
-            if spare:
+            if into is not None:
+                d_banks[i, m] = into
+            elif spare:
                 d_banks[i, m] = psum.tile([P, BANK], F32, name="turn_bank", bufs=TURN_BANKS)
             else:
                 d_banks[i, m] = psum.tile([P, BANK], F32, name="d_bank", bufs=D_BANKS)
@@ -270,7 +274,9 @@ def tile_library_size_autoencoder_f6_kernel(
             )
 
         def scale_d(i):
-            z[i] = work.tile([P, 2, G], F32, name="z", bufs=Z_BUFS)
+            if i % 2 == 0:
+                z_group[i // 2] = keep.tile([P, PACK, G], F32, name=f"z{i // 2}")
+            z[i] = z_group[i // 2][:, 2 * (i % 2) : 2 * (i % 2) + 2, :]
             slot = 2 * (i % 2)
             nc.scalar.activation(
                 out=z[i][:, 0, :BANK], in_=d_banks[i, 0][:], func=ACT.Copy, scale=invlib[:, i // 2, slot : slot + 1]
@@ -280,11 +286,11 @@ def tile_library_size_autoencoder_f6_kernel(
             nc.gpsimd.tensor_tensor(out=res, in0=z[i][:, 0, :BANK], in1=bdec_bc[:, :BANK], op=ALU.add)
 
         def exp_from(i, res):
-            nc.scalar.activation(out=z[i][:, 0, :BANK], in_=res, func=ACT.Exp)
             nc.scalar.activation(out=z[i][:, 0, BANK:], in_=z[i][:, 0, BANK:], func=ACT.Exp)
+            nc.scalar.activation(out=z[i][:, 0, :BANK], in_=res, func=ACT.Exp)
 
-        def exp(i, lo=0, hi=2):
-            part = z[i][:, lo:hi, :]
+        def exp(i, lo=0, hi=2, c0=0, c1=G):
+            part = z[i][:, lo:hi, c0:c1]
             nc.scalar.activation(out=part, in_=part, func=ACT.Exp)
 
         def exp_group(g):
@@ -457,35 +463,40 @@ def tile_library_size_autoencoder_f6_kernel(
             for m in range(D_BANKS):
                 decode(j, m)
 
-        open_decoder(0)
+        quant_h(0)
+        decode(0, 3, into=y_banks[1, 1])
+        for m in range(D_BANKS):
+            decode(0, m)
+        scale_d(0)
         leaky(1)
         turn_h(1)
         quant_x(3)
+        first_bank = x_grouped[3][:, 0].rearrange("p c n j -> p (c n j)").bitcast(F32)
+        add_bdec(0, first_bank)
         copy_h(1)
         move_x(4, 1)
-        group_hc(0, "G")
-        bias_d(0, 0)
-        decode(0, 3)
+        bias_d(0, 3)
         encode(2, 1)
         turn_x(5, 0)
         turn_x(5, 1)
         bias_d(0, 1)
-        exp(0, 0, 1)
+        exp(0, 0, 1, BANK, G)
         bias_d(0, 2)
-        bias_d(0, 3)
         exp(0, 1, 2)
+        nc.scalar.activation(out=z[0][:, 0, :BANK], in_=first_bank, func=ACT.Exp)
         copy_x(5, 0)
         copy_x(5, 1)
         bias_y(2, 0)
         encode(3, 0)
         bias_y(2, 1)
         open_decoder(1)
-        quant_x(4)
         turn_x(6, 0, into=y_banks[2, 1])
         copy_x(6, 0)
         move_x(6, 1)
         leaky(2)
         turn_h(2)
+        quant_x(4)
+        group_hc(0, "G", into=x_grouped[4])
         bias_d(1, 0)
         decode(1, 3)
         encode(3, 1)
@@ -524,8 +535,8 @@ def tile_library_size_autoencoder_f6_kernel(
         group_hc(1, "G", into=x_grouped[6])
         bias_d(3, 0)
         decode(3, 3)
+        encode(5, 0, psum.tile([P, H], F32, name="turn_bank", bufs=TURN_BANKS))
         turn_q(2)
-        turn_q(3)
         bias_d(3, 1)
         exp(3, 0, 1)
         bias_d(3, 2)
@@ -534,21 +545,28 @@ def tile_library_size_autoencoder_f6_kernel(
         copy_q(2)
         log_group(0)
         bias_y(4, 0)
-        encode(5, 0)
-        bias_y(4, 1)
         encode(5, 1)
+        bias_y(4, 1)
         leaky(4, 0, 1)
         leaky(4, 1, 2)
         turn_h(4)
         bias_y(5, 0)
-        encode(6, 0)
         bias_y(5, 1)
+        encode(6, 0, y_banks[5, 1])
         copy_h(4, "V")
         quant_x(7)
         for i in range(5, PAIRS):
             j = i - 1
-            open_decoder(j)
-            leaky(i)
+            if i < 7:
+                open_decoder(j)
+                leaky(i)
+            else:
+                quant_h(j)
+                decode(j, 0)
+                decode(j, 1)
+                leaky(i)
+                turn_h(i)
+                decode(j, 2)
             if i == 5:
                 group_hc(2, "G")
             if i == 6:
@@ -557,25 +575,28 @@ def tile_library_size_autoencoder_f6_kernel(
             if i == 7:
                 finish(1, 0, "G", res=sums[i][:])
             bias_d(j, 0)
-            if i == 7 or i == 5:
+            if i == 5:
                 turn_h(i)
             decode(j, 3)
             if i == 6:
                 turn_h(i)
-            if i + 1 < PAIRS:
+            if i == 5:
                 encode(i + 1, 1)
             if i == 5:
+                turn_q(3)
                 copy_h(i, "S")
                 log_group(1)
             bias_d(j, 1)
             if i == 7:
                 copy_h(i, "V")
             bias_d(j, 2)
+            if i == 6:
+                encode(7, 1, d_banks[j, 2])
             if i == 7:
                 quant_h(i)
                 paced = work.tile([P, G], F32, name="h_grouped", align_bytes=256, bufs=1)
                 finish(1, 1, "G", res=paced[:])
-                finish(2, 0, "G")
+                finish(2, 0, "G", 0, 640)
                 decode(i, 0)
                 decode(i, 1)
             bias_d(j, 3)
@@ -600,6 +621,7 @@ def tile_library_size_autoencoder_f6_kernel(
         LEFT = [(2, 1), (3, 0), (3, 1)]
         exp(7, 0, 1)
         exp(7, 1, 2)
+        finish(2, 0, "V", 640, G)
         for k, s in LEFT:
             finish(k, s)
         quant_q()

@@ -45,7 +45,7 @@ def tile_library_size_autoencoder_f6_kernel(
         lib_view = lib.rearrange("(g p s) -> p g s", p=P, s=PACK)
         mean_view = out_mean.rearrange("(g p s) n -> g p s n", p=P, s=PACK)
         x_sb = [work.tile([P, 2, G], BF16, name="x_pair", align_bytes=256, bufs=PAIRS + 1) for i in range(PAIRS)]
-        w_raw = [keep.tile([P, PACK, H], BF16, name=f"w_raw{c}") for c in range(KP)]
+        w_raw = [keep.tile([P, PACK, H], BF16, name=f"w_raw{c}", align_bytes=256) for c in range(KP)]
         wd_bytes = keep.tile([P, PACK, G], U8, name="wd_bytes")
         q_sb = keep.tile([P, 2, C], BF16, name="q_sb")
         lib_first = keep.tile([P, PACK], BF16, name="lib_first")
@@ -204,7 +204,9 @@ def tile_library_size_autoencoder_f6_kernel(
                 mx_pass(y_banks[i, s][:], x_mx[i], cols, we_mx[c], slice(0, H), c == 0, c == KP - 1)
 
         def bias_y(i, s):
-            if s == 0:
+            if s == 0 and i == 2:
+                sums[i] = keep.tile([P, 2 * H], F32, name="w_raw0", align_bytes=256)
+            elif s == 0:
                 sums[i] = work.tile([P, 2 * H], F32, name="sums", bufs=SUM_BUFS)
             slot = 2 * (i % 2) + s
             nc.vector.scalar_tensor_tensor(
@@ -229,6 +231,9 @@ def tile_library_size_autoencoder_f6_kernel(
                 op1=ALU.max,
             )
 
+        wide_h = {}
+        WIDE_H = {4: "we_grouped0", 5: "we_grouped1", 6: "wd_grouped0", 7: "h_last"}
+
         def turn_h(i):
             bank = psum.tile([P, 2, 2, P], F32, name="h_bank", bufs=1)
             words = h_rows[i // 2][:, (i % 2) * 2 * H : (i % 2 + 1) * 2 * H].bitcast(F32)
@@ -238,12 +243,16 @@ def tile_library_size_autoencoder_f6_kernel(
             h_banks[i] = bank
 
         def copy_h(i, engine="S"):
-            h_grouped[i] = work.tile([P, 2, P, PACK], BF16, name="h_grouped", align_bytes=256, bufs=1)
-            copy(engine, h_grouped[i][:].bitcast(F32), h_banks[i][:].rearrange("p s u n -> p s n u"))
+            if i in WIDE_H:
+                wide_h[i] = keep.tile([P, 2 * G], BF16, name=WIDE_H[i], align_bytes=256)
+                h_grouped[i] = wide_h[i][:, : 2 * H].rearrange("p (s n t) -> p s n t", s=2, t=PACK)
+            else:
+                h_grouped[i] = work.tile([P, 2, P, PACK], BF16, name="h_grouped", align_bytes=256, bufs=1)[:]
+            copy(engine, h_grouped[i].bitcast(F32), h_banks[i][:].rearrange("p s u n -> p s n u"))
 
         def quant_h(i):
             h_mx[i] = mx_tiles(work, "h", 2 * P, bufs=3)
-            quantize(h_mx[i][0][:], h_mx[i][1][:], h_grouped[i][:].rearrange("p s n t -> p (s n t)"))
+            quantize(h_mx[i][0][:], h_mx[i][1][:], h_grouped[i].rearrange("p s n t -> p (s n t)"))
 
         d_banks, z, z_group = {}, {}, {}
 
@@ -303,7 +312,7 @@ def tile_library_size_autoencoder_f6_kernel(
             part = z[i][:, lo:hi, c0:c1]
             nc.scalar.activation(out=part, in_=part, func=ACT.Ln, bias=1.0)
 
-        def finish(i, s, engine="V", lo=0, hi=G, res=None):
+        def finish(i, s, engine="V", lo=0, hi=G, res=None, store=True):
             slot = 2 * (i % 2) + s
             part = z[i][:, s, lo:hi]
             if res is None:
@@ -313,13 +322,18 @@ def tile_library_size_autoencoder_f6_kernel(
                 nc.vector.tensor_scalar(out=res, in0=part, scalar1=factor, scalar2=None, op0=ALU.mult)
             else:
                 nc.gpsimd.tensor_scalar(out=res, in0=part, scalar1=factor, scalar2=0.0, op0=ALU.mult, op1=ALU.add)
-            nc.sync.dma_start(out=mean_view[i // 2][:, slot, lo:hi], in_=res)
+            if store:
+                nc.sync.dma_start(out=mean_view[i // 2][:, slot, lo:hi], in_=res)
+
+        def store_pair(i):
+            first = 2 * (i % 2)
+            nc.sync.dma_start(out=mean_view[i // 2][:, first : first + 2, :], in_=z[i])
 
         hc_grouped, hc_mx = {}, {}
 
         def group_hc(g, engine, lo=0, hi=H, into=None):
             if into is not None:
-                hc_grouped[g] = into[:].rearrange("p s c n j -> p (s c n) j")
+                hc_grouped[g] = into.rearrange("p (c j) -> p c j", j=PACK)
             elif lo == 0:
                 hc_grouped[g] = keep.tile([P, H, PACK], BF16, name=("we_grouped", "wd_grouped")[g // 2] + str(g % 2), align_bytes=256)
             interleave(engine, hc_grouped[g], h_rows[g][:].rearrange("p (s j) -> p s j", s=PACK), lo, hi)
@@ -464,9 +478,10 @@ def tile_library_size_autoencoder_f6_kernel(
                 decode(j, m)
 
         quant_h(0)
+        decode(0, 0)
         decode(0, 3, into=y_banks[1, 1])
-        for m in range(D_BANKS):
-            decode(0, m)
+        decode(0, 1)
+        decode(0, 2)
         scale_d(0)
         leaky(1)
         turn_h(1)
@@ -496,7 +511,7 @@ def tile_library_size_autoencoder_f6_kernel(
         leaky(2)
         turn_h(2)
         quant_x(4)
-        group_hc(0, "G", into=x_grouped[4])
+        group_hc(0, "G", into=x_grouped[4][:].rearrange("p s c n j -> p (s c n j)"))
         bias_d(1, 0)
         decode(1, 3)
         encode(3, 1)
@@ -532,7 +547,7 @@ def tile_library_size_autoencoder_f6_kernel(
         open_decoder(3)
         quant_x(5)
         quant_x(6)
-        group_hc(1, "G", into=x_grouped[6])
+        group_hc(1, "G", into=x_grouped[6][:].rearrange("p s c n j -> p (s c n j)"))
         bias_d(3, 0)
         decode(3, 3)
         encode(5, 0, psum.tile([P, H], F32, name="turn_bank", bufs=TURN_BANKS))
@@ -568,10 +583,10 @@ def tile_library_size_autoencoder_f6_kernel(
                 turn_h(i)
                 decode(j, 2)
             if i == 5:
-                group_hc(2, "G")
+                group_hc(2, "G", into=wide_h[4][:])
             if i == 6:
                 finish(0, 0, "G", res=sums[i][:])
-                finish(0, 1, "G")
+                finish(0, 1, "G", 0, 704)
             if i == 7:
                 finish(1, 0, "G", res=sums[i][:])
             bias_d(j, 0)
@@ -594,9 +609,8 @@ def tile_library_size_autoencoder_f6_kernel(
                 encode(7, 1, d_banks[j, 2])
             if i == 7:
                 quant_h(i)
-                paced = work.tile([P, G], F32, name="h_grouped", align_bytes=256, bufs=1)
-                finish(1, 1, "G", res=paced[:])
-                finish(2, 0, "G", 0, 640)
+                finish(1, 1, "G", res=wide_h[7][:].bitcast(F32))
+
                 decode(i, 0)
                 decode(i, 1)
             bias_d(j, 3)
@@ -618,10 +632,10 @@ def tile_library_size_autoencoder_f6_kernel(
         decode(7, 3)
         for m in range(1, 4):
             bias_d(7, m)
-        LEFT = [(2, 1), (3, 0), (3, 1)]
+        LEFT = [(2, 0), (2, 1), (3, 0), (3, 1)]
         exp(7, 0, 1)
         exp(7, 1, 2)
-        finish(2, 0, "V", 640, G)
+        finish(0, 1, "V", 704, G)
         for k, s in LEFT:
             finish(k, s)
         quant_q()

@@ -557,13 +557,12 @@ def tile_library_size_autoencoder_f6_kernel(
         bias_d(3, 2)
         bias_d(3, 3)
         exp(3, 1, 2)
-        copy_q(2)
         log_group(0)
         bias_y(4, 0)
         encode(5, 1)
         bias_y(4, 1)
-        leaky(4, 0, 1)
-        leaky(4, 1, 2)
+        copy_q(2, "V")
+        leaky(4)
         turn_h(4)
         bias_y(5, 0)
         bias_y(5, 1)
@@ -586,7 +585,7 @@ def tile_library_size_autoencoder_f6_kernel(
                 group_hc(2, "G", into=wide_h[4][:])
             if i == 6:
                 finish(0, 0, "G", res=sums[i][:])
-                finish(0, 1, "G", 0, 704)
+                finish(0, 1, "G")
             if i == 7:
                 finish(1, 0, "G", res=sums[i][:])
             bias_d(j, 0)
@@ -610,7 +609,7 @@ def tile_library_size_autoencoder_f6_kernel(
             if i == 7:
                 quant_h(i)
                 finish(1, 1, "G", res=wide_h[7][:].bitcast(F32))
-
+                finish(2, 0, "G", 0, 640)
                 decode(i, 0)
                 decode(i, 1)
             bias_d(j, 3)
@@ -632,10 +631,10 @@ def tile_library_size_autoencoder_f6_kernel(
         decode(7, 3)
         for m in range(1, 4):
             bias_d(7, m)
-        LEFT = [(2, 0), (2, 1), (3, 0), (3, 1)]
+        LEFT = [(2, 1), (3, 0), (3, 1)]
         exp(7, 0, 1)
         exp(7, 1, 2)
-        finish(0, 1, "V", 704, G)
+        finish(2, 0, "V", 640, G)
         for k, s in LEFT:
             finish(k, s)
         quant_q()

@@ -19,20 +19,22 @@ ACT = mybir.ActivationFunctionType
 P = 128
 PACK = 4
 PASS = P * PACK
+BANK = 512
 GROUPS = C // PASS
 PAIRS = 2 * GROUPS
-TILES = 2 * PAIRS
 KP = G // PASS
-BANK = 512
 TURN_BANKS, Y_BANKS, D_BANKS = 2, 2, 3
-SUM_BUFS = 3
-Z_BUFS = 8
+X_BUFS = PAIRS + 1
+CODE_BUFS = 3
+BATCH = PAIRS // 2
+GPSIMD_COLS = 640
 
 
 def tile_library_size_autoencoder_f6_kernel(
     tc, x, lib, w_enc, b_enc, w_dec_bytes, w_dec_scale, b_dec, depth, q, unit, out_mean, out_contrast
 ):
     nc = tc.nc
+    scalar, vector, gpsimd = nc.scalar, nc.vector, nc.gpsimd
     with ExitStack() as ctx:
         keep = ctx.enter_context(tc.tile_pool(name="keep", bufs=1))
         work = ctx.enter_context(tc.tile_pool(name="work", bufs=2))
@@ -40,57 +42,61 @@ def tile_library_size_autoencoder_f6_kernel(
         ctx.enter_context(tc.manual_schedule())
 
         x_view = x.rearrange("(g p s) k -> g p s k", p=P, s=PACK)
-        w_view = w_enc.rearrange("(c p j) n -> c p j n", p=P, j=PACK)
+        w_view = w_enc.rearrange("(c p t) n -> c p t n", p=P, t=PACK)
         wd_view = w_dec_bytes.rearrange("(p t) g -> p t g", t=PACK)
         lib_view = lib.rearrange("(g p s) -> p g s", p=P, s=PACK)
         mean_view = out_mean.rearrange("(g p s) n -> g p s n", p=P, s=PACK)
-        x_sb = [work.tile([P, 2, G], BF16, name="x_pair", align_bytes=256, bufs=PAIRS + 1) for i in range(PAIRS)]
-        w_raw = [keep.tile([P, PACK, H], BF16, name=f"w_raw{c}", align_bytes=256) for c in range(KP)]
+
+        x_sb = [work.tile([P, 2, G], BF16, name="x_pair", align_bytes=256, bufs=X_BUFS) for i in range(PAIRS)]
+        w_raw = [keep.tile([P, PACK, H], BF16, name=f"w_raw{c}") for c in range(KP)]
         wd_bytes = keep.tile([P, PACK, G], U8, name="wd_bytes")
         q_sb = keep.tile([P, 2, C], BF16, name="q_sb")
         lib_first = keep.tile([P, PACK], BF16, name="lib_first")
         lib_rest = keep.tile([P, GROUPS - 1, PACK], BF16, name="lib_rest")
         depth_sb = keep.tile([P, GROUPS, PACK], BF16, name="depth_sb")
         wsc_sb = keep.tile([P, PACK], F32, name="wsc_sb")
+        benc_sb = keep.tile([P, PACK], BF16, name="benc_sb")
+        bdec_sb = keep.tile([P, 2 * PACK], BF16, name="bdec_sb")
         benc_bc = keep.tile([P, H], BF16, name="benc_bc")
         bdec_bc = keep.tile([P, G], BF16, name="bdec_bc")
         unit_bc = keep.tile([P, H], BF16, name="unit_bc")
-        benc_sb = keep.tile([P, PACK], BF16, name="benc_sb")
-        bdec_sb = keep.tile([P, 2 * PACK], BF16, name="bdec_sb")
         ident = keep.tile([P, P], F32, name="ident")
         ident16 = keep.tile([P, P], BF16, name="ident16")
         invlib = keep.tile([P, GROUPS, PACK], F32, name="invlib")
 
+        def slot_of(i, s):
+            return 2 * (i % 2) + s
+
         def load_x(i, lo=0, hi=2):
-            first = 2 * (i % 2)
-            nc.sync.dma_start(out=x_sb[i][:, lo:hi], in_=x_view[i // 2][:, first + lo : first + hi, :])
+            nc.sync.dma_start(out=x_sb[i][:, lo:hi], in_=x_view[i // 2][:, slot_of(i, lo) : slot_of(i, hi), :])
 
-        def load_w(c):
-            nc.sync.dma_start(out=w_raw[c][:], in_=w_view[c])
+        def turn_bank(shape):
+            return psum.tile(shape, F32, name="turn_bank", bufs=TURN_BANKS)
 
-        def load_wd(lo, hi):
-            nc.sync.dma_start(out=wd_bytes[:, lo:hi], in_=wd_view[:, lo:hi])
+        def h_bank(shape):
+            return psum.tile(shape, F32, name="h_bank", bufs=1)
+
+        def y_bank():
+            return psum.tile([P, BANK], F32, name="y_bank", bufs=Y_BANKS)
+
+        def d_bank(shape):
+            return psum.tile(shape, F32, name="d_bank", bufs=D_BANKS)
 
         def copy(engine, out, in_):
-            if engine == "S":
-                nc.scalar.copy(out=out, in_=in_)
-            elif engine == "V":
-                nc.vector.tensor_copy(out=out, in_=in_)
+            if engine is scalar:
+                scalar.copy(out=out, in_=in_)
             else:
-                nc.gpsimd.tensor_scalar(out=out, in0=in_, scalar1=1.0, scalar2=0.0, op0=ALU.mult, op1=ALU.add)
+                vector.tensor_copy(out=out, in_=in_)
 
         def interleave(engine, grouped, rows, lo, hi):
-            if engine == "G":
-                copy(engine, grouped[:, lo:hi, :], rows[:, :, lo:hi].rearrange("p t c -> p c t"))
-                return
             copy(
                 engine,
                 grouped[:, lo:hi, :].rearrange("p (c i) t -> p c t i", i=PACK),
                 rows[:, :, lo:hi].rearrange("p t (c i) -> p c t i", i=PACK),
             )
 
-        def quantize(codes, scales, grouped):
-            nc.vector.quantize_mx(out=codes.bitcast(FP8X4), scales=scales, in_=grouped)
+        def quantize(mx, cols, grouped):
+            vector.quantize_mx(out=mx[0][:, cols].bitcast(FP8X4), scales=mx[1][:, cols], in_=grouped)
 
         def mx_tiles(pool, name, width, bufs=None):
             return (
@@ -98,283 +104,221 @@ def tile_library_size_autoencoder_f6_kernel(
                 pool.tile([P, width], U8, name=f"{name}_scales", align_bytes=256, bufs=bufs),
             )
 
-        def mx_pass(bank, lhs, lhs_cols, rhs, rhs_cols, start, stop):
+        def mx_pass(bank, lhs, lhs_cols, rhs, start, stop):
             nc.tensor.matmul_mx(
-                out=bank,
+                out=bank[:],
                 lhsT=lhs[0][:, lhs_cols].bitcast(FP8X4),
                 lhsT_scale=lhs[1][:, lhs_cols],
-                rhs=rhs[0][:, rhs_cols].bitcast(FP8X4),
-                rhs_scale=rhs[1][:, rhs_cols],
+                rhs=rhs[0][:].bitcast(FP8X4),
+                rhs_scale=rhs[1][:],
                 start=start,
                 stop=stop,
             )
 
-        spread_banks = {}
-
-        def spread(key, columns, first):
-            spread_banks[key] = psum.tile([P, PACK, P], F32, name="d_bank", bufs=D_BANKS)
+        def spread(columns):
+            bank = d_bank([P, PACK, P])
             for m in range(PACK):
                 nc.tensor.matmul(
-                    out=spread_banks[key][:, m, :],
-                    lhsT=columns[:, first + m : first + m + 1].to_broadcast([P, P]),
+                    out=bank[:, m, :],
+                    lhsT=columns[:, m : m + 1].to_broadcast([P, P]),
                     rhs=ident16[:],
                     start=True,
                     stop=True,
                 )
+            return bank
 
-        def copy_benc(engine):
-            out = benc_bc[:].rearrange("p (u n e) -> p u n e", u=2, e=2)
-            copy(engine, out, spread_banks["enc"][:].rearrange("p (u e) n -> p u n e", u=2))
-
-        def copy_bdec(half, engine):
-            out = bdec_bc[:, half * BANK : (half + 1) * BANK].rearrange("p (n m) -> p n m", m=PACK)
-            copy(engine, out, spread_banks[half][:].rearrange("p m n -> p n m"))
+        def copy_bdec(n, bank):
+            out = bdec_bc[:, n * BANK : (n + 1) * BANK].rearrange("p (n m) -> p n m", m=PACK)
+            copy(scalar, out, bank[:].rearrange("p m n -> p n m"))
 
         we_grouped = [keep.tile([P, H, PACK], BF16, name=f"we_grouped{c}", align_bytes=256) for c in range(KP)]
         we_mx = [mx_tiles(keep, f"we{c}", H) for c in range(KP)]
-
-        def group_we(c, engine, lo=0, hi=P):
-            copy(
-                engine,
-                we_grouped[c][:].rearrange("p (u m e) j -> p m u j e", u=2, e=2)[:, lo:hi],
-                w_raw[c][:].rearrange("p j (m u e) -> p m u j e", u=2, e=2)[:, lo:hi],
-            )
-
-        def quant_we(c):
-            quantize(we_mx[c][0][:], we_mx[c][1][:], we_grouped[c][:].rearrange("p c j -> p (c j)"))
-
         wd_wide = [keep.tile([P, PACK, BANK], BF16, name=f"wd_wide{n}") for n in range(2)]
         wd_grouped = [keep.tile([P, BANK, PACK], BF16, name=f"wd_grouped{n}", align_bytes=256) for n in range(2)]
         wd_mx = [mx_tiles(keep, f"wd{n}", BANK) for n in range(2)]
 
-        def widen_wd(n, engine, lo=0, hi=PACK):
-            for t in range(lo, hi):
-                src = wd_bytes[:, t, n * BANK : (n + 1) * BANK].bitcast(E4M3)
-                if engine == "S":
-                    nc.scalar.activation(out=wd_wide[n][:, t, :], in_=src, func=ACT.Copy, scale=wsc_sb[:, t : t + 1])
-                else:
-                    nc.vector.tensor_scalar(
-                        out=wd_wide[n][:, t, :], in0=src, scalar1=wsc_sb[:, t : t + 1], scalar2=None, op0=ALU.mult
-                    )
+        def group_we(c):
+            copy(
+                vector,
+                we_grouped[c][:].rearrange("p (u m e) t -> p m u t e", u=2, e=2),
+                w_raw[c][:].rearrange("p t (m u e) -> p m u t e", u=2, e=2),
+            )
 
-        def group_wd(n, engine, lo=0, hi=BANK):
-            interleave(engine, wd_grouped[n], wd_wide[n], lo, hi)
+        def quant_we(c):
+            quantize(we_mx[c], slice(0, H), we_grouped[c][:].rearrange("p c t -> p (c t)"))
+
+        def widen_wd(engine, n, rows):
+            for t in rows:
+                src = wd_bytes[:, t, n * BANK : (n + 1) * BANK].bitcast(E4M3)
+                factor = wsc_sb[:, t : t + 1]
+                if engine is scalar:
+                    scalar.activation(out=wd_wide[n][:, t, :], in_=src, func=ACT.Copy, scale=factor)
+                else:
+                    vector.tensor_scalar(out=wd_wide[n][:, t, :], in0=src, scalar1=factor, scalar2=None, op0=ALU.mult)
 
         def quant_wd(n):
-            quantize(wd_mx[n][0][:], wd_mx[n][1][:], wd_grouped[n][:].rearrange("p g t -> p (g t)"))
+            quantize(wd_mx[n], slice(0, BANK), wd_grouped[n][:].rearrange("p g t -> p (g t)"))
 
+        x_shape = [P, KP, 2, P]
         x_grouped, x_mx, x_banks = {}, {}, {}
 
-        def turn_x(i, s, name="turn_bank", bufs=TURN_BANKS, into=None):
-            if into is None:
-                bank = psum.tile([P, KP, 2, P], F32, name=name, bufs=bufs)
-            else:
-                bank = into[:].rearrange("p (c u n) -> p c u n", c=KP, u=2)
+        def turn_x(i, s, bank=None):
+            x_banks[i, s] = turn_bank(x_shape)[:] if bank is None else bank
             words = x_sb[i][:, s, :].bitcast(F32)
             for c in range(KP):
                 for u in range(2):
-                    nc.tensor.transpose(bank[:, c, u, :], words[:, 256 * c + u : 256 * (c + 1) : 2], ident[:])
-            x_banks[i, s] = bank
+                    nc.tensor.transpose(x_banks[i, s][:, c, u, :], words[:, 256 * c + u : 256 * (c + 1) : 2], ident[:])
 
-        def copy_x(i, s, engine="S"):
+        def copy_x(i, s):
             if s == 0:
-                x_grouped[i] = work.tile([P, 2, KP, P, PACK], BF16, name="x_pair", align_bytes=256, bufs=PAIRS + 1)
-            copy(engine, x_grouped[i][:, s].bitcast(F32), x_banks[i, s][:].rearrange("p c u n -> p c n u"))
+                x_grouped[i] = work.tile([P, 2, KP, P, PACK], BF16, name="x_pair", align_bytes=256, bufs=X_BUFS)
+            copy(scalar, x_grouped[i][:, s].bitcast(F32), x_banks[i, s].rearrange("p c u n -> p c n u"))
 
-        def move_x(i, s, engine="S"):
-            turn_x(i, s)
-            copy_x(i, s, engine)
+        def move_x(i, s, bank=None):
+            turn_x(i, s, bank)
+            copy_x(i, s)
 
         def quant_x(i, lo=0, hi=2):
             if lo == 0:
-                x_mx[i] = mx_tiles(work, "x", 2 * KP * P, bufs=3)
-            cols = slice(lo * KP * P, hi * KP * P)
-            quantize(
-                x_mx[i][0][:, cols], x_mx[i][1][:, cols], x_grouped[i][:, lo:hi].rearrange("p s c n j -> p (s c n j)")
-            )
+                x_mx[i] = mx_tiles(work, "x", 2 * KP * P, bufs=CODE_BUFS)
+            grouped = x_grouped[i][:, lo:hi].rearrange("p s c n t -> p (s c n t)")
+            quantize(x_mx[i], slice(lo * KP * P, hi * KP * P), grouped)
 
-        y_banks, sums, h_rows, h_grouped, h_mx, h_banks = {}, {}, {}, {}, {}, {}
+        y_banks, sums, h_rows, h_banks, h_grouped, h_mx = {}, {}, {}, {}, {}, {}
 
-        def encode(i, s, into=None):
-            if into is None:
-                into = psum.tile([P, H], F32, name="y_bank", bufs=Y_BANKS)
-            y_banks[i, s] = into
+        def encode(i, s, bank=None):
+            y_banks[i, s] = y_bank() if bank is None else bank
             for c in range(KP):
                 cols = slice((s * KP + c) * P, (s * KP + c + 1) * P)
-                mx_pass(y_banks[i, s][:], x_mx[i], cols, we_mx[c], slice(0, H), c == 0, c == KP - 1)
+                mx_pass(y_banks[i, s], x_mx[i], cols, we_mx[c], c == 0, c == KP - 1)
 
         def bias_y(i, s):
-            if s == 0 and i == 2:
-                sums[i] = keep.tile([P, 2 * H], F32, name="w_raw0", align_bytes=256)
-            elif s == 0:
-                sums[i] = work.tile([P, 2 * H], F32, name="sums", bufs=SUM_BUFS)
-            slot = 2 * (i % 2) + s
-            nc.vector.scalar_tensor_tensor(
+            if s == 0:
+                sums[i] = work.tile([P, 2 * H], F32, name="sums", bufs=CODE_BUFS)
+            slot = slice(slot_of(i, s), slot_of(i, s) + 1)
+            vector.scalar_tensor_tensor(
                 out=sums[i][:, s * H : (s + 1) * H],
                 in0=benc_bc[:],
-                scalar=lib_first[:, slot : slot + 1] if i < 2 else lib_rest[:, i // 2 - 1, slot : slot + 1],
+                scalar=lib_first[:, slot] if i < 2 else lib_rest[:, i // 2 - 1, slot],
                 in1=y_banks[i, s][:],
                 op0=ALU.mult,
                 op1=ALU.add,
             )
 
-        def leaky(i, lo=0, hi=2):
-            if i % 2 == 0 and lo == 0:
+        def pair_rows(i):
+            return h_rows[i // 2][:, slot_of(i, 0) * H : slot_of(i, 2) * H]
+
+        def leaky(i):
+            if i % 2 == 0:
                 h_rows[i // 2] = keep.tile([P, PACK * H], BF16, name=f"h_rows{i // 2}")
-            first = 2 * (i % 2)
-            nc.vector.scalar_tensor_tensor(
-                out=h_rows[i // 2][:, (first + lo) * H : (first + hi) * H],
-                in0=sums[i][:, lo * H : hi * H],
-                scalar=SLOPE,
-                in1=sums[i][:, lo * H : hi * H],
-                op0=ALU.mult,
-                op1=ALU.max,
+            vector.scalar_tensor_tensor(
+                out=pair_rows(i), in0=sums[i][:], scalar=SLOPE, in1=sums[i][:], op0=ALU.mult, op1=ALU.max
             )
 
-        wide_h = {}
-        WIDE_H = {4: "we_grouped0", 5: "we_grouped1", 6: "wd_grouped0", 7: "h_last"}
-
         def turn_h(i):
-            bank = psum.tile([P, 2, 2, P], F32, name="h_bank", bufs=1)
-            words = h_rows[i // 2][:, (i % 2) * 2 * H : (i % 2 + 1) * 2 * H].bitcast(F32)
+            h_banks[i] = h_bank([P, 2, 2, P])
+            words = pair_rows(i).bitcast(F32)
             for s in range(2):
                 for u in range(2):
-                    nc.tensor.transpose(bank[:, s, u, :], words[:, (2 * s + u) * P : (2 * s + u + 1) * P], ident[:])
-            h_banks[i] = bank
+                    part = words[:, (2 * s + u) * P : (2 * s + u + 1) * P]
+                    nc.tensor.transpose(h_banks[i][:, s, u, :], part, ident[:])
 
-        def copy_h(i, engine="S"):
-            if i in WIDE_H:
-                wide_h[i] = keep.tile([P, 2 * G], BF16, name=WIDE_H[i], align_bytes=256)
-                h_grouped[i] = wide_h[i][:, : 2 * H].rearrange("p (s n t) -> p s n t", s=2, t=PACK)
-            else:
-                h_grouped[i] = work.tile([P, 2, P, PACK], BF16, name="h_grouped", align_bytes=256, bufs=1)[:]
-            copy(engine, h_grouped[i].bitcast(F32), h_banks[i][:].rearrange("p s u n -> p s n u"))
+        def copy_h(engine, i, room=None):
+            if room is None:
+                room = work.tile([P, 2 * H], BF16, name="h_grouped", align_bytes=256, bufs=1)
+            h_grouped[i] = room[:, : 2 * H]
+            words = h_grouped[i].bitcast(F32).rearrange("p (s n u) -> p s n u", s=2, u=2)
+            copy(engine, words, h_banks[i][:].rearrange("p s u n -> p s n u"))
 
         def quant_h(i):
-            h_mx[i] = mx_tiles(work, "h", 2 * P, bufs=3)
-            quantize(h_mx[i][0][:], h_mx[i][1][:], h_grouped[i].rearrange("p s n t -> p (s n t)"))
+            h_mx[i] = mx_tiles(work, "h", 2 * P, bufs=CODE_BUFS)
+            quantize(h_mx[i], slice(0, 2 * P), h_grouped[i])
 
-        d_banks, z, z_group = {}, {}, {}
+        d_banks = {}
+        z = [keep.tile([P, PACK, G], F32, name=f"z{g}") for g in range(GROUPS)]
 
-        def decode(i, m, spare=False, into=None):
+        def z_tile(i, s, lo=0, hi=G):
+            return z[i // 2][:, slot_of(i, s), lo:hi]
+
+        def inv_of(i, s):
+            return invlib[:, i // 2, slot_of(i, s) : slot_of(i, s) + 1]
+
+        def decode(i, m, bank=None):
             s, n = divmod(m, 2)
-            if into is not None:
-                d_banks[i, m] = into
-            elif spare:
-                d_banks[i, m] = psum.tile([P, BANK], F32, name="turn_bank", bufs=TURN_BANKS)
-            else:
-                d_banks[i, m] = psum.tile([P, BANK], F32, name="d_bank", bufs=D_BANKS)
-            mx_pass(d_banks[i, m][:], h_mx[i], slice(s * P, (s + 1) * P), wd_mx[n], slice(0, BANK), True, True)
+            d_banks[i, m] = d_bank([P, BANK]) if bank is None else bank
+            mx_pass(d_banks[i, m], h_mx[i], slice(s * P, (s + 1) * P), wd_mx[n], True, True)
+
+        def open_decoder(i):
+            quant_h(i)
+            for m in range(D_BANKS):
+                decode(i, m)
 
         def bias_d(i, m):
             s, n = divmod(m, 2)
-            slot = 2 * (i % 2) + s
-            if i not in z:
-                if i % 2 == 0:
-                    z_group[i // 2] = keep.tile([P, PACK, G], F32, name=f"z{i // 2}")
-                z[i] = z_group[i // 2][:, 2 * (i % 2) : 2 * (i % 2) + 2, :]
-            nc.vector.scalar_tensor_tensor(
-                out=z[i][:, s, n * BANK : (n + 1) * BANK],
+            vector.scalar_tensor_tensor(
+                out=z_tile(i, s, n * BANK, (n + 1) * BANK),
                 in0=d_banks[i, m][:],
-                scalar=invlib[:, i // 2, slot : slot + 1],
+                scalar=inv_of(i, s),
                 in1=bdec_bc[:, n * BANK : (n + 1) * BANK],
                 op0=ALU.mult,
                 op1=ALU.add,
             )
 
-        def scale_d(i):
-            if i % 2 == 0:
-                z_group[i // 2] = keep.tile([P, PACK, G], F32, name=f"z{i // 2}")
-            z[i] = z_group[i // 2][:, 2 * (i % 2) : 2 * (i % 2) + 2, :]
-            slot = 2 * (i % 2)
-            nc.scalar.activation(
-                out=z[i][:, 0, :BANK], in_=d_banks[i, 0][:], func=ACT.Copy, scale=invlib[:, i // 2, slot : slot + 1]
-            )
+        def exp(part):
+            scalar.activation(out=part, in_=part, func=ACT.Exp)
 
-        def add_bdec(i, res):
-            nc.gpsimd.tensor_tensor(out=res, in0=z[i][:, 0, :BANK], in1=bdec_bc[:, :BANK], op=ALU.add)
+        def log1p(part):
+            scalar.activation(out=part, in_=part, func=ACT.Ln, bias=1.0)
 
-        def exp_from(i, res):
-            nc.scalar.activation(out=z[i][:, 0, BANK:], in_=z[i][:, 0, BANK:], func=ACT.Exp)
-            nc.scalar.activation(out=z[i][:, 0, :BANK], in_=res, func=ACT.Exp)
-
-        def exp(i, lo=0, hi=2, c0=0, c1=G):
-            part = z[i][:, lo:hi, c0:c1]
-            nc.scalar.activation(out=part, in_=part, func=ACT.Exp)
-
-        def exp_group(g):
-            nc.scalar.activation(out=z_group[g][:], in_=z_group[g][:], func=ACT.Exp)
-
-        def log_group(g):
-            nc.scalar.activation(out=z_group[g][:], in_=z_group[g][:], func=ACT.Ln, bias=1.0)
-
-        def log(i, lo=0, hi=2, c0=0, c1=G):
-            part = z[i][:, lo:hi, c0:c1]
-            nc.scalar.activation(out=part, in_=part, func=ACT.Ln, bias=1.0)
-
-        def finish(i, s, engine="V", lo=0, hi=G, res=None, store=True):
-            slot = 2 * (i % 2) + s
-            part = z[i][:, s, lo:hi]
-            if res is None:
-                res = part
-            factor = depth_sb[:, i // 2, slot : slot + 1]
-            if engine == "V":
-                nc.vector.tensor_scalar(out=res, in0=part, scalar1=factor, scalar2=None, op0=ALU.mult)
+        def finish(engine, i, s, lo=0, hi=G, res=None):
+            part = z_tile(i, s, lo, hi)
+            res = part if res is None else res
+            factor = depth_sb[:, i // 2, slot_of(i, s) : slot_of(i, s) + 1]
+            if engine is vector:
+                vector.tensor_scalar(out=res, in0=part, scalar1=factor, scalar2=None, op0=ALU.mult)
             else:
-                nc.gpsimd.tensor_scalar(out=res, in0=part, scalar1=factor, scalar2=0.0, op0=ALU.mult, op1=ALU.add)
-            if store:
-                nc.sync.dma_start(out=mean_view[i // 2][:, slot, lo:hi], in_=res)
+                gpsimd.tensor_scalar(out=res, in0=part, scalar1=factor, scalar2=0.0, op0=ALU.mult, op1=ALU.add)
+            nc.sync.dma_start(out=mean_view[i // 2][:, slot_of(i, s), lo:hi], in_=res)
 
-        def store_pair(i):
-            first = 2 * (i % 2)
-            nc.sync.dma_start(out=mean_view[i // 2][:, first : first + 2, :], in_=z[i])
-
-        hc_grouped, hc_mx = {}, {}
-
-        def group_hc(g, engine, lo=0, hi=H, into=None):
-            if into is not None:
-                hc_grouped[g] = into.rearrange("p (c j) -> p c j", j=PACK)
-            elif lo == 0:
-                hc_grouped[g] = keep.tile([P, H, PACK], BF16, name=("we_grouped", "wd_grouped")[g // 2] + str(g % 2), align_bytes=256)
-            interleave(engine, hc_grouped[g], h_rows[g][:].rearrange("p (s j) -> p s j", s=PACK), lo, hi)
-
-        def quant_hc(g):
-            hc_mx[g] = mx_tiles(keep, f"hc{g}", H)
-            quantize(hc_mx[g][0][:], hc_mx[g][1][:], hc_grouped[g][:].rearrange("p c j -> p (c j)"))
-
+        hc_grouped, hc_mx, q_banks, k_banks = {}, {}, {}, {}
         q_grouped = keep.tile([P, GROUPS * R * PACK], BF16, name="q_grouped", align_bytes=256)
         q_mx = mx_tiles(keep, "q", GROUPS * R)
-        q_banks, k_banks = {}, {}
+
+        def group_slots(g):
+            return h_rows[g][:].rearrange("p (s j) -> p s j", s=PACK)
+
+        def group_hc(g, room):
+            hc_grouped[g] = room.rearrange("p (j s) -> p j s", s=PACK)
+            in0 = group_slots(g).rearrange("p s j -> p j s")
+            gpsimd.tensor_scalar(out=hc_grouped[g], in0=in0, scalar1=1.0, scalar2=0.0, op0=ALU.mult, op1=ALU.add)
+
+        def x_room(i):
+            return x_grouped[i][:].rearrange("p s c n t -> p (s c n t)")
 
         def turn_q(g):
-            bank = psum.tile([P, 2, 2, P], F32, name="turn_bank", bufs=TURN_BANKS)
+            q_banks[g] = turn_bank([P, 2, 2, P])
             for b in range(2):
                 words = q_sb[:, b, :].bitcast(F32)
                 for u in range(2):
-                    nc.tensor.transpose(bank[:, b, u, :], words[:, 256 * g + u : 256 * (g + 1) : 2], ident[:])
-            q_banks[g] = bank
+                    nc.tensor.transpose(q_banks[g][:, b, u, :], words[:, 256 * g + u : 256 * (g + 1) : 2], ident[:])
 
-        def copy_q(g, engine="S"):
+        def copy_q(engine, g):
             words = q_grouped[:, g * R * PACK : (g + 1) * R * PACK].bitcast(F32)
-            copy(engine, words.rearrange("p (b r u) -> p b r u", b=2, u=2), q_banks[g][:].rearrange("p b u r -> p b r u"))
-
-        def move_q(g, engine="S"):
-            turn_q(g)
-            copy_q(g, engine)
-
-        def quant_q():
-            quantize(q_mx[0][:], q_mx[1][:], q_grouped[:])
+            out = words.rearrange("p (b r u) -> p b r u", b=2, u=2)
+            copy(engine, out, q_banks[g][:].rearrange("p b u r -> p b r u"))
 
         def contrast(g):
+            hc_mx[g] = mx_tiles(keep, f"hc{g}", H)
+            quantize(hc_mx[g], slice(0, H), hc_grouped[g].rearrange("p j s -> p (j s)"))
             for b in range(2):
                 if g == 0:
-                    k_banks[b] = psum.tile([P, H], F32, name="y_bank", bufs=Y_BANKS)
+                    k_banks[b] = y_bank()
                 cols = slice(g * R + b * P, g * R + (b + 1) * P)
-                mx_pass(k_banks[b][:], q_mx, cols, hc_mx[g], slice(0, H), g == 0, g == GROUPS - 1)
+                mx_pass(k_banks[b], q_mx, cols, hc_mx[g], g == 0, g == GROUPS - 1)
 
         def finish_contrast(b):
             res = work.tile([P, H], F32, name="contrast_sb")
-            nc.vector.tensor_tensor(
+            vector.tensor_tensor(
                 out=res[:].rearrange("p (m u e) -> p m u e", u=2, e=2),
                 in0=k_banks[b][:].rearrange("p (u m e) -> p m u e", u=2, e=2),
                 in1=unit_bc[:].rearrange("p (m u e) -> p m u e", u=2, e=2),
@@ -382,35 +326,15 @@ def tile_library_size_autoencoder_f6_kernel(
             )
             nc.sync.dma_start(out=out_contrast[b * P : (b + 1) * P, :], in_=res[:])
 
-        def warm(source, count, name="h_bank", bufs=1):
-            bank = psum.tile([P, BANK], F32, name=name, bufs=bufs)
-            for n in range(count):
-                nc.tensor.matmul(out=bank[:], lhsT=ident16[:], rhs=source, start=True, stop=True)
-
-        def load_small():
-            nc.scalar.dma_start(out=wsc_sb[:], in_=w_dec_scale.rearrange("(p t) o -> p (t o)", t=PACK))
-            nc.scalar.dma_start(out=benc_sb[:], in_=b_enc.rearrange("(n m) -> n m", n=P))
-
-        def load_bdec():
-            nc.scalar.dma_start(
-                out=bdec_sb[:].rearrange("n (h m) -> n h m", h=2), in_=b_dec.rearrange("(h n m) -> n h m", h=2, n=P)
-            )
-
-        def identities():
-            nc.vector.memset(ident[:], 0.0)
-            make_identity(nc, ident[:], nomemset=True)
-            nc.scalar.copy(out=ident16[:], in_=ident[:])
-
-        def reciprocals():
-            nc.vector.reciprocal(out=invlib[:, 0, :], in_=lib_first[:])
-            nc.vector.reciprocal(out=invlib[:, 1:, :], in_=lib_rest[:])
-
-        load_small()
-        load_bdec()
-        load_wd(0, 2)
-        load_wd(2, 4)
-        load_w(0)
-        load_w(1)
+        scalar.dma_start(out=wsc_sb[:], in_=w_dec_scale.rearrange("(p t) o -> p (t o)", t=PACK))
+        scalar.dma_start(out=benc_sb[:], in_=b_enc.rearrange("(n m) -> n m", n=P))
+        scalar.dma_start(
+            out=bdec_sb[:].rearrange("n (h m) -> n h m", h=2), in_=b_dec.rearrange("(h n m) -> n h m", h=2, n=P)
+        )
+        for lo in (0, 2):
+            nc.sync.dma_start(out=wd_bytes[:, lo : lo + 2], in_=wd_view[:, lo : lo + 2])
+        for c in range(KP):
+            nc.sync.dma_start(out=w_raw[c][:], in_=w_view[c])
         load_x(0, 0, 1)
         load_x(0, 1, 2)
         load_x(1)
@@ -425,46 +349,51 @@ def tile_library_size_autoencoder_f6_kernel(
         load_x(7)
         nc.sync.dma_start(out=depth_sb[:], in_=depth.rearrange("(g p s) -> p g s", p=P, s=PACK))
         nc.sync.dma_start(out=unit_bc[:], in_=unit.partition_broadcast(P))
-        identities()
-        widen_wd(0, "V")
-        widen_wd(1, "S", 0, 2)
-        spread("enc", benc_sb, 0)
-        spread(0, bdec_sb, 0)
-        spread(1, bdec_sb, PACK)
-        widen_wd(1, "S", 2, 4)
-        group_wd(0, "S", 256, 512)
-        copy_benc("S")
-        copy_bdec(0, "S")
+
+        vector.memset(ident[:], 0.0)
+        make_identity(nc, ident[:], nomemset=True)
+        scalar.copy(out=ident16[:], in_=ident[:])
+        widen_wd(vector, 0, range(PACK))
+        widen_wd(scalar, 1, range(2))
+        benc_bank = spread(benc_sb[:])
+        bdec_banks = [spread(bdec_sb[:, n * PACK : (n + 1) * PACK]) for n in range(2)]
+        widen_wd(scalar, 1, range(2, PACK))
+        interleave(scalar, wd_grouped[0], wd_wide[0], BANK // 2, BANK)
+        copy(
+            scalar,
+            benc_bc[:].rearrange("p (u m e) -> p u m e", u=2, e=2),
+            benc_bank[:].rearrange("p (u e) m -> p u m e", u=2),
+        )
+        copy_bdec(0, bdec_banks[0])
         move_x(0, 0)
         move_x(0, 1)
-        copy_bdec(1, "S")
-        turn_x(1, 0, "h_bank", 1)
-        copy_x(1, 0)
+        copy_bdec(1, bdec_banks[1])
+        move_x(1, 0, h_bank(x_shape)[:])
         move_x(1, 1)
-        group_wd(0, "V", 0, 256)
-        group_we(0, "V")
-        group_we(1, "V")
-        quant_we(0)
-        quant_we(1)
+        interleave(vector, wd_grouped[0], wd_wide[0], 0, BANK // 2)
+        for c in range(KP):
+            group_we(c)
+        for c in range(KP):
+            quant_we(c)
         quant_x(0, 0, 1)
         quant_wd(0)
         quant_x(0, 1, 2)
         encode(0, 0)
         encode(0, 1)
-        group_wd(1, "S")
+        interleave(scalar, wd_grouped[1], wd_wide[1], 0, BANK)
         bias_y(0, 0)
         quant_x(1)
         move_x(2, 0)
         move_x(2, 1)
         encode(1, 0)
         bias_y(0, 1)
-        turn_x(3, 0, "d_bank", D_BANKS)
-        copy_x(3, 0)
-        reciprocals()
+        move_x(3, 0, d_bank(x_shape)[:])
+        vector.reciprocal(out=invlib[:, 0, :], in_=lib_first[:])
+        vector.reciprocal(out=invlib[:, 1:, :], in_=lib_rest[:])
         leaky(0)
         turn_h(0)
         encode(1, 1)
-        copy_h(0)
+        copy_h(scalar, 0)
         move_x(3, 1)
         move_x(4, 0)
         quant_wd(1)
@@ -472,188 +401,175 @@ def tile_library_size_autoencoder_f6_kernel(
         quant_x(2)
         encode(2, 0)
         bias_y(1, 1)
-        def open_decoder(j):
-            quant_h(j)
-            for m in range(D_BANKS):
-                decode(j, m)
+
 
         quant_h(0)
         decode(0, 0)
-        decode(0, 3, into=y_banks[1, 1])
+        decode(0, 3, y_banks[1, 1])
         decode(0, 1)
         decode(0, 2)
-        scale_d(0)
+        scalar.activation(out=z_tile(0, 0, 0, BANK), in_=d_banks[0, 0][:], func=ACT.Copy, scale=inv_of(0, 0))
         leaky(1)
         turn_h(1)
         quant_x(3)
-        first_bank = x_grouped[3][:, 0].rearrange("p c n j -> p (c n j)").bitcast(F32)
-        add_bdec(0, first_bank)
-        copy_h(1)
+        first_z = x_room(3)[:, : 2 * BANK].bitcast(F32)
+        gpsimd.tensor_tensor(out=first_z, in0=z_tile(0, 0, 0, BANK), in1=bdec_bc[:, :BANK], op=ALU.add)
+        copy_h(scalar, 1)
         move_x(4, 1)
         bias_d(0, 3)
         encode(2, 1)
         turn_x(5, 0)
         turn_x(5, 1)
         bias_d(0, 1)
-        exp(0, 0, 1, BANK, G)
+        exp(z_tile(0, 0, BANK, G))
         bias_d(0, 2)
-        exp(0, 1, 2)
-        nc.scalar.activation(out=z[0][:, 0, :BANK], in_=first_bank, func=ACT.Exp)
+        exp(z_tile(0, 1))
+        scalar.activation(out=z_tile(0, 0, 0, BANK), in_=first_z, func=ACT.Exp)
         copy_x(5, 0)
         copy_x(5, 1)
         bias_y(2, 0)
         encode(3, 0)
         bias_y(2, 1)
+
+        def read_decoder(j, scalar_first=None):
+            bias_d(j, 1)
+            if scalar_first is not None:
+                copy_h(scalar, scalar_first)
+            exp(z_tile(j, 0))
+            bias_d(j, 2)
+            bias_d(j, 3)
+            exp(z_tile(j, 1))
+
         open_decoder(1)
-        turn_x(6, 0, into=y_banks[2, 1])
-        copy_x(6, 0)
+        move_x(6, 0, y_banks[2, 1][:].rearrange("p (c u n) -> p c u n", c=KP, u=2))
         move_x(6, 1)
         leaky(2)
         turn_h(2)
         quant_x(4)
-        group_hc(0, "G", into=x_grouped[4][:].rearrange("p s c n j -> p (s c n j)"))
+        group_hc(0, x_room(4))
         bias_d(1, 0)
         decode(1, 3)
         encode(3, 1)
         turn_x(7, 0)
         turn_x(7, 1)
-        bias_d(1, 1)
-        copy_h(2)
-        exp(1, 0, 1)
-        bias_d(1, 2)
-        bias_d(1, 3)
-        exp(1, 1, 2)
+        read_decoder(1, scalar_first=2)
         bias_y(3, 0)
         encode(4, 0)
         bias_y(3, 1)
         copy_x(7, 0)
         copy_x(7, 1)
+
         open_decoder(2)
         leaky(3)
         turn_h(3)
-        copy_h(3)
+        copy_h(scalar, 3)
         bias_d(2, 0)
         decode(2, 3)
         encode(4, 1)
         turn_q(0)
         turn_q(1)
-        bias_d(2, 1)
-        exp(2, 0, 1)
-        bias_d(2, 2)
-        bias_d(2, 3)
-        exp(2, 1, 2)
-        copy_q(0)
-        copy_q(1)
+        read_decoder(2)
+        copy_q(scalar, 0)
+        copy_q(scalar, 1)
         open_decoder(3)
         quant_x(5)
         quant_x(6)
-        group_hc(1, "G", into=x_grouped[6][:].rearrange("p s c n j -> p (s c n j)"))
+        group_hc(1, x_room(6))
         bias_d(3, 0)
         decode(3, 3)
-        encode(5, 0, psum.tile([P, H], F32, name="turn_bank", bufs=TURN_BANKS))
+        encode(5, 0, turn_bank([P, BANK]))
         turn_q(2)
-        bias_d(3, 1)
-        exp(3, 0, 1)
-        bias_d(3, 2)
-        bias_d(3, 3)
-        exp(3, 1, 2)
-        log_group(0)
+        read_decoder(3)
+        log1p(z[0][:])
+
         bias_y(4, 0)
         encode(5, 1)
         bias_y(4, 1)
-        copy_q(2, "V")
+        copy_q(vector, 2)
         leaky(4)
         turn_h(4)
         bias_y(5, 0)
         bias_y(5, 1)
         encode(6, 0, y_banks[5, 1])
-        copy_h(4, "V")
+        hc_room = keep.tile([P, H * PACK], BF16, name="we_grouped0", align_bytes=256)
+        copy_h(vector, 4, hc_room)
         quant_x(7)
-        for i in range(5, PAIRS):
-            j = i - 1
-            if i < 7:
-                open_decoder(j)
-                leaky(i)
-            else:
-                quant_h(j)
-                decode(j, 0)
-                decode(j, 1)
-                leaky(i)
-                turn_h(i)
-                decode(j, 2)
-            if i == 5:
-                group_hc(2, "G", into=wide_h[4][:])
-            if i == 6:
-                finish(0, 0, "G", res=sums[i][:])
-                finish(0, 1, "G")
-            if i == 7:
-                finish(1, 0, "G", res=sums[i][:])
-            bias_d(j, 0)
-            if i == 5:
-                turn_h(i)
-            decode(j, 3)
-            if i == 6:
-                turn_h(i)
-            if i == 5:
-                encode(i + 1, 1)
-            if i == 5:
-                turn_q(3)
-                copy_h(i, "S")
-                log_group(1)
-            bias_d(j, 1)
-            if i == 7:
-                copy_h(i, "V")
-            bias_d(j, 2)
-            if i == 6:
-                encode(7, 1, d_banks[j, 2])
-            if i == 7:
-                quant_h(i)
-                finish(1, 1, "G", res=wide_h[7][:].bitcast(F32))
-                finish(2, 0, "G", 0, 640)
-                decode(i, 0)
-                decode(i, 1)
-            bias_d(j, 3)
-            if i < 7:
-                bias_y(i + 1, 0)
-                if i + 2 < PAIRS:
-                    encode(i + 2, 0)
-                if i == 6:
-                    copy_h(i, "V")
-                bias_y(i + 1, 1)
-            else:
-                decode(i, 2)
-                copy_q(3, "V")
-            if i == 6:
-                exp_group(2)
-        exp(6, 0, 1)
-        exp(6, 1, 2)
+
+        open_decoder(4)
+        leaky(5)
+        group_hc(2, hc_room[:])
+        bias_d(4, 0)
+        turn_h(5)
+        decode(4, 3)
+        encode(6, 1)
+        turn_q(3)
+        copy_h(scalar, 5)
+        log1p(z[1][:])
+        for m in range(1, 4):
+            bias_d(4, m)
+        bias_y(6, 0)
+        encode(7, 0)
+        bias_y(6, 1)
+
+        open_decoder(5)
+        leaky(6)
+        finish(gpsimd, 0, 0, res=sums[6][:])
+        finish(gpsimd, 0, 1)
+        bias_d(5, 0)
+        decode(5, 3)
+        turn_h(6)
+        bias_d(5, 1)
+        bias_d(5, 2)
+        encode(7, 1, d_banks[5, 2])
+        bias_d(5, 3)
+        bias_y(7, 0)
+        copy_h(vector, 6)
+        bias_y(7, 1)
+        exp(z[2][:])
+
+        quant_h(6)
+        decode(6, 0)
+        decode(6, 1)
+        leaky(7)
+        turn_h(7)
+        decode(6, 2)
+        finish(gpsimd, 1, 0, res=sums[7][:])
+        bias_d(6, 0)
+        decode(6, 3)
+        bias_d(6, 1)
+        last_room = keep.tile([P, 2 * G], BF16, name="last_room", align_bytes=256)
+        copy_h(vector, 7, last_room)
+        bias_d(6, 2)
+        quant_h(7)
+        finish(gpsimd, 1, 1, res=last_room[:].bitcast(F32))
+        finish(gpsimd, 2, 0, 0, GPSIMD_COLS)
+        decode(7, 0)
+        decode(7, 1)
+        bias_d(6, 3)
+        decode(7, 2)
+        copy_q(vector, 3)
+        exp(z_tile(6, 0))
+        exp(z_tile(6, 1))
         bias_d(7, 0)
         decode(7, 3)
         for m in range(1, 4):
             bias_d(7, m)
-        LEFT = [(2, 1), (3, 0), (3, 1)]
-        exp(7, 0, 1)
-        exp(7, 1, 2)
-        finish(2, 0, "V", 640, G)
-        for k, s in LEFT:
-            finish(k, s)
-        quant_q()
-        group_hc(3, "V")
-        for g in range(0):
-            quant_hc(g)
-            contrast(g)
-        for k in range(4, PAIRS):
-            for s in range(2):
-                if (k, s) in ((4, 0), (7, 1)):
-                    for lo in (0, BANK):
-                        log(k, s, s + 1, lo, lo + BANK)
-                        finish(k, s, "V", lo, lo + BANK)
-                else:
-                    log(k, s, s + 1)
-                    finish(k, s)
-                n = 2 * (k - 4) + s
-                if n + 0 < GROUPS:
-                    quant_hc(n + 0)
-                    contrast(n + 0)
-                if n + 0 in (GROUPS, GROUPS + 1):
-                    finish_contrast(n + 0 - GROUPS)
+        exp(z_tile(7, 0))
+        exp(z_tile(7, 1))
+
+        finish(vector, 2, 0, GPSIMD_COLS, G)
+        finish(vector, 2, 1)
+        finish(vector, 3, 0)
+        finish(vector, 3, 1)
+        quantize(q_mx, slice(0, GROUPS * R), q_grouped[:])
+        last = GROUPS - 1
+        hc_grouped[last] = keep.tile([P, H, PACK], BF16, name="wd_grouped1", align_bytes=256)[:]
+        interleave(vector, hc_grouped[last], group_slots(last), 0, H)
+        for n in range(2 * BATCH):
+            i, s = BATCH + n // 2, n % 2
+            log1p(z_tile(i, s))
+            finish(vector, i, s)
+            if n < GROUPS:
+                contrast(n)
+            elif n < GROUPS + 2:
+                finish_contrast(n - GROUPS)

@@ -27,7 +27,6 @@ TURN_BANKS, Y_BANKS, D_BANKS = 2, 2, 3
 X_BUFS = PAIRS + 1
 CODE_BUFS = 3
 BATCH = PAIRS // 2
-GPSIMD_COLS = 640
 
 
 def tile_library_size_autoencoder_f6_kernel(
@@ -270,15 +269,24 @@ def tile_library_size_autoencoder_f6_kernel(
         def log1p(part):
             scalar.activation(out=part, in_=part, func=ACT.Ln, bias=1.0)
 
-        def finish(engine, i, s, lo=0, hi=G, res=None):
-            part = z_tile(i, s, lo, hi)
-            res = part if res is None else res
+        def times_depth(engine, i, s, res):
+            part = z_tile(i, s)
             factor = depth_sb[:, i // 2, slot_of(i, s) : slot_of(i, s) + 1]
             if engine is vector:
                 vector.tensor_scalar(out=res, in0=part, scalar1=factor, scalar2=None, op0=ALU.mult)
             else:
                 gpsimd.tensor_scalar(out=res, in0=part, scalar1=factor, scalar2=0.0, op0=ALU.mult, op1=ALU.add)
-            nc.sync.dma_start(out=mean_view[i // 2][:, slot_of(i, s), lo:hi], in_=res)
+
+        def finish(engine, i, s, res=None):
+            res = z_tile(i, s) if res is None else res
+            times_depth(engine, i, s, res)
+            nc.sync.dma_start(out=mean_view[i // 2][:, slot_of(i, s), :], in_=res)
+
+        def finish_pair(i):
+            slots = slice(slot_of(i, 0), slot_of(i, 2))
+            for s in range(2):
+                times_depth(vector, i, s, z_tile(i, s))
+            nc.sync.dma_start(out=mean_view[i // 2][:, slots, :], in_=z[i // 2][:, slots, :])
 
         hc_grouped, hc_mx, q_banks, k_banks = {}, {}, {}, {}
         q_grouped = keep.tile([P, GROUPS * R * PACK], BF16, name="q_grouped", align_bytes=256)
@@ -542,7 +550,7 @@ def tile_library_size_autoencoder_f6_kernel(
         bias_d(6, 2)
         quant_h(7)
         finish(gpsimd, 1, 1, res=last_room[:].bitcast(F32))
-        finish(gpsimd, 2, 0, 0, GPSIMD_COLS)
+        finish(gpsimd, 2, 0)
         decode(7, 0)
         decode(7, 1)
         bias_d(6, 3)
@@ -554,13 +562,11 @@ def tile_library_size_autoencoder_f6_kernel(
         decode(7, 3)
         for m in range(1, 4):
             bias_d(7, m)
-        exp(z_tile(7, 0))
-        exp(z_tile(7, 1))
+        for m in range(4):
+            exp(z_tile(7, m // 2, m % 2 * BANK, (m % 2 + 1) * BANK))
 
-        finish(vector, 2, 0, GPSIMD_COLS, G)
         finish(vector, 2, 1)
-        finish(vector, 3, 0)
-        finish(vector, 3, 1)
+        finish_pair(3)
         quantize(q_mx, slice(0, GROUPS * R), q_grouped[:])
         last = GROUPS - 1
         hc_grouped[last] = keep.tile([P, H, PACK], BF16, name="wd_grouped1", align_bytes=256)[:]

@@ -334,6 +334,11 @@ def tile_library_size_autoencoder_f6_kernel(
             )
             nc.sync.dma_start(out=out_contrast[b * P : (b + 1) * P, :], in_=res[:])
 
+        def warm_up(count, moving):
+            bank = y_bank()
+            for n in range(count):
+                nc.tensor.matmul(out=bank[:], lhsT=ident16[:], rhs=moving, start=True, stop=True)
+
         scalar.dma_start(out=wsc_sb[:], in_=w_dec_scale.rearrange("(p t) o -> p (t o)", t=PACK))
         scalar.dma_start(out=benc_sb[:], in_=b_enc.rearrange("(n m) -> n m", n=P))
         scalar.dma_start(
@@ -366,6 +371,7 @@ def tile_library_size_autoencoder_f6_kernel(
         benc_bank = spread(benc_sb[:])
         bdec_banks = [spread(bdec_sb[:, n * PACK : (n + 1) * PACK]) for n in range(2)]
         widen_wd(scalar, 1, range(2, PACK))
+        warm_up(3, w_raw[0][:, 0, :])
         interleave(scalar, wd_grouped[0], wd_wide[0], BANK // 2, BANK)
         copy(
             scalar,
@@ -375,6 +381,7 @@ def tile_library_size_autoencoder_f6_kernel(
         copy_bdec(0, bdec_banks[0])
         move_x(0, 0)
         move_x(0, 1)
+        warm_up(2, w_raw[0][:, 0, :])
         copy_bdec(1, bdec_banks[1])
         move_x(1, 0, h_bank(x_shape)[:])
         move_x(1, 1)

@@ -75,8 +75,8 @@ def tile_library_size_autoencoder_f6_kernel(
         def h_bank(shape):
             return psum.tile(shape, F32, name="h_bank", bufs=1)
 
-        def y_bank():
-            return psum.tile([P, BANK], F32, name="y_bank", bufs=Y_BANKS)
+        def y_bank(shape=(P, BANK)):
+            return psum.tile(list(shape), F32, name="y_bank", bufs=Y_BANKS)
 
         def d_bank(shape):
             return psum.tile(shape, F32, name="d_bank", bufs=D_BANKS)
@@ -214,8 +214,8 @@ def tile_library_size_autoencoder_f6_kernel(
                 out=pair_rows(i), in0=sums[i][:], scalar=SLOPE, in1=sums[i][:], op0=ALU.mult, op1=ALU.max
             )
 
-        def turn_h(i):
-            h_banks[i] = h_bank([P, 2, 2, P])
+        def turn_h(i, new_bank=h_bank):
+            h_banks[i] = new_bank([P, 2, 2, P])
             words = pair_rows(i).bitcast(F32)
             for s in range(2):
                 for u in range(2):
@@ -224,7 +224,7 @@ def tile_library_size_autoencoder_f6_kernel(
 
         def copy_h(engine, i, room=None):
             if room is None:
-                room = work.tile([P, 2 * H], BF16, name="h_grouped", align_bytes=256, bufs=1)
+                room = work.tile([P, 2 * H], BF16, name="h_grouped", align_bytes=256, bufs=2)
             h_grouped[i] = room[:, : 2 * H]
             words = h_grouped[i].bitcast(F32).rearrange("p (s n u) -> p s n u", s=2, u=2)
             copy(engine, words, h_banks[i][:].rearrange("p s u n -> p s n u"))
@@ -303,8 +303,8 @@ def tile_library_size_autoencoder_f6_kernel(
         def x_room(i):
             return x_grouped[i][:].rearrange("p s c n t -> p (s c n t)")
 
-        def turn_q(g):
-            q_banks[g] = turn_bank([P, 2, 2, P])
+        def turn_q(g, new_bank):
+            q_banks[g] = new_bank([P, 2, 2, P])
             for b in range(2):
                 words = q_sb[:, b, :].bitcast(F32)
                 for u in range(2):
@@ -320,7 +320,7 @@ def tile_library_size_autoencoder_f6_kernel(
             quantize(hc_mx[g], slice(0, H), hc_grouped[g].rearrange("p j s -> p (j s)"))
             for b in range(2):
                 if g == 0:
-                    k_banks[b] = y_bank()
+                    k_banks[b] = next_bank()
                 cols = slice(g * R + b * P, g * R + (b + 1) * P)
                 mx_pass(k_banks[b], q_mx, cols, hc_mx[g], g == 0, g == GROUPS - 1)
 
@@ -384,7 +384,6 @@ def tile_library_size_autoencoder_f6_kernel(
         warm_up(2, w_raw[0][:, 0, :])
         copy_bdec(1, bdec_banks[1])
         move_x(1, 0, h_bank(x_shape)[:])
-        move_x(1, 1)
         interleave(vector, wd_grouped[0], wd_wide[0], 0, BANK // 2)
         for c in range(KP):
             group_we(c)
@@ -395,194 +394,209 @@ def tile_library_size_autoencoder_f6_kernel(
         quant_x(0, 1, 2)
         encode(0, 0)
         encode(0, 1)
-        interleave(scalar, wd_grouped[1], wd_wide[1], 0, BANK)
+        interleave(scalar, wd_grouped[1], wd_wide[1], 0, BANK // 2)
         bias_y(0, 0)
-        quant_x(1)
-        move_x(2, 0)
-        move_x(2, 1)
+        quant_x(1, 0, 1)
+        move_x(1, 1)
         encode(1, 0)
+        interleave(scalar, wd_grouped[1], wd_wide[1], BANK // 2, BANK)
+        move_x(2, 0)
         bias_y(0, 1)
-        move_x(3, 0, d_bank(x_shape)[:])
         vector.reciprocal(out=invlib[:, 0, :], in_=lib_first[:])
         vector.reciprocal(out=invlib[:, 1:, :], in_=lib_rest[:])
         leaky(0)
         turn_h(0)
-        encode(1, 1)
         copy_h(scalar, 0)
-        move_x(3, 1)
-        move_x(4, 0)
-        quant_wd(1)
+        quant_x(1, 1, 2)
+        encode(1, 1)
+        move_x(2, 1)
         bias_y(1, 0)
-        quant_x(2)
-        encode(2, 0)
+        quant_wd(1)
+        move_x(3, 0)
         bias_y(1, 1)
 
+        def add_bdec(i, room):
+            res = room[:, : 2 * BANK].bitcast(F32)
+            gpsimd.tensor_tensor(out=res, in0=z_tile(i, 0, 0, BANK), in1=bdec_bc[:, :BANK], op=ALU.add)
+            return res
 
-        quant_h(0)
-        decode(0, 0)
-        decode(0, 3, y_banks[1, 1])
-        decode(0, 1)
-        decode(0, 2)
-        scalar.activation(out=z_tile(0, 0, 0, BANK), in_=d_banks[0, 0][:], func=ACT.Copy, scale=inv_of(0, 0))
+        def divide_d(i):
+            scalar.activation(out=z_tile(i, 0, 0, BANK), in_=d_banks[i, 0][:], func=ACT.Copy, scale=inv_of(i, 0))
+
+        open_decoder(0)
+        decode(0, 3, y_bank())
+        divide_d(0)
+        move_x(3, 1)
         leaky(1)
         turn_h(1)
-        quant_x(3)
-        first_z = x_room(3)[:, : 2 * BANK].bitcast(F32)
-        gpsimd.tensor_tensor(out=first_z, in0=z_tile(0, 0, 0, BANK), in1=bdec_bc[:, :BANK], op=ALU.add)
         copy_h(scalar, 1)
-        move_x(4, 1)
-        bias_d(0, 3)
-        encode(2, 1)
-        turn_x(5, 0)
-        turn_x(5, 1)
+        quant_x(2)
+        biased = add_bdec(0, x_room(2))
+        encode(2, 0)
+        encode(2, 1, d_bank([P, BANK]))
+        turn_x(4, 0)
+        turn_x(4, 1)
         bias_d(0, 1)
         exp(z_tile(0, 0, BANK, G))
         bias_d(0, 2)
+        bias_d(0, 3)
         exp(z_tile(0, 1))
-        scalar.activation(out=z_tile(0, 0, 0, BANK), in_=first_z, func=ACT.Exp)
-        copy_x(5, 0)
-        copy_x(5, 1)
+        copy_x(4, 0)
+        copy_x(4, 1)
+        scalar.activation(out=z_tile(0, 0, 0, BANK), in_=biased, func=ACT.Exp)
         bias_y(2, 0)
-        encode(3, 0)
         bias_y(2, 1)
 
-        def read_decoder(j, scalar_first=None):
-            bias_d(j, 1)
-            if scalar_first is not None:
-                copy_h(scalar, scalar_first)
-            exp(z_tile(j, 0))
-            bias_d(j, 2)
-            bias_d(j, 3)
-            exp(z_tile(j, 1))
-
         open_decoder(1)
-        move_x(6, 0, y_banks[2, 1][:].rearrange("p (c u n) -> p c u n", c=KP, u=2))
-        move_x(6, 1)
+        decode(1, 3, y_bank())
+        move_x(5, 0)
         leaky(2)
         turn_h(2)
-        quant_x(4)
-        group_hc(0, x_room(4))
+        copy_h(scalar, 2)
+        quant_x(3)
+        group_hc(0, x_room(3))
+        encode(3, 0)
+        turn_x(5, 1)
         bias_d(1, 0)
-        decode(1, 3)
-        encode(3, 1)
-        turn_x(7, 0)
-        turn_x(7, 1)
-        read_decoder(1, scalar_first=2)
+        encode(3, 1, d_bank([P, BANK]))
+        bias_d(1, 1)
+        exp(z_tile(1, 0))
+        copy_x(5, 1)
+        turn_x(6, 0)
+        turn_x(6, 1)
+        bias_d(1, 2)
+        bias_d(1, 3)
+        exp(z_tile(1, 1))
         bias_y(3, 0)
-        encode(4, 0)
         bias_y(3, 1)
-        copy_x(7, 0)
-        copy_x(7, 1)
 
         open_decoder(2)
+        decode(2, 3, y_bank())
+        copy_x(6, 0)
+        divide_d(2)
+        copy_x(6, 1)
         leaky(3)
         turn_h(3)
         copy_h(scalar, 3)
-        bias_d(2, 0)
-        decode(2, 3)
-        encode(4, 1)
-        turn_q(0)
-        turn_q(1)
-        read_decoder(2)
-        copy_q(scalar, 0)
-        copy_q(scalar, 1)
-        open_decoder(3)
-        quant_x(5)
-        quant_x(6)
-        group_hc(1, x_room(6))
-        bias_d(3, 0)
-        decode(3, 3)
-        encode(5, 0, turn_bank([P, BANK]))
-        turn_q(2)
-        read_decoder(3)
-        log1p(z[0][:])
-
+        quant_x(4)
+        biased = add_bdec(2, x_room(4))
+        encode(4, 0)
+        turn_x(7, 0)
+        turn_x(7, 1)
+        bias_d(2, 1)
+        exp(z_tile(2, 0, BANK, G))
+        bias_d(2, 2)
+        bias_d(2, 3)
+        exp(z_tile(2, 1))
+        scalar.activation(out=z_tile(2, 0, 0, BANK), in_=biased, func=ACT.Exp)
+        copy_x(7, 0)
+        copy_x(7, 1)
         bias_y(4, 0)
-        encode(5, 1)
+
+        open_decoder(3)
+        decode(3, 3, y_bank())
+        encode(4, 1)
+        quant_x(5)
+        group_hc(1, x_room(5))
+        encode(5, 0, h_bank([P, BANK]))
+        encode(5, 1, turn_bank([P, BANK]))
+        bias_d(3, 0)
+        bias_d(3, 1)
+        exp(z_tile(3, 0))
+        bias_d(3, 2)
+        bias_d(3, 3)
+        exp(z_tile(3, 1))
+        log1p(z[0][:])
+        log1p(z[1][:])
+
+        order = [turn_bank, d_bank, d_bank, d_bank, y_bank, y_bank, h_bank, turn_bank]
+        taken = []
+
+        def next_bank(shape=(P, BANK)):
+            taken.append(shape)
+            return order[(len(taken) - 1) % len(order)](list(shape))
+
+        def exp_bank(i, m):
+            exp(z_tile(i, m // 2, m % 2 * BANK, (m % 2 + 1) * BANK))
+
         bias_y(4, 1)
-        copy_q(vector, 2)
-        leaky(4)
-        turn_h(4)
         bias_y(5, 0)
         bias_y(5, 1)
-        encode(6, 0, y_banks[5, 1])
-        hc_room = keep.tile([P, H * PACK], BF16, name="we_grouped0", align_bytes=256)
-        copy_h(vector, 4, hc_room)
+        quant_x(6)
+        encode(6, 0, next_bank())
+        leaky(4)
+        encode(6, 1, next_bank())
+        turn_h(4, next_bank)
         quant_x(7)
-
-        open_decoder(4)
+        encode(7, 0, next_bank())
         leaky(5)
-        group_hc(2, hc_room[:])
-        bias_d(4, 0)
-        turn_h(5)
-        decode(4, 3)
-        encode(6, 1)
-        turn_q(3)
-        copy_h(scalar, 5)
-        log1p(z[1][:])
-        for m in range(1, 4):
-            bias_d(4, m)
+        turn_h(5, next_bank)
+        encode(7, 1, next_bank())
+        group_hc(2, sums[5][:].bitcast(BF16))
         bias_y(6, 0)
-        encode(7, 0)
+        copy_h(vector, 4)
         bias_y(6, 1)
-
-        open_decoder(5)
-        leaky(6)
-        finish(gpsimd, 0, 0, res=sums[6][:])
-        finish(gpsimd, 0, 1)
-        bias_d(5, 0)
-        decode(5, 3)
-        turn_h(6)
-        bias_d(5, 1)
-        bias_d(5, 2)
-        encode(7, 1, d_banks[5, 2])
-        bias_d(5, 3)
+        copy_h(vector, 5)
         bias_y(7, 0)
-        copy_h(vector, 6)
         bias_y(7, 1)
-        exp(z[2][:])
 
-        quant_h(6)
-        decode(6, 0)
-        decode(6, 1)
+        quant_h(4)
+        for m in range(2):
+            decode(4, m, next_bank())
+        quant_h(5)
+        leaky(6)
+        for m in range(2, 4):
+            decode(4, m, next_bank())
+        turn_h(6, next_bank)
+        decode(5, 0, next_bank())
         leaky(7)
-        turn_h(7)
-        decode(6, 2)
-        finish(gpsimd, 1, 0, res=sums[7][:])
-        bias_d(6, 0)
-        decode(6, 3)
-        bias_d(6, 1)
-        last_room = keep.tile([P, 2 * G], BF16, name="last_room", align_bytes=256)
-        copy_h(vector, 7, last_room)
-        bias_d(6, 2)
-        quant_h(7)
-        finish(gpsimd, 1, 1, res=last_room[:].bitcast(F32))
-        finish(gpsimd, 2, 0)
-        decode(7, 0)
-        decode(7, 1)
-        bias_d(6, 3)
-        decode(7, 2)
-        copy_q(vector, 3)
-        exp(z_tile(6, 0))
-        exp(z_tile(6, 1))
-        bias_d(7, 0)
-        decode(7, 3)
-        for m in range(1, 4):
-            bias_d(7, m)
+        turn_h(7, next_bank)
+        decode(5, 1, next_bank())
+        finish(gpsimd, 0, 0, res=sums[7][:])
+        finish(gpsimd, 0, 1)
         for m in range(4):
-            exp(z_tile(7, m // 2, m % 2 * BANK, (m % 2 + 1) * BANK))
+            bias_d(4, m)
+        decode(5, 2, next_bank())
+        decode(5, 3, next_bank())
+        exp(z[2][:, :2, :])
+        copy_h(vector, 6)
+        copy_h(vector, 7, x_room(6))
+        quant_h(6)
+        for m in range(2):
+            decode(6, m, next_bank())
+        quant_h(7)
+        finish(gpsimd, 1, 0, res=x_room(6).bitcast(F32))
+        for i, s in ((1, 1), (2, 0), (2, 1), (3, 0), (3, 1)):
+            finish(gpsimd, i, s)
+        decode(6, 2, next_bank())
+        decode(6, 3, next_bank())
+        for m in range(4):
+            bias_d(5, m)
+            decode(7, m, next_bank())
+            exp_bank(5, m)
+        for m in range(4):
+            bias_d(6, m)
+            turn_q(m, next_bank)
+            exp_bank(6, m)
+        for m in range(4):
+            bias_d(7, m)
+            exp_bank(7, m)
+        for g in range(GROUPS):
+            copy_q(vector, g)
 
-        finish(vector, 2, 1)
-        finish_pair(3)
-        quantize(q_mx, slice(0, GROUPS * R), q_grouped[:])
+        def quant_q(half):
+            cols = slice(half * 2 * R, (half + 1) * 2 * R)
+            quantize(q_mx, cols, q_grouped[:, cols.start * PACK : cols.stop * PACK])
+
         last = GROUPS - 1
-        hc_grouped[last] = keep.tile([P, H, PACK], BF16, name="wd_grouped1", align_bytes=256)[:]
+        hc_grouped[last] = x_room(7).rearrange("p (j s) -> p j s", s=PACK)
         interleave(vector, hc_grouped[last], group_slots(last), 0, H)
+        quant_q(0)
+        jobs = [(contrast, 0), (contrast, 1), (quant_q, 1), (contrast, 2), (contrast, 3)]
+        jobs = jobs + [(finish_contrast, 0), (finish_contrast, 1)]
         for n in range(2 * BATCH):
             i, s = BATCH + n // 2, n % 2
             log1p(z_tile(i, s))
             finish(vector, i, s)
-            if n < GROUPS:
-                contrast(n)
-            elif n < GROUPS + 2:
-                finish_contrast(n - GROUPS)
+            if n < len(jobs):
+                jobs[n][0](jobs[n][1])

@@ -191,9 +191,9 @@ def tile_library_size_autoencoder_f6_kernel(
                 cols = slice((s * KP + c) * P, (s * KP + c + 1) * P)
                 mx_pass(y_banks[i, s], x_mx[i], cols, we_mx[c], c == 0, c == KP - 1)
 
-        def bias_y(i, s):
+        def bias_y(i, s, room=None):
             if s == 0:
-                sums[i] = work.tile([P, 2 * H], F32, name="sums", bufs=CODE_BUFS)
+                sums[i] = work.tile([P, 2 * H], F32, name="sums", bufs=CODE_BUFS) if room is None else room
             slot = slice(slot_of(i, s), slot_of(i, s) + 1)
             vector.scalar_tensor_tensor(
                 out=sums[i][:, s * H : (s + 1) * H],
@@ -444,7 +444,7 @@ def tile_library_size_autoencoder_f6_kernel(
         copy_x(4, 0)
         copy_x(4, 1)
         scalar.activation(out=z_tile(0, 0, 0, BANK), in_=biased, func=ACT.Exp)
-        bias_y(2, 0)
+        bias_y(2, 0, x_room(1).bitcast(F32))
         bias_y(2, 1)
 
         open_decoder(1)
@@ -453,8 +453,8 @@ def tile_library_size_autoencoder_f6_kernel(
         leaky(2)
         turn_h(2)
         copy_h(scalar, 2)
+        group_hc(0, x_room(1))
         quant_x(3)
-        group_hc(0, x_room(3))
         encode(3, 0)
         turn_x(5, 1)
         bias_d(1, 0)
@@ -463,7 +463,7 @@ def tile_library_size_autoencoder_f6_kernel(
         exp(z_tile(1, 0))
         copy_x(5, 1)
         turn_x(6, 0)
-        turn_x(6, 1)
+        turn_x(6, 1, h_bank(x_shape)[:])
         bias_d(1, 2)
         bias_d(1, 3)
         exp(z_tile(1, 1))
@@ -472,17 +472,17 @@ def tile_library_size_autoencoder_f6_kernel(
 
         open_decoder(2)
         decode(2, 3, y_bank())
-        copy_x(6, 0)
         divide_d(2)
+        copy_x(6, 0)
         copy_x(6, 1)
         leaky(3)
-        turn_h(3)
-        copy_h(scalar, 3)
+        biased = add_bdec(2, sums[3][:].bitcast(BF16))
+        turn_h(3, turn_bank)
+        copy_h(scalar, 3, x_room(3))
         quant_x(4)
-        biased = add_bdec(2, x_room(4))
         encode(4, 0)
         turn_x(7, 0)
-        turn_x(7, 1)
+        turn_x(7, 1, h_bank(x_shape)[:])
         bias_d(2, 1)
         exp(z_tile(2, 0, BANK, G))
         bias_d(2, 2)
@@ -496,9 +496,9 @@ def tile_library_size_autoencoder_f6_kernel(
         open_decoder(3)
         decode(3, 3, y_bank())
         encode(4, 1)
+        group_hc(1, x_room(3))
         quant_x(5)
-        group_hc(1, x_room(5))
-        encode(5, 0, h_bank([P, BANK]))
+        encode(5, 0, turn_bank([P, BANK]))
         encode(5, 1, turn_bank([P, BANK]))
         bias_d(3, 0)
         bias_d(3, 1)
@@ -509,7 +509,7 @@ def tile_library_size_autoencoder_f6_kernel(
         log1p(z[0][:])
         log1p(z[1][:])
 
-        order = [turn_bank, d_bank, d_bank, d_bank, y_bank, y_bank, h_bank, turn_bank]
+        order = [h_bank, d_bank, d_bank, d_bank, y_bank, y_bank, turn_bank, turn_bank]
         taken = []
 
         def next_bank(shape=(P, BANK)):
@@ -527,12 +527,12 @@ def tile_library_size_autoencoder_f6_kernel(
         leaky(4)
         encode(6, 1, next_bank())
         turn_h(4, next_bank)
-        quant_x(7)
-        encode(7, 0, next_bank())
         leaky(5)
         turn_h(5, next_bank)
+        group_hc(2, x_room(5))
+        quant_x(7)
+        encode(7, 0, next_bank())
         encode(7, 1, next_bank())
-        group_hc(2, sums[5][:].bitcast(BF16))
         bias_y(6, 0)
         copy_h(vector, 4)
         bias_y(6, 1)
@@ -552,15 +552,15 @@ def tile_library_size_autoencoder_f6_kernel(
         leaky(7)
         turn_h(7, next_bank)
         decode(5, 1, next_bank())
-        finish(gpsimd, 0, 0, res=sums[7][:])
+        finish(gpsimd, 0, 0, res=sums[6][:])
         finish(gpsimd, 0, 1)
         for m in range(4):
             bias_d(4, m)
         decode(5, 2, next_bank())
         decode(5, 3, next_bank())
         exp(z[2][:, :2, :])
-        copy_h(vector, 6)
-        copy_h(vector, 7, x_room(6))
+        copy_h(vector, 6, x_room(6))
+        copy_h(vector, 7)
         quant_h(6)
         for m in range(2):
             decode(6, m, next_bank())

@@ -26,6 +26,7 @@ KP = G // PASS
 TURN_BANKS, Y_BANKS, D_BANKS = 2, 2, 3
 X_BUFS = PAIRS + 1
 CODE_BUFS = 3
+HC_SPLIT = 320
 BATCH = PAIRS // 2
 
 
@@ -168,10 +169,10 @@ def tile_library_size_autoencoder_f6_kernel(
                 for u in range(2):
                     nc.tensor.transpose(x_banks[i, s][:, c, u, :], words[:, 256 * c + u : 256 * (c + 1) : 2], ident[:])
 
-        def copy_x(i, s):
+        def copy_x(i, s, engine=scalar):
             if s == 0:
                 x_grouped[i] = work.tile([P, 2, KP, P, PACK], BF16, name="x_pair", align_bytes=256, bufs=X_BUFS)
-            copy(scalar, x_grouped[i][:, s].bitcast(F32), x_banks[i, s].rearrange("p c u n -> p c n u"))
+            copy(engine, x_grouped[i][:, s].bitcast(F32), x_banks[i, s].rearrange("p c u n -> p c n u"))
 
         def move_x(i, s, bank=None):
             turn_x(i, s, bank)
@@ -295,10 +296,11 @@ def tile_library_size_autoencoder_f6_kernel(
         def group_slots(g):
             return h_rows[g][:].rearrange("p (s j) -> p s j", s=PACK)
 
-        def group_hc(g, room):
+        def group_hc(g, room, lo=0, hi=H):
             hc_grouped[g] = room.rearrange("p (j s) -> p j s", s=PACK)
-            in0 = group_slots(g).rearrange("p s j -> p j s")
-            gpsimd.tensor_scalar(out=hc_grouped[g], in0=in0, scalar1=1.0, scalar2=0.0, op0=ALU.mult, op1=ALU.add)
+            in0 = group_slots(g)[:, :, lo:hi].rearrange("p s j -> p j s")
+            out = hc_grouped[g][:, lo:hi]
+            gpsimd.tensor_scalar(out=out, in0=in0, scalar1=1.0, scalar2=0.0, op0=ALU.mult, op1=ALU.add)
 
         def x_room(i):
             return x_grouped[i][:].rearrange("p s c n t -> p (s c n t)")
@@ -401,6 +403,7 @@ def tile_library_size_autoencoder_f6_kernel(
         encode(1, 0)
         interleave(scalar, wd_grouped[1], wd_wide[1], BANK // 2, BANK)
         move_x(2, 0)
+        turn_x(2, 1)
         bias_y(0, 1)
         vector.reciprocal(out=invlib[:, 0, :], in_=lib_first[:])
         vector.reciprocal(out=invlib[:, 1:, :], in_=lib_rest[:])
@@ -409,107 +412,112 @@ def tile_library_size_autoencoder_f6_kernel(
         copy_h(scalar, 0)
         quant_x(1, 1, 2)
         encode(1, 1)
-        move_x(2, 1)
+        copy_x(2, 1)
+        move_x(3, 0)
+        move_x(3, 1, h_bank(x_shape)[:])
         bias_y(1, 0)
         quant_wd(1)
-        move_x(3, 0)
         bias_y(1, 1)
 
-        def add_bdec(i, room):
-            res = room[:, : 2 * BANK].bitcast(F32)
-            gpsimd.tensor_tensor(out=res, in0=z_tile(i, 0, 0, BANK), in1=bdec_bc[:, :BANK], op=ALU.add)
-            return res
+        def add_bdec(i, n, res):
+            cols = slice(n * BANK, (n + 1) * BANK)
+            gpsimd.tensor_tensor(out=res[:, cols], in0=z_tile(i, 0)[:, cols], in1=bdec_bc[:, cols], op=ALU.add)
 
-        def divide_d(i):
-            scalar.activation(out=z_tile(i, 0, 0, BANK), in_=d_banks[i, 0][:], func=ACT.Copy, scale=inv_of(i, 0))
+        def divide_d(i, n):
+            out = z_tile(i, 0, n * BANK, (n + 1) * BANK)
+            scalar.activation(out=out, in_=d_banks[i, n][:], func=ACT.Copy, scale=inv_of(i, 0))
+
+        def exp_biased(i, n, biased):
+            cols = slice(n * BANK, (n + 1) * BANK)
+            scalar.activation(out=z_tile(i, 0)[:, cols], in_=biased[:, cols], func=ACT.Exp)
 
         open_decoder(0)
         decode(0, 3, y_bank())
-        divide_d(0)
-        move_x(3, 1)
+        divide_d(0, 0)
+        divide_d(0, 1)
         leaky(1)
         turn_h(1)
         copy_h(scalar, 1)
         quant_x(2)
-        biased = add_bdec(0, x_room(2))
+        first_biased = x_room(2).bitcast(F32)
+        add_bdec(0, 0, first_biased)
         encode(2, 0)
         encode(2, 1, d_bank([P, BANK]))
         turn_x(4, 0)
         turn_x(4, 1)
-        bias_d(0, 1)
-        exp(z_tile(0, 0, BANK, G))
         bias_d(0, 2)
         bias_d(0, 3)
         exp(z_tile(0, 1))
         copy_x(4, 0)
         copy_x(4, 1)
-        scalar.activation(out=z_tile(0, 0, 0, BANK), in_=biased, func=ACT.Exp)
+        move_x(5, 0, h_bank(x_shape)[:])
+        exp_biased(0, 0, first_biased)
         bias_y(2, 0, x_room(1).bitcast(F32))
         bias_y(2, 1)
 
         open_decoder(1)
         decode(1, 3, y_bank())
-        move_x(5, 0)
+        move_x(5, 1)
         leaky(2)
+        group_hc(0, x_room(1), 0, HC_SPLIT)
+        add_bdec(0, 1, first_biased)
         turn_h(2)
         copy_h(scalar, 2)
-        group_hc(0, x_room(1))
         quant_x(3)
         encode(3, 0)
-        turn_x(5, 1)
         bias_d(1, 0)
         encode(3, 1, d_bank([P, BANK]))
         bias_d(1, 1)
         exp(z_tile(1, 0))
-        copy_x(5, 1)
-        turn_x(6, 0)
-        turn_x(6, 1, h_bank(x_shape)[:])
+        move_x(6, 0)
+        turn_x(6, 1)
         bias_d(1, 2)
         bias_d(1, 3)
-        exp(z_tile(1, 1))
+        copy_x(6, 1)
         bias_y(3, 0)
         bias_y(3, 1)
 
         open_decoder(2)
         decode(2, 3, y_bank())
-        divide_d(2)
-        copy_x(6, 0)
-        copy_x(6, 1)
+        divide_d(2, 0)
+        exp_biased(0, 1, first_biased)
         leaky(3)
-        biased = add_bdec(2, sums[3][:].bitcast(BF16))
-        turn_h(3, turn_bank)
+        biased = sums[3][:]
+        add_bdec(2, 0, biased)
+        turn_h(3)
         copy_h(scalar, 3, x_room(3))
+        exp(z_tile(1, 1))
         quant_x(4)
         encode(4, 0)
         turn_x(7, 0)
-        turn_x(7, 1, h_bank(x_shape)[:])
+        turn_x(7, 1)
         bias_d(2, 1)
         exp(z_tile(2, 0, BANK, G))
+        copy_x(7, 0)
         bias_d(2, 2)
         bias_d(2, 3)
         exp(z_tile(2, 1))
-        scalar.activation(out=z_tile(2, 0, 0, BANK), in_=biased, func=ACT.Exp)
-        copy_x(7, 0)
-        copy_x(7, 1)
-        bias_y(4, 0)
+        exp_biased(2, 0, biased)
 
         open_decoder(3)
         decode(3, 3, y_bank())
-        encode(4, 1)
         group_hc(1, x_room(3))
+        group_hc(0, x_room(1), HC_SPLIT, H)
         quant_x(5)
-        encode(5, 0, turn_bank([P, BANK]))
-        encode(5, 1, turn_bank([P, BANK]))
+        bias_y(4, 0)
+        encode(4, 1)
         bias_d(3, 0)
+        encode(5, 0, d_bank([P, BANK]))
         bias_d(3, 1)
         exp(z_tile(3, 0))
         bias_d(3, 2)
         bias_d(3, 3)
+        encode(5, 1)
         exp(z_tile(3, 1))
         log1p(z[0][:])
         log1p(z[1][:])
 
-        order = [h_bank, d_bank, d_bank, d_bank, y_bank, y_bank, turn_bank, turn_bank]
+        order = [h_bank, turn_bank, d_bank, d_bank, turn_bank, y_bank, d_bank, y_bank]
         taken = []
 
         def next_bank(shape=(P, BANK)):
@@ -520,6 +528,7 @@ def tile_library_size_autoencoder_f6_kernel(
             exp(z_tile(i, m // 2, m % 2 * BANK, (m % 2 + 1) * BANK))
 
         bias_y(4, 1)
+        copy_x(7, 1, vector)
         bias_y(5, 0)
         bias_y(5, 1)
         quant_x(6)
@@ -556,9 +565,10 @@ def tile_library_size_autoencoder_f6_kernel(
         finish(gpsimd, 0, 1)
         for m in range(4):
             bias_d(4, m)
+            if m % 2:
+                exp(z_tile(4, m // 2))
         decode(5, 2, next_bank())
         decode(5, 3, next_bank())
-        exp(z[2][:, :2, :])
         copy_h(vector, 6, x_room(6))
         copy_h(vector, 7)
         quant_h(6)

@@ -27,6 +27,7 @@ TURN_BANKS, Y_BANKS, D_BANKS = 2, 2, 3
 X_BUFS = PAIRS + 1
 CODE_BUFS = 3
 HC_SPLIT = 320
+LAST_SPLIT = 128
 BATCH = PAIRS // 2
 
 
@@ -270,24 +271,15 @@ def tile_library_size_autoencoder_f6_kernel(
         def log1p(part):
             scalar.activation(out=part, in_=part, func=ACT.Ln, bias=1.0)
 
-        def times_depth(engine, i, s, res):
-            part = z_tile(i, s)
+        def finish(engine, i, s, res=None, lo=0, hi=G):
+            part = z_tile(i, s, lo, hi)
+            res = part if res is None else res
             factor = depth_sb[:, i // 2, slot_of(i, s) : slot_of(i, s) + 1]
             if engine is vector:
                 vector.tensor_scalar(out=res, in0=part, scalar1=factor, scalar2=None, op0=ALU.mult)
             else:
                 gpsimd.tensor_scalar(out=res, in0=part, scalar1=factor, scalar2=0.0, op0=ALU.mult, op1=ALU.add)
-
-        def finish(engine, i, s, res=None):
-            res = z_tile(i, s) if res is None else res
-            times_depth(engine, i, s, res)
-            nc.sync.dma_start(out=mean_view[i // 2][:, slot_of(i, s), :], in_=res)
-
-        def finish_pair(i):
-            slots = slice(slot_of(i, 0), slot_of(i, 2))
-            for s in range(2):
-                times_depth(vector, i, s, z_tile(i, s))
-            nc.sync.dma_start(out=mean_view[i // 2][:, slots, :], in_=z[i // 2][:, slots, :])
+            nc.sync.dma_start(out=mean_view[i // 2][:, slot_of(i, s), lo:hi], in_=res)
 
         hc_grouped, hc_mx, q_banks, k_banks = {}, {}, {}, {}
         q_grouped = keep.tile([P, GROUPS * R * PACK], BF16, name="q_grouped", align_bytes=256)
@@ -563,6 +555,7 @@ def tile_library_size_autoencoder_f6_kernel(
         decode(5, 1, next_bank())
         finish(gpsimd, 0, 0, res=sums[6][:])
         finish(gpsimd, 0, 1)
+        finish(gpsimd, 1, 0)
         for m in range(4):
             bias_d(4, m)
             if m % 2:
@@ -571,16 +564,21 @@ def tile_library_size_autoencoder_f6_kernel(
         decode(5, 3, next_bank())
         copy_h(vector, 6, x_room(6))
         copy_h(vector, 7)
-        quant_h(6)
         for m in range(2):
+            bias_d(5, m)
+            exp_bank(5, m)
+        quant_h(6)
+        for m in range(4):
             decode(6, m, next_bank())
         quant_h(7)
-        finish(gpsimd, 1, 0, res=x_room(6).bitcast(F32))
-        for i, s in ((1, 1), (2, 0), (2, 1), (3, 0), (3, 1)):
+        finish(gpsimd, 1, 1, res=x_room(6).bitcast(F32))
+        for i, s in ((2, 0), (2, 1), (3, 0), (3, 1)):
             finish(gpsimd, i, s)
-        decode(6, 2, next_bank())
-        decode(6, 3, next_bank())
-        for m in range(4):
+        last = GROUPS - 1
+        group_hc(last, x_room(7), 0, LAST_SPLIT)
+        decode(7, 0, next_bank())
+        decode(7, 1, next_bank())
+        for m in range(2, 4):
             bias_d(5, m)
             decode(7, m, next_bank())
             exp_bank(5, m)
@@ -598,15 +596,16 @@ def tile_library_size_autoencoder_f6_kernel(
             cols = slice(half * 2 * R, (half + 1) * 2 * R)
             quantize(q_mx, cols, q_grouped[:, cols.start * PACK : cols.stop * PACK])
 
-        last = GROUPS - 1
-        hc_grouped[last] = x_room(7).rearrange("p (j s) -> p j s", s=PACK)
-        interleave(vector, hc_grouped[last], group_slots(last), 0, H)
-        quant_q(0)
-        jobs = [(contrast, 0), (contrast, 1), (quant_q, 1), (contrast, 2), (contrast, 3)]
+        interleave(vector, hc_grouped[last], group_slots(last), LAST_SPLIT, H)
+        jobs = [(quant_q, 0), (contrast, 0), (contrast, 1), (quant_q, 1), (contrast, 2), (contrast, 3)]
         jobs = jobs + [(finish_contrast, 0), (finish_contrast, 1)]
+        for job, which in jobs[:1]:
+            job(which)
         for n in range(2 * BATCH):
             i, s = BATCH + n // 2, n % 2
-            log1p(z_tile(i, s))
-            finish(vector, i, s)
-            if n < len(jobs):
-                jobs[n][0](jobs[n][1])
+            width = BANK if n < 8 else G
+            for lo in range(0, G, width):
+                log1p(z_tile(i, s, lo, lo + width))
+                finish(vector, i, s, None, lo, lo + width)
+            for job, which in jobs[1 + n : 1 + n + 1]:
+                job(which)

@@ -603,7 +603,7 @@ def tile_library_size_autoencoder_f6_kernel(
             job(which)
         for n in range(2 * BATCH):
             i, s = BATCH + n // 2, n % 2
-            width = BANK if n < 8 else G
+            width = BANK if n < 6 else G
             for lo in range(0, G, width):
                 log1p(z_tile(i, s, lo, lo + width))
                 finish(vector, i, s, None, lo, lo + width)

@@ -27,7 +27,7 @@ TURN_BANKS, Y_BANKS, D_BANKS = 2, 2, 3
 X_BUFS = PAIRS + 1
 CODE_BUFS = 3
 HC_SPLIT = 320
-LAST_SPLIT = 128
+LAST_SPLIT = 256
 BATCH = PAIRS // 2
 
 

from contextlib import ExitStack

import concourse.mybir as mybir
from concourse.masks import make_identity

C, G, H, R = 2048, 1024, 512, 256
FLOPS = 2 * C * G * H + 2 * C * H * G + 2 * R * C * H
SLOPE = 0.1

F32 = mybir.dt.float32
BF16 = mybir.dt.bfloat16
U32 = mybir.dt.uint32
U8 = mybir.dt.uint8
E4M3 = mybir.dt.float8_e4m3fn
FP8X4 = mybir.dt.float8_e4m3fn_x4
ALU = mybir.AluOpType
ACT = mybir.ActivationFunctionType

P = 128
PACK = 4
PASS = P * PACK
BANK = 512
GROUPS = C // PASS
PAIRS = 2 * GROUPS
KP = G // PASS
TURN_BANKS, Y_BANKS, D_BANKS = 2, 2, 3
X_BUFS = PAIRS + 1
CODE_BUFS = 3
HC_SPLIT = 320
LAST_SPLIT = 256
BATCH = PAIRS // 2


def tile_library_size_autoencoder_f6_kernel(
    tc, x, lib, w_enc, b_enc, w_dec_bytes, w_dec_scale, b_dec, depth, q, unit, out_mean, out_contrast
):
    nc = tc.nc
    scalar, vector, gpsimd = nc.scalar, nc.vector, nc.gpsimd
    with ExitStack() as ctx:
        keep = ctx.enter_context(tc.tile_pool(name="keep", bufs=1))
        work = ctx.enter_context(tc.tile_pool(name="work", bufs=2))
        psum = ctx.enter_context(tc.psum_pool(name="psum", bufs=2))
        ctx.enter_context(tc.manual_schedule())

        x_view = x.rearrange("(g p s) k -> g p s k", p=P, s=PACK)
        w_view = w_enc.rearrange("(c p t) n -> c p t n", p=P, t=PACK)
        wd_view = w_dec_bytes.rearrange("(p t) g -> p t g", t=PACK)
        lib_view = lib.rearrange("(g p s) -> p g s", p=P, s=PACK)
        mean_view = out_mean.rearrange("(g p s) n -> g p s n", p=P, s=PACK)

        x_sb = [work.tile([P, 2, G], BF16, name="x_pair", align_bytes=256, bufs=X_BUFS) for i in range(PAIRS)]
        w_raw = [keep.tile([P, PACK, H], BF16, name=f"w_raw{c}") for c in range(KP)]
        wd_bytes = keep.tile([P, PACK, G], U8, name="wd_bytes")
        q_sb = keep.tile([P, 2, C], BF16, name="q_sb")
        lib_first = keep.tile([P, PACK], BF16, name="lib_first")
        lib_rest = keep.tile([P, GROUPS - 1, PACK], BF16, name="lib_rest")
        depth_sb = keep.tile([P, GROUPS, PACK], BF16, name="depth_sb")
        wsc_sb = keep.tile([P, PACK], F32, name="wsc_sb")
        benc_sb = keep.tile([P, PACK], BF16, name="benc_sb")
        bdec_sb = keep.tile([P, 2 * PACK], BF16, name="bdec_sb")
        benc_bc = keep.tile([P, H], BF16, name="benc_bc")
        bdec_bc = keep.tile([P, G], BF16, name="bdec_bc")
        unit_bc = keep.tile([P, H], BF16, name="unit_bc")
        ident = keep.tile([P, P], F32, name="ident")
        ident16 = keep.tile([P, P], BF16, name="ident16")
        invlib = keep.tile([P, GROUPS, PACK], F32, name="invlib")

        def slot_of(i, s):
            return 2 * (i % 2) + s

        def load_x(i, lo=0, hi=2):
            nc.sync.dma_start(out=x_sb[i][:, lo:hi], in_=x_view[i // 2][:, slot_of(i, lo) : slot_of(i, hi), :])

        def turn_bank(shape):
            return psum.tile(shape, F32, name="turn_bank", bufs=TURN_BANKS)

        def h_bank(shape):
            return psum.tile(shape, F32, name="h_bank", bufs=1)

        def y_bank(shape=(P, BANK)):
            return psum.tile(list(shape), F32, name="y_bank", bufs=Y_BANKS)

        def d_bank(shape):
            return psum.tile(shape, F32, name="d_bank", bufs=D_BANKS)

        def copy(engine, out, in_):
            if engine is scalar:
                scalar.copy(out=out, in_=in_)
            else:
                vector.tensor_copy(out=out, in_=in_)

        def interleave(engine, grouped, rows, lo, hi):
            copy(
                engine,
                grouped[:, lo:hi, :].rearrange("p (c i) t -> p c t i", i=PACK),
                rows[:, :, lo:hi].rearrange("p t (c i) -> p c t i", i=PACK),
            )

        def quantize(mx, cols, grouped):
            vector.quantize_mx(out=mx[0][:, cols].bitcast(FP8X4), scales=mx[1][:, cols], in_=grouped)

        def mx_tiles(pool, name, width, bufs=None):
            return (
                pool.tile([P, width], U32, name=f"{name}_codes", align_bytes=256, bufs=bufs),
                pool.tile([P, width], U8, name=f"{name}_scales", align_bytes=256, bufs=bufs),
            )

        def mx_pass(bank, lhs, lhs_cols, rhs, start, stop):
            nc.tensor.matmul_mx(
                out=bank[:],
                lhsT=lhs[0][:, lhs_cols].bitcast(FP8X4),
                lhsT_scale=lhs[1][:, lhs_cols],
                rhs=rhs[0][:].bitcast(FP8X4),
                rhs_scale=rhs[1][:],
                start=start,
                stop=stop,
            )

        def spread(columns):
            bank = d_bank([P, PACK, P])
            for m in range(PACK):
                nc.tensor.matmul(
                    out=bank[:, m, :],
                    lhsT=columns[:, m : m + 1].to_broadcast([P, P]),
                    rhs=ident16[:],
                    start=True,
                    stop=True,
                )
            return bank

        def copy_bdec(n, bank):
            out = bdec_bc[:, n * BANK : (n + 1) * BANK].rearrange("p (n m) -> p n m", m=PACK)
            copy(scalar, out, bank[:].rearrange("p m n -> p n m"))

        we_grouped = [keep.tile([P, H, PACK], BF16, name=f"we_grouped{c}", align_bytes=256) for c in range(KP)]
        we_mx = [mx_tiles(keep, f"we{c}", H) for c in range(KP)]
        wd_wide = [keep.tile([P, PACK, BANK], BF16, name=f"wd_wide{n}") for n in range(2)]
        wd_grouped = [keep.tile([P, BANK, PACK], BF16, name=f"wd_grouped{n}", align_bytes=256) for n in range(2)]
        wd_mx = [mx_tiles(keep, f"wd{n}", BANK) for n in range(2)]

        def group_we(c):
            copy(
                vector,
                we_grouped[c][:].rearrange("p (u m e) t -> p m u t e", u=2, e=2),
                w_raw[c][:].rearrange("p t (m u e) -> p m u t e", u=2, e=2),
            )

        def quant_we(c):
            quantize(we_mx[c], slice(0, H), we_grouped[c][:].rearrange("p c t -> p (c t)"))

        def widen_wd(engine, n, rows):
            for t in rows:
                src = wd_bytes[:, t, n * BANK : (n + 1) * BANK].bitcast(E4M3)
                factor = wsc_sb[:, t : t + 1]
                if engine is scalar:
                    scalar.activation(out=wd_wide[n][:, t, :], in_=src, func=ACT.Copy, scale=factor)
                else:
                    vector.tensor_scalar(out=wd_wide[n][:, t, :], in0=src, scalar1=factor, scalar2=None, op0=ALU.mult)

        def quant_wd(n):
            quantize(wd_mx[n], slice(0, BANK), wd_grouped[n][:].rearrange("p g t -> p (g t)"))

        x_shape = [P, KP, 2, P]
        x_grouped, x_mx, x_banks = {}, {}, {}

        def turn_x(i, s, bank=None):
            x_banks[i, s] = turn_bank(x_shape)[:] if bank is None else bank
            words = x_sb[i][:, s, :].bitcast(F32)
            for c in range(KP):
                for u in range(2):
                    nc.tensor.transpose(x_banks[i, s][:, c, u, :], words[:, 256 * c + u : 256 * (c + 1) : 2], ident[:])

        def copy_x(i, s, engine=scalar):
            if s == 0:
                x_grouped[i] = work.tile([P, 2, KP, P, PACK], BF16, name="x_pair", align_bytes=256, bufs=X_BUFS)
            copy(engine, x_grouped[i][:, s].bitcast(F32), x_banks[i, s].rearrange("p c u n -> p c n u"))

        def move_x(i, s, bank=None):
            turn_x(i, s, bank)
            copy_x(i, s)

        def quant_x(i, lo=0, hi=2):
            if lo == 0:
                x_mx[i] = mx_tiles(work, "x", 2 * KP * P, bufs=CODE_BUFS)
            grouped = x_grouped[i][:, lo:hi].rearrange("p s c n t -> p (s c n t)")
            quantize(x_mx[i], slice(lo * KP * P, hi * KP * P), grouped)

        y_banks, sums, h_rows, h_banks, h_grouped, h_mx = {}, {}, {}, {}, {}, {}

        def encode(i, s, bank=None):
            y_banks[i, s] = y_bank() if bank is None else bank
            for c in range(KP):
                cols = slice((s * KP + c) * P, (s * KP + c + 1) * P)
                mx_pass(y_banks[i, s], x_mx[i], cols, we_mx[c], c == 0, c == KP - 1)

        def bias_y(i, s, room=None):
            if s == 0:
                sums[i] = work.tile([P, 2 * H], F32, name="sums", bufs=CODE_BUFS) if room is None else room
            slot = slice(slot_of(i, s), slot_of(i, s) + 1)
            vector.scalar_tensor_tensor(
                out=sums[i][:, s * H : (s + 1) * H],
                in0=benc_bc[:],
                scalar=lib_first[:, slot] if i < 2 else lib_rest[:, i // 2 - 1, slot],
                in1=y_banks[i, s][:],
                op0=ALU.mult,
                op1=ALU.add,
            )

        def pair_rows(i):
            return h_rows[i // 2][:, slot_of(i, 0) * H : slot_of(i, 2) * H]

        def leaky(i):
            if i % 2 == 0:
                h_rows[i // 2] = keep.tile([P, PACK * H], BF16, name=f"h_rows{i // 2}")
            vector.scalar_tensor_tensor(
                out=pair_rows(i), in0=sums[i][:], scalar=SLOPE, in1=sums[i][:], op0=ALU.mult, op1=ALU.max
            )

        def turn_h(i, new_bank=h_bank):
            h_banks[i] = new_bank([P, 2, 2, P])
            words = pair_rows(i).bitcast(F32)
            for s in range(2):
                for u in range(2):
                    part = words[:, (2 * s + u) * P : (2 * s + u + 1) * P]
                    nc.tensor.transpose(h_banks[i][:, s, u, :], part, ident[:])

        def copy_h(engine, i, room=None):
            if room is None:
                room = work.tile([P, 2 * H], BF16, name="h_grouped", align_bytes=256, bufs=2)
            h_grouped[i] = room[:, : 2 * H]
            words = h_grouped[i].bitcast(F32).rearrange("p (s n u) -> p s n u", s=2, u=2)
            copy(engine, words, h_banks[i][:].rearrange("p s u n -> p s n u"))

        def quant_h(i):
            h_mx[i] = mx_tiles(work, "h", 2 * P, bufs=CODE_BUFS)
            quantize(h_mx[i], slice(0, 2 * P), h_grouped[i])

        d_banks = {}
        z = [keep.tile([P, PACK, G], F32, name=f"z{g}") for g in range(GROUPS)]

        def z_tile(i, s, lo=0, hi=G):
            return z[i // 2][:, slot_of(i, s), lo:hi]

        def inv_of(i, s):
            return invlib[:, i // 2, slot_of(i, s) : slot_of(i, s) + 1]

        def decode(i, m, bank=None):
            s, n = divmod(m, 2)
            d_banks[i, m] = d_bank([P, BANK]) if bank is None else bank
            mx_pass(d_banks[i, m], h_mx[i], slice(s * P, (s + 1) * P), wd_mx[n], True, True)

        def open_decoder(i):
            quant_h(i)
            for m in range(D_BANKS):
                decode(i, m)

        def bias_d(i, m):
            s, n = divmod(m, 2)
            vector.scalar_tensor_tensor(
                out=z_tile(i, s, n * BANK, (n + 1) * BANK),
                in0=d_banks[i, m][:],
                scalar=inv_of(i, s),
                in1=bdec_bc[:, n * BANK : (n + 1) * BANK],
                op0=ALU.mult,
                op1=ALU.add,
            )

        def exp(part):
            scalar.activation(out=part, in_=part, func=ACT.Exp)

        def log1p(part):
            scalar.activation(out=part, in_=part, func=ACT.Ln, bias=1.0)

        def finish(engine, i, s, res=None, lo=0, hi=G):
            part = z_tile(i, s, lo, hi)
            res = part if res is None else res
            factor = depth_sb[:, i // 2, slot_of(i, s) : slot_of(i, s) + 1]
            if engine is vector:
                vector.tensor_scalar(out=res, in0=part, scalar1=factor, scalar2=None, op0=ALU.mult)
            else:
                gpsimd.tensor_scalar(out=res, in0=part, scalar1=factor, scalar2=0.0, op0=ALU.mult, op1=ALU.add)
            nc.sync.dma_start(out=mean_view[i // 2][:, slot_of(i, s), lo:hi], in_=res)

        hc_grouped, hc_mx, q_banks, k_banks = {}, {}, {}, {}
        q_grouped = keep.tile([P, GROUPS * R * PACK], BF16, name="q_grouped", align_bytes=256)
        q_mx = mx_tiles(keep, "q", GROUPS * R)

        def group_slots(g):
            return h_rows[g][:].rearrange("p (s j) -> p s j", s=PACK)

        def group_hc(g, room, lo=0, hi=H):
            hc_grouped[g] = room.rearrange("p (j s) -> p j s", s=PACK)
            in0 = group_slots(g)[:, :, lo:hi].rearrange("p s j -> p j s")
            out = hc_grouped[g][:, lo:hi]
            gpsimd.tensor_scalar(out=out, in0=in0, scalar1=1.0, scalar2=0.0, op0=ALU.mult, op1=ALU.add)

        def x_room(i):
            return x_grouped[i][:].rearrange("p s c n t -> p (s c n t)")

        def turn_q(g, new_bank):
            q_banks[g] = new_bank([P, 2, 2, P])
            for b in range(2):
                words = q_sb[:, b, :].bitcast(F32)
                for u in range(2):
                    nc.tensor.transpose(q_banks[g][:, b, u, :], words[:, 256 * g + u : 256 * (g + 1) : 2], ident[:])

        def copy_q(engine, g):
            words = q_grouped[:, g * R * PACK : (g + 1) * R * PACK].bitcast(F32)
            out = words.rearrange("p (b r u) -> p b r u", b=2, u=2)
            copy(engine, out, q_banks[g][:].rearrange("p b u r -> p b r u"))

        def contrast(g):
            hc_mx[g] = mx_tiles(keep, f"hc{g}", H)
            quantize(hc_mx[g], slice(0, H), hc_grouped[g].rearrange("p j s -> p (j s)"))
            for b in range(2):
                if g == 0:
                    k_banks[b] = next_bank()
                cols = slice(g * R + b * P, g * R + (b + 1) * P)
                mx_pass(k_banks[b], q_mx, cols, hc_mx[g], g == 0, g == GROUPS - 1)

        def finish_contrast(b):
            res = work.tile([P, H], F32, name="contrast_sb")
            vector.tensor_tensor(
                out=res[:].rearrange("p (m u e) -> p m u e", u=2, e=2),
                in0=k_banks[b][:].rearrange("p (u m e) -> p m u e", u=2, e=2),
                in1=unit_bc[:].rearrange("p (m u e) -> p m u e", u=2, e=2),
                op=ALU.mult,
            )
            nc.sync.dma_start(out=out_contrast[b * P : (b + 1) * P, :], in_=res[:])

        def warm_up(count, moving):
            bank = y_bank()
            for n in range(count):
                nc.tensor.matmul(out=bank[:], lhsT=ident16[:], rhs=moving, start=True, stop=True)

        scalar.dma_start(out=wsc_sb[:], in_=w_dec_scale.rearrange("(p t) o -> p (t o)", t=PACK))
        scalar.dma_start(out=benc_sb[:], in_=b_enc.rearrange("(n m) -> n m", n=P))
        scalar.dma_start(
            out=bdec_sb[:].rearrange("n (h m) -> n h m", h=2), in_=b_dec.rearrange("(h n m) -> n h m", h=2, n=P)
        )
        for lo in (0, 2):
            nc.sync.dma_start(out=wd_bytes[:, lo : lo + 2], in_=wd_view[:, lo : lo + 2])
        for c in range(KP):
            nc.sync.dma_start(out=w_raw[c][:], in_=w_view[c])
        load_x(0, 0, 1)
        load_x(0, 1, 2)
        load_x(1)
        nc.sync.dma_start(out=lib_first[:], in_=lib_view[:, 0, :])
        load_x(2)
        load_x(3)
        nc.sync.dma_start(out=lib_rest[:], in_=lib_view[:, 1:, :])
        load_x(4)
        load_x(5)
        nc.sync.dma_start(out=q_sb[:], in_=q.rearrange("(b r) c -> r b c", r=P))
        load_x(6)
        load_x(7)
        nc.sync.dma_start(out=depth_sb[:], in_=depth.rearrange("(g p s) -> p g s", p=P, s=PACK))
        nc.sync.dma_start(out=unit_bc[:], in_=unit.partition_broadcast(P))

        vector.memset(ident[:], 0.0)
        make_identity(nc, ident[:], nomemset=True)
        scalar.copy(out=ident16[:], in_=ident[:])
        widen_wd(vector, 0, range(PACK))
        widen_wd(scalar, 1, range(2))
        benc_bank = spread(benc_sb[:])
        bdec_banks = [spread(bdec_sb[:, n * PACK : (n + 1) * PACK]) for n in range(2)]
        widen_wd(scalar, 1, range(2, PACK))
        warm_up(3, w_raw[0][:, 0, :])
        interleave(scalar, wd_grouped[0], wd_wide[0], BANK // 2, BANK)
        copy(
            scalar,
            benc_bc[:].rearrange("p (u m e) -> p u m e", u=2, e=2),
            benc_bank[:].rearrange("p (u e) m -> p u m e", u=2),
        )
        copy_bdec(0, bdec_banks[0])
        move_x(0, 0)
        move_x(0, 1)
        warm_up(2, w_raw[0][:, 0, :])
        copy_bdec(1, bdec_banks[1])
        move_x(1, 0, h_bank(x_shape)[:])
        interleave(vector, wd_grouped[0], wd_wide[0], 0, BANK // 2)
        for c in range(KP):
            group_we(c)
        for c in range(KP):
            quant_we(c)
        quant_x(0, 0, 1)
        quant_wd(0)
        quant_x(0, 1, 2)
        encode(0, 0)
        encode(0, 1)
        interleave(scalar, wd_grouped[1], wd_wide[1], 0, BANK // 2)
        bias_y(0, 0)
        quant_x(1, 0, 1)
        move_x(1, 1)
        encode(1, 0)
        interleave(scalar, wd_grouped[1], wd_wide[1], BANK // 2, BANK)
        move_x(2, 0)
        turn_x(2, 1)
        bias_y(0, 1)
        vector.reciprocal(out=invlib[:, 0, :], in_=lib_first[:])
        vector.reciprocal(out=invlib[:, 1:, :], in_=lib_rest[:])
        leaky(0)
        turn_h(0)
        copy_h(scalar, 0)
        quant_x(1, 1, 2)
        encode(1, 1)
        copy_x(2, 1)
        move_x(3, 0)
        move_x(3, 1, h_bank(x_shape)[:])
        bias_y(1, 0)
        quant_wd(1)
        bias_y(1, 1)

        def add_bdec(i, n, res):
            cols = slice(n * BANK, (n + 1) * BANK)
            gpsimd.tensor_tensor(out=res[:, cols], in0=z_tile(i, 0)[:, cols], in1=bdec_bc[:, cols], op=ALU.add)

        def divide_d(i, n):
            out = z_tile(i, 0, n * BANK, (n + 1) * BANK)
            scalar.activation(out=out, in_=d_banks[i, n][:], func=ACT.Copy, scale=inv_of(i, 0))

        def exp_biased(i, n, biased):
            cols = slice(n * BANK, (n + 1) * BANK)
            scalar.activation(out=z_tile(i, 0)[:, cols], in_=biased[:, cols], func=ACT.Exp)

        open_decoder(0)
        decode(0, 3, y_bank())
        divide_d(0, 0)
        divide_d(0, 1)
        leaky(1)
        turn_h(1)
        copy_h(scalar, 1)
        quant_x(2)
        first_biased = x_room(2).bitcast(F32)
        add_bdec(0, 0, first_biased)
        encode(2, 0)
        encode(2, 1, d_bank([P, BANK]))
        turn_x(4, 0)
        turn_x(4, 1)
        bias_d(0, 2)
        bias_d(0, 3)
        exp(z_tile(0, 1))
        copy_x(4, 0)
        copy_x(4, 1)
        move_x(5, 0, h_bank(x_shape)[:])
        exp_biased(0, 0, first_biased)
        bias_y(2, 0, x_room(1).bitcast(F32))
        bias_y(2, 1)

        open_decoder(1)
        decode(1, 3, y_bank())
        move_x(5, 1)
        leaky(2)
        group_hc(0, x_room(1), 0, HC_SPLIT)
        add_bdec(0, 1, first_biased)
        turn_h(2)
        copy_h(scalar, 2)
        quant_x(3)
        encode(3, 0)
        bias_d(1, 0)
        encode(3, 1, d_bank([P, BANK]))
        bias_d(1, 1)
        exp(z_tile(1, 0))
        move_x(6, 0)
        turn_x(6, 1)
        bias_d(1, 2)
        bias_d(1, 3)
        copy_x(6, 1)
        bias_y(3, 0)
        bias_y(3, 1)

        open_decoder(2)
        decode(2, 3, y_bank())
        divide_d(2, 0)
        exp_biased(0, 1, first_biased)
        leaky(3)
        biased = sums[3][:]
        add_bdec(2, 0, biased)
        turn_h(3)
        copy_h(scalar, 3, x_room(3))
        exp(z_tile(1, 1))
        quant_x(4)
        encode(4, 0)
        turn_x(7, 0)
        turn_x(7, 1)
        bias_d(2, 1)
        exp(z_tile(2, 0, BANK, G))
        copy_x(7, 0)
        bias_d(2, 2)
        bias_d(2, 3)
        exp(z_tile(2, 1))
        exp_biased(2, 0, biased)

        open_decoder(3)
        decode(3, 3, y_bank())
        group_hc(1, x_room(3))
        group_hc(0, x_room(1), HC_SPLIT, H)
        quant_x(5)
        bias_y(4, 0)
        encode(4, 1)
        bias_d(3, 0)
        encode(5, 0, d_bank([P, BANK]))
        bias_d(3, 1)
        exp(z_tile(3, 0))
        bias_d(3, 2)
        bias_d(3, 3)
        encode(5, 1)
        exp(z_tile(3, 1))
        log1p(z[0][:])
        log1p(z[1][:])

        order = [h_bank, turn_bank, d_bank, d_bank, turn_bank, y_bank, d_bank, y_bank]
        taken = []

        def next_bank(shape=(P, BANK)):
            taken.append(shape)
            return order[(len(taken) - 1) % len(order)](list(shape))

        def exp_bank(i, m):
            exp(z_tile(i, m // 2, m % 2 * BANK, (m % 2 + 1) * BANK))

        bias_y(4, 1)
        copy_x(7, 1, vector)
        bias_y(5, 0)
        bias_y(5, 1)
        quant_x(6)
        encode(6, 0, next_bank())
        leaky(4)
        encode(6, 1, next_bank())
        turn_h(4, next_bank)
        leaky(5)
        turn_h(5, next_bank)
        group_hc(2, x_room(5))
        quant_x(7)
        encode(7, 0, next_bank())
        encode(7, 1, next_bank())
        bias_y(6, 0)
        copy_h(vector, 4)
        bias_y(6, 1)
        copy_h(vector, 5)
        bias_y(7, 0)
        bias_y(7, 1)

        quant_h(4)
        for m in range(2):
            decode(4, m, next_bank())
        quant_h(5)
        leaky(6)
        for m in range(2, 4):
            decode(4, m, next_bank())
        turn_h(6, next_bank)
        decode(5, 0, next_bank())
        leaky(7)
        turn_h(7, next_bank)
        decode(5, 1, next_bank())
        finish(gpsimd, 0, 0, res=sums[6][:])
        finish(gpsimd, 0, 1)
        finish(gpsimd, 1, 0)
        for m in range(4):
            bias_d(4, m)
            if m % 2:
                exp(z_tile(4, m // 2))
        decode(5, 2, next_bank())
        decode(5, 3, next_bank())
        copy_h(vector, 6, x_room(6))
        copy_h(vector, 7)
        for m in range(2):
            bias_d(5, m)
            exp_bank(5, m)
        quant_h(6)
        for m in range(4):
            decode(6, m, next_bank())
        quant_h(7)
        finish(gpsimd, 1, 1, res=x_room(6).bitcast(F32))
        for i, s in ((2, 0), (2, 1), (3, 0), (3, 1)):
            finish(gpsimd, i, s)
        last = GROUPS - 1
        group_hc(last, x_room(7), 0, LAST_SPLIT)
        decode(7, 0, next_bank())
        decode(7, 1, next_bank())
        for m in range(2, 4):
            bias_d(5, m)
            decode(7, m, next_bank())
            exp_bank(5, m)
        for m in range(4):
            bias_d(6, m)
            turn_q(m, next_bank)
            exp_bank(6, m)
        for m in range(4):
            bias_d(7, m)
            exp_bank(7, m)
        for g in range(GROUPS):
            copy_q(vector, g)

        def quant_q(half):
            cols = slice(half * 2 * R, (half + 1) * 2 * R)
            quantize(q_mx, cols, q_grouped[:, cols.start * PACK : cols.stop * PACK])

        interleave(vector, hc_grouped[last], group_slots(last), LAST_SPLIT, H)
        jobs = [(quant_q, 0), (contrast, 0), (contrast, 1), (quant_q, 1), (contrast, 2), (contrast, 3)]
        jobs = jobs + [(finish_contrast, 0), (finish_contrast, 1)]
        for job, which in jobs[:1]:
            job(which)
        for n in range(2 * BATCH):
            i, s = BATCH + n // 2, n % 2
            width = BANK if n < 6 else G
            for lo in range(0, G, width):
                log1p(z_tile(i, s, lo, lo + width))
                finish(vector, i, s, None, lo, lo + width)
            for job, which in jobs[1 + n : 1 + n + 1]:
                job(which)
